import numpy as np, ml_dtypes
CORES = [2,3,42,43,82,83,122,123]
N = 8
BF = ml_dtypes.bfloat16
def gentries(a):
    return np.ascontiguousarray(a.reshape(8, 16, -1).transpose(0, 2, 1)).reshape(8, -1)
def gtable(e):
    e = np.asarray(e); return np.ascontiguousarray(e.reshape(8, -1, 16).transpose(0, 2, 1)).reshape(128, -1).astype(np.int32)
W, NW, P, RO, F = 4096, 512, 8, 3, 1
S = W // NW
def parts(rng):
    x = rng.integers(0, 16, (N, 8, 16, W)); l = rng.integers(0, W, (N, 8, NW, P))
    n = np.where(rng.random((N, 8, NW)) < 0.12, rng.integers(0, P + 1, (N, 8, NW)), rng.integers(P // 2, P + 1, (N, 8, NW)))
    return x, l, n, rng.integers(0, 256, (N, 8, 16)), rng.integers(68, 100, (N, 8))
def pack(x, l, n, w, t):
    return {"xv": np.ascontiguousarray(x.reshape(N, 128, W)).astype(np.float32).astype(BF), "wl": np.stack([gtable(a.reshape(8, NW * P)) for a in l]),
            "wn": np.ascontiguousarray(n).astype(np.int32), "wt": np.ascontiguousarray(w.reshape(N, 128, 1)).astype(np.int32), "th": np.ascontiguousarray(t.reshape(N, 8, 1)).astype(np.int32)}
def setup_inputs(rng):
    return pack(*parts(rng))
def setup_inputs_alike(rng):
    x, l, n, w, t = parts(rng)
    l[:, ::2] = rng.choice(np.array([0, W - 1, W // 2, 3]), (N, 4, NW, P))
    l[:, 1] = l[:, 1, :, :1]; x[:, 3] = x[:, 3, :, :1]; w[:, 5] = 0; n[:, 6] = P; t[:, 7] = 0
    return pack(x, l, n, w, t)
def setup_inputs_corners(rng):
    x, l, n, w, t = parts(rng); k = np.arange(P)
    x = rng.integers(0, 4, (N, 8, 16, W)) + 12 * (np.arange(W) & 1); t = rng.integers(48, 144, (N, 8)); t[:, 0] = 48; t[:, 7] = 143
    w = np.where(rng.random((N, 8, 1)) < 0.3, 255 * rng.integers(0, 2, (N, 8, 1)), w)
    n = rng.choice(np.array([0, 1, 2, P - 1, P, P, P, P]), (N, 8, NW)); m = np.minimum(n, rng.choice(np.array([1, 2, P // 2, P // 2 + 1, P - 1, P]), (N, 8, NW)))
    pick = rng.random((8, NW)) < 0.4; a = rng.integers(P // 2, P + 1, (8, NW)); a[:, 0] = P // 2 + 1; a[:, NW - 1] = P; pick[:, 0] = True; pick[:, NW - 1] = True
    for q in range(0, N - 1, 2):
        m[q] = np.where(pick, a, m[q]); n[q] = np.where(pick, np.maximum(a, rng.integers(0, P + 1, (8, NW))), n[q])
        m[q + 1] = np.where(pick, P - a, m[q + 1]); n[q + 1] = np.where(pick, np.where(a == P, 0, np.maximum(P - a, rng.integers(1, P + 1, (8, NW)))), n[q + 1])
    m[0, 5] = P; n[0, 5] = P; m[1, 4] = 0; n[1, 4] = 0
    m[N - 2] = P; n[N - 2] = P; m[N - 1] = 0; n[N - 1] = 0
    for q in (0, 1):
        fr = np.where(pick, 0, m[q]); fr[5] = 0; fr = fr.reshape(-1); o = rng.permutation(8 * NW); b = fr[o]; cut = np.zeros_like(b)
        cut[o] = np.clip((int(np.sum(m[q])) - 256) % 512 - (np.add.accumulate(b) - b), 0, b)
        m[q] = m[q] - cut.reshape(8, NW); n[q] = np.where(m[q] == 0, 0, n[q])
    sc = np.where((k == 0) | (k >= n[..., None]), 2.0, rng.random((N, 8, NW, P)))
    brk = np.argsort(np.argsort(sc, axis=-1), axis=-1) < (m - 1)[..., None]
    cl = (rng.integers(0, 2, (N, 8, NW, 1)) + np.add.accumulate(brk.astype(np.int64), axis=-1)) & 1
    l = np.where(rng.random((N, 8, NW, P)) < 0.1, cl * (W - 1), 2 * rng.integers(0, W // 2, (N, 8, NW, P)) + cl)
    return pack(x, l, n, w, t)
def setup_inputs_ends(rng):
    kind = rng.integers(0, 3, (N, 8, 1, W)); k = np.arange(P); c = np.arange(1, P + 1)
    x = np.where(kind == 0, 0, np.where(kind == 1, 15, 15 * rng.integers(0, 2, (N, 8, 16, W))))
    for u, v in ((0, 15), ((240 * 255) & (W - 1), 0)):
        hh = ((u * u >> 5) + 37 * u + 611 * c) & (W - 1)
        for g in (0, 7): x[:, g][..., hh] = v
    x[..., 0] = 0; x[..., W - 1] = 15
    w = 255 * rng.integers(0, 2, (N, 8, 16)); w[:, 0] = 255; w[:, 7] = 255; w[:, 3, 0] = 0; w[:, 4] = 0
    t = 239 * rng.integers(0, 2, (N, 8)); t[:, 0] = 0; t[:, 1] = 239; t[:, 7] = 239
    kd = rng.integers(0, 4, (N, 8, NW, 1)); s = rng.integers(0, 2, (N, 8, NW, 1)); em = np.where(np.arange(N) == N - 1, 0.05, 0.25).reshape(N, 1, 1)
    kd[N - 1] = np.where(rng.random((8, NW, 1)) < 0.9, 1, kd[N - 1]); kd[:, :, 0] = 1; kd[:, 7, NW - 1] = 1; kd[:, 7, NW - 2] = 0; s[:, 7, NW - 2] = 1
    b = np.where(kd == 0, s, np.where(kd == 1, (k + s) & 1, rng.integers(0, 2, (N, 8, NW, P))))
    n = P * (rng.random((N, 8, NW)) > em).astype(np.int64); n[:, :, 0] = P; n[:, :, 1] = 0; n[:, :, NW - 2] = P; n[:, :, NW - 1] = P
    return pack(x, (W - 1) * b, n, w, t)
def setup_inputs_spread(rng):
    x, l, n, w, t = parts(rng)
    x = (rng.random((N, 8, 16, W)) * np.exp2(rng.integers(0, 5, (N, 8, 1, W)))).astype(np.int64)
    l = np.minimum((W * rng.random((N, 8, NW, P)) ** rng.choice(np.array([0.3, 1.0, 3.0]), (N, 8, 1, 1))).astype(np.int64), W - 1)
    n = rng.integers(0, P + 1, (N, 8, NW)); w = (256 * rng.random((N, 8, 16)) ** 2).astype(np.int64)
    t = np.exp2(7.9 * rng.random((N, 8))).astype(np.int64) - 1
    return pack(x, l, n, w, t)
def setup_inputs_ties(rng):
    x, l, n, w, t = parts(rng)
    lane = np.argsort(rng.random((N, 8, 16)), axis=-1); pm = np.argsort(rng.random((N, 8, W)), axis=-1)
    lev = np.zeros((N, 8, W), np.int64); np.put_along_axis(lev, pm, np.broadcast_to(np.arange(W) % 241, (N, 8, W)), 2)
    x = np.clip(lev[:, :, None, :] - 15 * lane[..., None], 0, 15)
    t = rng.choice(np.array([0, 1, 15, 16, 47, 80, 100]), (N, 8)); s = rng.integers(0, 241, (N, 8, NW))
    for k in range(P):
        l[..., k] = np.take_along_axis(pm, s + 241 * rng.integers(0, W // 241, (N, 8, NW)), 2)
        st = np.abs(t[:, :, None] + rng.integers(-1, 2, (N, 8, NW))); up = ((rng.random((N, 8, NW)) < 0.5) & (s + st <= 240)) | (s - st < 0)
        s = np.where(up, s + st, s - st)
    t[:, 7] = 239
    hl = 239 * ((np.arange(P) + rng.integers(0, 2, (N, NW, 1))) & 1) + rng.integers(0, 2, (N, NW, P)) + 241 * rng.integers(0, W // 241, (N, NW, P))
    l[:, 7] = np.take_along_axis(pm[:, 7], hl.reshape(N, NW * P), 1).reshape(N, NW, P)
    return pack(x, l, n, w, t)
def check_inputs(d):
    bad = []
    for k, lo, hi in (("xv", 0, 15), ("wl", 0, W - 1), ("wn", 0, P), ("wt", 0, 255), ("th", 0, 239)):
        v = np.asarray(d[k]).astype(np.float64)
        if not (np.min(v) >= lo and np.max(v) <= hi): bad.append("range of " + k)
        elif np.any(v != np.floor(v)): bad.append("whole numbers of " + k)
    return bad
def reference(xv, wl, wn, wt, th):
    x = xv.astype(np.int32).reshape(N, 8, 16, W); w = wt.astype(np.int32).reshape(N, 8, 16, 1, 1); lim = th.astype(np.int64).reshape(N, 8, 1, 1)
    l = np.stack([gentries(a) for a in wl]).astype(np.int64).reshape(N, 8, NW, P); n = wn.astype(np.int64)
    last = np.zeros((N, 1, 1, 1), np.int64); k = np.arange(P); M = W - 1
    for t in range(RO):
        if t > 0:
            l = np.roll(l, (1, 1), axis=(0, 1)); n = np.roll(n, (1, 1), axis=(0, 1))
        live = k < n[..., None]
        v = np.take_along_axis(x, l.reshape(N, 8, 1, NW * P), 3).reshape(N, 8, 16, NW, P)
        dist = np.add.reduce(np.abs(v[..., 1:] - v[..., :-1]), axis=2)
        start = live.copy(); start[..., 1:] &= dist > lim
        end = live.copy(); end[..., :-1] &= start[..., 1:] | ~live[..., 1:]
        num = np.add.accumulate(start.astype(np.int64), axis=-1) - 1; m = np.add.reduce(start.astype(np.int64), axis=-1)
        z = v.copy(); c = np.ones((N, 8, NW, P), np.int64); f = l.copy()
        for j in range(1, P):
            s = start[..., j]
            z[..., j] = np.where(s[:, :, None], v[..., j], np.maximum(z[..., j - 1], v[..., j]))
            c[..., j] = np.where(s, 1, c[..., j - 1] + 1); f[..., j] = np.where(s, l[..., j], f[..., j - 1])
        u = np.add.reduce(w * z, axis=2).astype(np.int64) & M
        h = ((u * u >> 5) + 37 * u + 611 * c) & M
        xh = np.take_along_axis(x, h.reshape(N, 8, 1, NW * P), 3).reshape(N, 8, 16, NW, P)
        dd = np.add.reduce(np.abs(xh - z), axis=2).astype(np.int64)
        y = np.zeros((N, 8, NW, 2 * P + 2), np.int64)
        np.put_along_axis(y, np.where(end, 2 * num, 2 * P), ((f * (2 * c + 1) >> 2) + last) & M, 3)
        np.put_along_axis(y, np.where(end, 2 * num + 1, 2 * P + 1), (h + dd * (2 * c + 1)) & M, 3)
        own = np.minimum(2 * m, P); over = np.roll(2 * m - own, 1, axis=0); oy = np.roll(y[..., P:2 * P], 1, axis=0)
        n = np.minimum(own + over, P); o = own[..., None]
        l = np.where(k < o, y[..., :P], np.where(k < n[..., None], np.take_along_axis(oy, np.clip(k - o, 0, P - 1), 3), 0))
        e = np.argmax(end, axis=-1)[..., None]; e5 = e[:, :, None]
        val = ((np.take_along_axis(z, e5, 4) + np.take_along_axis(xh, e5, 4)) >> 1)[..., 0]
        at = (S * np.arange(NW) + (np.take_along_axis(u, e, 3)[..., 0] & (S - 1)))[:, :, None]
        np.put_along_axis(x, at, np.where((m > 0)[:, :, None], val, np.take_along_axis(x, at, 3)), 3)
        last = np.add.reduce(m.reshape(N, 8 * NW), axis=1).reshape(N, 1, 1, 1) & 255
    return {"yx": np.add.reduce(x.reshape(N, 128, W // F, F), axis=3).astype(np.float32).astype(BF), "yl": np.stack([gtable(a.reshape(8, NW * P)) for a in l]).astype(np.float32), "yn": n.astype(np.float32)}

@@ -1,0 +1,558 @@
+from concourse.bass import DstId, RemoteDMATransfer
+from concourse.mybir import dt, AluOpType, AxisListType, ActivationFunctionType
+
+NV, W = 3, 4096
+CALLS1 = [[("s", 0, 1), ("v", 1, 2), ("s", 2, 3), ("v", 3, 4)], [("s", 0, 2), ("s", 2, 4)]]
+CALLS2 = [[("s", 0, 2), ("s", 2, 4)], [("s", 0, 2), ("s", 2, 4)]]
+BFT, F32, I32, U16 = "bfloat16", "float32", "int32", "uint16"
+SCRATCH = {}
+VIEWS = {}
+
+
+def _sb(name, shape, ty):
+    buf = "b_" + "_".join(str(n) for n in shape) + "_" + ty
+    k = SCRATCH[buf][1][1] if buf in SCRATCH else 0
+    SCRATCH[buf] = ("sbuf", [shape[0], k + 1] + shape[1:], ty)
+    VIEWS[name] = (buf, k)
+
+
+SCRATCH["X"] = ("sbuf", [128, 8192], BFT)
+SCRATCH["Z"] = ("sbuf", [128, 4096], BFT)
+for _n in ("L0", "L1", "L2", "PT", "W0", "W1", "UB"):
+    SCRATCH[_n] = ("psum", [128, 512], F32)
+SCRATCH["PV"] = ("psum", [128, 4, 16, 8], F32)
+for _n, _s, _t in (
+        ("ONES", [128, 128], BFT), ("B1", [128, 128], BFT), ("B", [128, 128], BFT), ("IB", [128, 128], BFT), ("NIB", [128, 128], BFT),
+        ("NB", [128, 128], BFT), ("N4", [128, 128], BFT), ("P4", [128, 128], BFT), ("P16", [128, 128], BFT), ("CL", [128, 128], BFT),
+        ("CR", [128, 512], BFT), ("IDF", [128, 128], F32), ("PR32", [128, 32], F32), ("E81", [8, 128], BFT), ("E8", [8, 128], BFT),
+        ("BIASC", [128, 16, 8], BFT), ("WM", [128, 8], BFT), ("KA0", [128, 16, 8], BFT), ("KA1", [128, 16, 8], BFT), ("KB", [128, 16, 8], BFT),
+        ("NK0", [128, 128], BFT), ("C129", [128, 16, 8], BFT), ("C128", [128, 16, 8], BFT),
+        ("FR", [128, 256], F32), ("CRO", [128, 512], F32), ("CRV", [128, 256], F32), ("THB", [8, 1], BFT), ("THF", [8, 1], F32), ("DT", [8, 8], BFT),
+        ("PID", [128, 1], I32), ("PI2", [128, 1], I32), ("WT", [128, 4], I32), ("AI", [128, 1], I32), ("AI2", [128, 1], I32), ("BX", [128, 1], I32), ("BY", [128, 1], I32),
+        ("NZ", [128, 1], F32), ("COEF", [128, 1], F32), ("WCOL", [128, 1], F32), ("AR", [128, 1], F32), ("A4", [128, 1], F32), ("CSQ", [128, 1], F32), ("CCT", [128, 1], F32),
+        ("K1", [128, 1], F32), ("K2", [128, 1], F32), ("KM", [128, 1], F32), ("KZ", [128, 1], F32), ("PF0", [128, 1], F32), ("PF1", [128, 1], F32), ("BA", [128, 1], F32), ("BB", [128, 1], F32), ("BC", [128, 1], F32),
+        ("BD", [128, 1], F32), ("BE", [128, 1], F32), ("TH", [8, 1], I32), ("WN", [8, 512], I32), ("WNF", [8, 512], F32), ("WL", [128, 256], I32),
+        ("BW1", [128, 32], I32), ("BW0", [128, 32], I32), ("L7", [128, 32], I32), ("FVM", [128, 256], F32), ("LI", [128, 64], I32), ("LQ", [128, 96], I32),
+        ("LOFF", [128, 96], U16), ("ZS", [128, 512], F32), ("ZX", [128, 512], BFT), ("ZI", [128, 512], BFT), ("YN", [8, 512], F32)):
+    _sb(_n, _s, _t)
+for _b in "01":
+    for _n, _s, _t in (
+            ("V", [128, 2064], BFT), ("AD", [128, 2048], BFT), ("XH", [128, 2048], BFT), ("AE", [128, 2048], BFT),
+            ("OFF", [128, 128], U16), ("HOFF", [128, 128], U16), ("DEAD", [128, 16, 8], BFT), ("NM", [128, 16, 8], I32), ("NF", [128, 128], F32),
+            ("S", [128, 16, 9], BFT), ("NS", [128, 128], BFT), ("SP", [128, 128], BFT), ("C", [128, 128], BFT), ("CN", [128, 128], BFT), ("CE", [128, 16, 8], BFT),
+            ("CX", [128, 16, 4], BFT), ("SN", [128, 128], F32), ("AX", [128, 128], F32), ("T0", [128, 16, 8], F32), ("TI", [128, 16, 8], I32), ("TJ", [128, 16, 8], I32),
+            ("KP", [128, 16, 8], BFT), ("CT", [128, 16, 8], F32), ("WI", [128, 16, 8], I32), ("HI", [128, 16, 8], I32), ("HF", [128, 128], F32),
+            ("FS", [128, 256], F32), ("FO", [128, 256], F32),
+            ("MO", [128, 512], BFT), ("MV", [128, 256], BFT), ("N2", [128, 16, 8], I32), ("N3", [128, 16, 8], I32),
+            ("PRO", [128, 512], F32), ("PRV", [128, 256], F32), ("OSO", [128, 512], F32), ("OSV", [128, 256], F32),
+            ("J", [128, 16, 4], I32), ("JM", [128, 16, 4], I32), ("YL", [128, 128], F32), ("NA", [128, 16, 4], F32), ("NC", [128, 16, 2], F32), ("NN", [128, 16], F32)):
+        _sb(_n + _b, _s, _t)
+    for _i in range(NV):
+        for _n in ("SO", "SV", "RO", "RV"):
+            _sb("%s%d%s" % (_n, _i, _b), [128, 16, 4], F32)
+        for _n in ("MX", "MR"):
+            _sb("%s%d%s" % (_n, _i, _b), [128, 16], BFT)
+
+DMAS = ["xv", "wl", "wn", "wt", "th", "yx", "yl0", "yl1", "yn"]
+SEMAPHORES = ["qv", "qs", "qp", "qg", "ls"] + ["d_" + n for n in DMAS] + ["r%s%d%d" % (k, t, b) for k in "xm" for t in range(NV) for b in (0, 1)]
+CY = 0.00104
+PC = 0.00052
+HOP = 0.08
+
+
+def rank_program(g, core, T, topo):
+    rank = T.rank_of(core)
+    if rank is None:
+        return
+    n = len(T.cores)
+    nxt, nx2, prv, pr2 = [T.cores[(rank + k) % n] for k in (1, 2, -1, -2)]
+    A, F = AluOpType, ActivationFunctionType
+    V, S, P = g.vector, g.scalar, g.tensor
+    D = {k: T[b][:, i] for k, (b, i) in VIEWS.items()}
+    X, Z, PT, PV, L = T.X, T.Z, T.PT, T.PV, [T.L0, T.L1, T.L2]
+    tiles = [slice(128 * k, 128 * k + 128) for k in range(4)]
+    UB, WB = [T.UB[:, k] for k in tiles], [[w[:, k] for k in tiles] for w in (T.W0, T.W1)]
+    tt, mm, sc, act, mset, copy = V.tensor_tensor, P.matmul, V.tensor_tensor_scan, S.activation, V.memset, V.tensor_copy
+    ops, cur = [], [""]
+
+    def op(q, r, w, cost, fn, b=(), sem=None, inc=0, after=(), lat=0.0):
+        ops.append({"k": cur[0] + q if cur[0] else "", "q": q, "r": r.split(), "w": w.split(), "cost": cost, "fn": fn, "b": list(b), "sem": sem, "inc": inc, "after": list(after), "lat": lat})
+        return len(ops) - 1
+
+    def v(r, w, cyc, fn, b=()):
+        return op("v", r, w, 0.03 + CY * max(cyc, 64), lambda: [fn()], b)
+
+    def s(r, w, cyc, fn, b=()):
+        return op("s", r, w, 0.03 + CY * max(cyc, 64), lambda: [fn()], b)
+
+    def p(r, w, cyc, fn, b):
+        return op("p", r, w, PC * cyc, fn, b)
+
+    def gg(r, w, cost, fn):
+        return op("g", r, w, cost, lambda: [fn()])
+
+    def ld(q, name, out, in_, r, w, cost):
+        return op(q, r, w, 0.06, lambda: [(g.sync if q == "y" else S).dma_start(out, in_)], sem="d_" + name, inc=16, lat=cost)
+
+    def ts(out, in0, s1, s2, o0, o1=None):
+        if o1 is None:
+            return V.tensor_scalar(out, in0, s1, None, o0)
+        return V.tensor_scalar(out, in0, s1, s2, o0, o1)
+
+    def gcopy(out, in_, n):
+        return g.affine_select(out, in_, [[0, n]], A.is_equal, 0.0, 0, 0)
+
+    nl = [0]
+
+    def lane():
+        nl[0] += 1
+        return (nl[0] - 1) % len(L)
+
+    ld("y", "wl", D["WL"], T.wl[:], "", "WL", 2.0)
+    ld("y", "xv", X[:, 0:W], T.xv[:], "", "X", 7.0)
+    ld("d", "th", D["TH"], T.th[:], "", "TH", 2.0)
+    ld("d", "wt", D["WT"][:, 0:1], T.wt[:], "", "WT", 2.0)
+    ld("d", "wn", D["WN"], T.wn[:], "", "WN", 2.0)
+    v("", "ONES", 64, lambda: mset(D["ONES"], 1.0))
+    gg("ONES", "B1", 0.5, lambda: g.affine_select(D["B1"], D["ONES"], [[-16, 8], [0, 16]], A.is_ge, 0.0, 0, 1))
+    gg("B1", "B", 0.5, lambda: g.affine_select(D["B"], D["B1"], [[16, 8], [0, 16]], A.is_ge, 0.0, 15, -1))
+    gg("ONES", "IB", 0.5, lambda: g.affine_select(D["IB"], D["ONES"], [[-1, 128]], A.is_equal, 0.0, 0, 1))
+    gg("ONES", "E81", 0.5, lambda: g.affine_select(D["E81"], T.b_128_128_bfloat16[0:8, VIEWS["ONES"][1]], [[1, 128]], A.is_ge, 0.0, 0, -16))
+    gg("E81", "E8", 0.5, lambda: g.affine_select(D["E8"], D["E81"], [[-1, 128]], A.is_ge, 0.0, 15, 16))
+    gg("", "PID", 0.2, lambda: g.iota(D["PID"], [[0, 1]], 0, 1))
+    gg("", "BW1", 0.3, lambda: g.iota(D["BW1"], [[16, 32]], 0, 0))
+    for b in (0, 1):
+        v("WL", "OFF%d" % b, 128, lambda b=b: copy(D["OFF%d" % b], D["WL"][:, 128 * b:128 * b + 128]))
+        v("", "V%dz" % b, 64, lambda b=b: mset(D["V%d" % b][:, 0:16], 0.0))
+        v("", "S%d9" % b, 64, lambda b=b: mset(D["S%d" % b][:, :, 8], 1.0))
+    v("IB", "IDF", 128, lambda: copy(D["IDF"], D["IB"]))
+    for k, src, c in (("NIB", "IB", -1.0), ("NB", "B", -16.0), ("N4", "IB", -4096.0), ("P4", "IB", 4096.0), ("P16", "IB", 65536.0)):
+        v(src, k, 64, lambda k=k, src=src, c=c: ts(D[k], D[src], c, None, A.mult))
+    v("", "CRa", 256, lambda: mset(D["CR"], 1.0))
+    v("CRa", "CR", 64, lambda: mset(D["CR"][:, 0:512:8], -64.0))
+    v("TH", "THB", 64, lambda: copy(D["THB"], D["TH"]))
+    v("TH", "THF", 64, lambda: copy(D["THF"], D["TH"]))
+    v("PID", "PI2", 64, lambda: ts(D["PI2"], D["PID"], 15, None, A.bitwise_and))
+    v("PI2", "NZ", 64, lambda: ts(D["NZ"], D["PI2"], 0.0, None, A.is_gt))
+    p("E8 THB", "PTth", 64, lambda: [mm(PT[:, 304:305], D["E8"], D["THB"], True, True)], ["PT"])
+    v("PTth NZ", "COEF", 64, lambda: tt(D["COEF"], PT[:, 304:305], D["NZ"], A.add), ["PT"])
+    v("B COEF", "CL", 64, lambda: ts(D["CL"], D["B"], D["COEF"], None, A.mult))
+    v("THF IB", "DT", 64, lambda: ts(D["DT"], D["IB"][0:8, 0:8], D["THF"], None, A.mult))
+    p("ONES DT", "W0.0", 1024, lambda: [mm(WB[0][0][:, m:128:16], D["ONES"][0:8, :], D["DT"], True, True) for m in range(16)], ["W0"])
+    v("W0.0", "BIa", 128, lambda: ts(D["BIASC"], WB[0][0], -1.0, None, A.mult), ["W0"])
+    v("BIa", "BIASC", 64, lambda: mset(D["BIASC"][:, :, 0], 8192.0))
+    v("WT", "WCOL", 64, lambda: copy(D["WCOL"], D["WT"][:, 0:1]))
+    v("B WCOL", "WM", 64, lambda: ts(D["WM"], D["B"][:, 0:128:16], D["WCOL"], None, A.mult))
+    for k, c in (("C129", 129.0), ("C128", 128.0), ("A4", 0.0), ("CSQ", 4096.0 + 592.0), ("CCT", -360240.0), ("K1", 1.0), ("K2", 2.0), ("KM", -1.0), ("KZ", 257.5)):
+        v("", k, 64, lambda k=k, c=c: mset(D[k], c))
+    v("", "NKa", 64, lambda: mset(D["NK0"], 1.0))
+    v("NKa", "NK0", 64, lambda: mset(D["NK0"][:, 0::8], 0.0))
+    v("WN", "WNF", 512, lambda: copy(D["WNF"], D["WN"]))
+    for b in (0, 1):
+        p("WNF IDF", "PTn%d" % b, 512, lambda b=b: [P.transpose(PT[:, 320 + 16 * b + w1:336 + 16 * b:2], D["WNF"][:, 256 * b + w1:256 * b + 256:2], D["IDF"][0:8, 0:8]) for w1 in (0, 1)], ["PT"])
+        for k in range(8):
+            v("PTn%d" % b + (" " + " ".join("DE%d%d" % (b, i) for i in range(7)) if k == 7 else ""), "DEAD%d" % b if k == 7 else "DE%d%d" % (b, k), 64,
+              lambda b=b, k=k: ts(D["DEAD%d" % b][:, :, k], PT[:, 320 + 16 * b:336 + 16 * b], float(k), None, A.is_le), ["PT"])
+        v("WL", "NF%d" % b, 128, lambda b=b: copy(D["NF%d" % b], D["WL"][:, 128 * b:128 * b + 128]))
+        p("NF%d IDF" % b, "PTN", 512, lambda b=b: [P.transpose(PT[:, 128:256], D["NF%d" % b], D["IDF"])], ["PT"])
+        v("PTN", "NM%d" % b, 128, lambda b=b: copy(D["NM%d" % b], PT[:, 128:256]), ["PT"])
+
+    def late_constants():
+        v("", "FRa", 256, lambda: mset(D["FR"], 1.0))
+        v("FRa", "FR", 64, lambda: mset(D["FR"][:, 0::8], 0.0))
+        v("", "CROa", 512, lambda: mset(D["CRO"], 1.0))
+        v("CROa", "CRO", 64, lambda: mset(D["CRO"][:, 0::8], 0.0))
+        v("", "CRVa", 256, lambda: mset(D["CRV"], 1.0))
+        v("CRVa", "CRV", 64, lambda: mset(D["CRV"][:, 0::4], 0.0))
+        v("", "FVM", 256, lambda: mset(D["FVM"], 0.0))
+        v("PID", "PF0", 64, lambda: copy(D["PF0"], D["PID"]))
+        v("PF0", "PF1", 64, lambda: ts(D["PF1"], D["PF0"], 128.0, None, A.add))
+        for b in (0, 1):
+            v("PF%d C129" % b, "KA%d" % b, 64, lambda b=b: ts(D["KA%d" % b], D["C129"], 0.0, D["PF%d" % b], A.mult, A.add))
+        for k in range(16):
+            v("", "KB.%d" % k, 64, lambda k=k: mset(D["KB"][:, k // 8::2, k % 8], float(k)))
+        for q in range(4):
+            v("IDF", "PR%d" % q, 64, lambda q=q: copy(D["PR32"][32 * q:32 * q + 32, :], D["IDF"][32 * q:32 * q + 32, 32 * q:32 * q + 32]))
+        v("PI2", "BX", 64, lambda: ts(D["BX"], D["PI2"], 3, None, A.bitwise_and))
+        v("PI2", "BY", 64, lambda: ts(D["BY"], D["PI2"], 2, 1, A.arith_shift_right, A.bitwise_and))
+        v("BX", "BA", 64, lambda: ts(D["BA"], D["BX"], 512.0, None, A.mult))
+        v("BY", "BB", 64, lambda: ts(D["BB"], D["BY"], 2048.0, None, A.mult))
+        v("BA BB", "BC", 64, lambda: tt(D["BC"], D["BA"], D["BB"], A.add))
+        v("PI2", "BD", 64, lambda: ts(D["BD"], D["PI2"], 8.0, 8.0, A.is_ge, A.mult))
+        v("BC BD", "BE", 64, lambda: tt(D["BE"], D["BC"], D["BD"], A.add))
+        v("BW1 BE", "BW0", 64, lambda: ts(D["BW0"], D["BW1"], D["BE"], None, A.add))
+
+    def gather(out, base, off, r, tok, calls):
+        for q, a, e in calls:
+            w = " ".join("%s.%d" % (tok, i) for i in range(a, e))
+            o, x = out[:, base + 512 * a:base + 512 * e], off[:, 32 * a:32 * e]
+            if q == "s":
+                s(r, w, (e - a) * 512 * 1.5, lambda o=o, x=x: act(o, X[:, 0:W].indirect(x), F.Copy))
+            else:
+                v(r, w, (e - a) * 512 * 1.5, lambda o=o, x=x: copy(o, X[:, 0:W].indirect(x)))
+
+    def lanesum(wb, k, m, src, mov, start, stop, o=0):
+        return mm(wb[k][:, m:128:16], src[:, o + m:o + 2048:16], mov, start, stop)
+
+    def phase1(t, b):
+        x = str(b)
+        Vb, AD, wb, w_ = D["V" + x], D["AD" + x], WB[b], "W" + x
+        gather(Vb, 16, D["OFF" + x], "X OFF" + x, "V" + x, CALLS1[b])
+        for c in range(4):
+            j = 512 * c
+            i = lane()
+            p("V%s.%d %s IB NIB" % (x, c, "V%sz" % x if c == 0 else "V%s.%d" % (x, c - 1)), "L%d" % i, 1024,
+              lambda j=j, i=i: [mm(L[i][:], D["IB"], Vb[:, 16 + j:528 + j], True, False), mm(L[i][:], D["NIB"], Vb[:, 15 + j:527 + j], False, True)], ["L%d" % i])
+            s("L%d" % i, "AD%s.%d" % (x, c), 512, lambda j=j, i=i: act(AD[:, j:j + 512], L[i][:], F.Abs), ["L%d" % i])
+            i = lane()
+            p("CL CR", "L%d" % i, 512, lambda i=i: [mm(L[i][:], D["CL"], D["CR"], True, False)], ["L%d" % i])
+            p("AD%s.%d NB" % (x, c), "L%d" % i, 512, lambda j=j, i=i: [mm(L[i][:], D["NB"], AD[:, j:j + 512], False, True)], ["L%d" % i])
+            v("L%d V%s.%d" % (i, x, c), "Z%s.%d" % (x, c), 512, lambda j=j, i=i: sc(Z[:, 2048 * b + j:2048 * b + j + 512], L[i][:], Vb[:, 16 + j:528 + j], 0.0, A.min, A.max), ["L%d" % i])
+        p("IB BIASC P4 DEAD%s DE%sa" % (x, x), w_ + ".0", 256, lambda: [mm(wb[0], D["IB"], D["BIASC"], True, False), mm(wb[0], D["P4"], D["DEAD" + x], False, False)], [w_])
+        p(" ".join("AD%s.%d" % (x, c) for c in range(4)) + " B", w_ + ".0", 1024,
+          lambda: [lanesum(wb, 0, m, AD, D["B"][:, 0:128:16], False, m == 15) for m in range(16)], [w_])
+        v(w_ + ".0", "S" + x, 128, lambda: ts(D["S" + x][:, :, 0:8], wb[0], 0.0, None, A.is_gt), [w_])
+        p("S%s S%s9 DEAD%s DE%sa IB NIB" % (x, x, x, x), w_ + ".1", 256, lambda: [mm(wb[1], D["IB"], D["S" + x][:, :, 1:9], True, False), mm(wb[1], D["NIB"], D["DEAD" + x], False, True)], [w_])
+
+    def runs(t, b):
+        x, y = str(b), "%d%d" % (t, b)
+        wb, w_, Sx = WB[b], "W" + x, D["S" + x][:, :, 0:8]
+        s("S%s K1" % x, "NS" + x, 128, lambda: act(D["NS" + x], Sx, F.Identity, bias=D["K1"], scale=-1.0))
+        s("S%s K2" % x, "SP" + x, 128, lambda: act(D["SP" + x], Sx, F.Identity, bias=D["K2"]))
+        v("NS%s SP%s" % (x, x), "C" + x, 64, lambda: sc(D["C" + x], D["NS" + x], D["SP" + x], 0.0, A.mult, A.add))
+        s("C%s CCT" % x, "CT" + x, 128, lambda: act(D["CT" + x], D["C" + x], F.Identity, bias=D["CCT"], scale=9776.0))
+        v(w_ + ".1 NK0", "CN" + x, 128, lambda: sc(D["CN" + x], D["NK0"], wb[1], 0.0, A.mult, A.add), [w_])
+        s("CN" + x, "MX" + y, 16, lambda: act(D["MX" + y], D["CN" + x][:, 7::8], F.Copy))
+        i = op("g", "MX" + y, "", 0.8, lambda: [send_counts(y)], sem="none")
+        op("r", "", "MR" + y, 0.0, None, sem="rm" + y, inc=len(count_engines(nxt, core)), after=[i], lat=3.0)
+
+    def upart(t, b):
+        x = str(b)
+        wb, w_ = WB[b], "W" + x
+        zs = " ".join("Z%s.%d" % (x, c) for c in range(4))
+        zo = 2048 * b
+        p(zs + " P4 C129 WM", w_ + ".2", 1200, lambda: [mm(wb[2], D["P4"], D["C129"], True, False)] + [lanesum(wb, 2, m, Z[:, zo:zo + 2048], D["WM"], False, m == 15) for m in range(16)], [w_])
+        p(zs + " P4 C128 WM", "UB%sa" % x, 1200, lambda: [mm(UB[b], D["P4"], D["C128"], True, False)] + [lanesum(UB, b, m, Z[:, zo:zo + 2048], D["WM"], False, False) for m in range(16)], ["UB"])
+        v(w_ + ".2", "KP" + x, 128, lambda: ts(D["KP" + x], wb[2], 1.0 / 4096, -0.5 + 1.0 / 8192, A.mult, A.add), [w_])
+        p("KP%s N4 UB%sa" % (x, x), "UB%s UB%sa" % (x, x), 128, lambda: [mm(UB[b], D["N4"], D["KP" + x], False, True)], ["UB"])
+        s("UB%s CSQ" % x, "SQ" + x, 128, lambda: act(UB[2 + b], UB[b], F.Square, bias=D["CSQ"]), ["UB"])
+
+    def hpart(t, b):
+        x = str(b)
+        v("SQ%s CT%s" % (x, x), "WI" + x, 128, lambda: tt(D["WI" + x], D["CT" + x], UB[2 + b], A.add), ["UB"])
+        v("WI" + x, "HI" + x, 128, lambda: ts(D["HI" + x], D["WI" + x], 5, 4095, A.arith_shift_right, A.bitwise_and))
+        v("HI" + x, "HF" + x, 128, lambda: copy(D["HF" + x], D["HI" + x]))
+        p("HF%s IDF" % x, "PTH", 512, lambda: [P.transpose(PT[:, 0:128], D["HF" + x], D["IDF"])], ["PT"])
+        v("PTH", "HOFF" + x, 128, lambda: copy(D["HOFF" + x], PT[:, 0:128]), ["PT"])
+
+    def first1(t, b):
+        x = str(b)
+        wb, w_, FS, M0 = WB[b], "W" + x, D["FS" + x], D["MO" + x][:, 0:128]
+        v("CN%s %s.1" % (x, w_), "CE" + x, 128, lambda: tt(D["CE" + x], D["CN" + x], wb[1], A.mult), [w_])
+        v("CE" + x, "MO%s.0" % x, 64, lambda: ts(M0, D["CE" + x], 1.0, None, A.is_equal))
+        v("MO%s.0 UB%s" % (x, x), "FS%sc" % x, 128, lambda: tt(FS[:, 128:256], M0, UB[b], A.mult), ["UB"])
+        p("HF%s IDF P16 P4 KA%s " % (x, x) + " ".join("KB.%d" % k for k in range(16)), w_ + ".2", 768,
+          lambda: [mm(wb[2], D["IDF"], D["HF" + x], True, False), mm(wb[2], D["P16"], D["KA" + x], False, False), mm(wb[2], D["P4"], D["KB"], False, True)], [w_])
+        v("MO%s.0 %s.2" % (x, w_), "FS%sa" % x, 128, lambda: tt(FS[:, 0:128], M0, wb[2], A.mult), [w_])
+        v("FR FS%sa FS%sc" % (x, x), "FO" + x, 256, lambda: sc(D["FO" + x], D["FR"], FS, 0.0, A.mult, A.add))
+        for q in range(4):
+            r = slice(32 * q, 32 * q + 32)
+            gg("FVM FO" + x, "FV%s%d" % (x, q), 0.24, lambda r=r, q=q: gcopy(D["FVM"][r, 4 * b + q::8], D["FO" + x][r, 7::8], 32))
+
+    def first2(t):
+        p(" ".join("FV%d%d" % (b, q) for b in (0, 1) for q in range(4)) + " ".join(" PR%d" % q for q in range(4)) + " P4 ONES", "PTL", 640,
+          lambda: [mm(PT[:, 256:288], D["FVM"][:, 0:128], D["PR32"], True, True), mm(PT[:, 288:320], D["P4"], D["ONES"][:, 0:32], True, False),
+                   mm(PT[:, 288:320], D["FVM"][:, 128:256], D["PR32"], False, True)], ["PT"])
+        LI, LQ = D["LI"], D["LQ"]
+        v("PTL", "LI", 64, lambda: copy(LI, PT[:, 256:320]), ["PT"])
+        v("LI", "L7", 64, lambda: ts(D["L7"], LI[:, 32:64], 4096 + 7, None, A.bitwise_and))
+        v("LI", "LQa", 64, lambda: ts(LQ[:, 0:32], LI[:, 0:32], 4095, None, A.bitwise_and))
+        v("LI", "LQb", 64, lambda: ts(LQ[:, 32:64], LI[:, 0:32], 12, None, A.arith_shift_right))
+        v("L7 BW0", "LQc", 64, lambda: tt(LQ[:, 64:96], D["L7"], D["BW0"], A.add))
+        v("LQa LQb LQc", "LOFF", 96, lambda: copy(D["LOFF"], LQ))
+
+    def update(t):
+        zs = " ".join("Z%d.%d" % (b, c) for b in (0, 1) for c in range(4))
+        s(zs + " LOFF KZ", "ZS", 512 * 1.5, lambda: act(D["ZS"], Z[:].indirect(D["LOFF"][:, 32:64]), F.Identity, bias=D["KZ"]))
+        v("X LOFF ZS", "ZX", 512 * 1.5, lambda: tt(D["ZX"], X[:, 0:W].indirect(D["LOFF"][:, 0:32]), D["ZS"], A.add))
+        v("ZX", "ZI", 256, lambda: ts(D["ZI"], D["ZX"], 0.5, -129.0, A.mult, A.add))
+        v("ZI LOFF", "X", 512 * 3.5, lambda: copy(X[:].indirect(D["LOFF"][:, 64:96]), D["ZI"]))
+
+    def phase2(t, b):
+        x = str(b)
+        XH, AE = D["XH" + x], D["AE" + x]
+        gather(XH, 0, D["HOFF" + x], "X HOFF" + x, "XH" + x, CALLS2[b])
+        for c in range(4):
+            j = 512 * c
+            i = lane()
+            p("Z%s.%d NIB" % (x, c), "L%d" % i, 512, lambda j=j, i=i: [mm(L[i][:], D["NIB"], Z[:, 2048 * b + j:2048 * b + j + 512], True, False)], ["L%d" % i])
+            p("XH%s.%d IB" % (x, c), "L%d" % i, 512, lambda j=j, i=i: [mm(L[i][:], D["IB"], XH[:, j:j + 512], False, True)], ["L%d" % i])
+            s("L%d" % i, "AE%s.%d" % (x, c), 512, lambda j=j, i=i: act(AE[:, j:j + 512], L[i][:], F.Abs), ["L%d" % i])
+
+    def dpart(t, b):
+        x = str(b)
+        p(" ".join("AE%s.%d" % (x, c) for c in range(4)) + " B", "W%s.0" % x, 1024, lambda: [lanesum(WB[b], 0, m, D["AE" + x], D["B"][:, 0:128:16], True, True) for m in range(16)], ["W" + x])
+
+    def names1(t, b):
+        x, y = str(b), "%d%d" % (t, b)
+        wb, w_, MO, MV = WB[b], "W" + x, D["MO" + x], D["MV" + x]
+        v("S%s NM%s NM%sa" % (x, x, x), "SN" + x, 256, lambda: tt(D["SN" + x], D["S" + x][:, :, 0:8], D["NM" + x], A.mult))
+        v("NS%s SN%s" % (x, x), "AX" + x, 128, lambda: sc(D["AX" + x], D["NS" + x], D["SN" + x], 0.0, A.mult, A.add))
+        v("AX%s C%s" % (x, x), "T0" + x, 256, lambda: tt(D["T0" + x], D["C" + x], D["AX" + x], A.mult))
+        v("T0%s A4" % x, "TI" + x, 128, lambda: ts(D["TI" + x], D["T0" + x], D["A4"], 1024.0, A.add, A.mult))
+        v("TI" + x, "TJ" + x, 128, lambda: ts(D["TJ" + x], D["TI" + x], 4095 << 12, None, A.bitwise_and))
+        v("TJ" + x, "P1" + x, 128, lambda: ts(PV[:, 1 + b], D["TJ" + x], 1.0, None, A.add), ["PV"])
+        v("CE" + x, "CX" + x, 64, lambda: ts(D["CX" + x], D["CE" + x][:, :, 4:8], 4.5, None, A.max))
+        p("CX%s MR%s IB" % (x, y), w_ + ".3", 320, lambda: [mm(wb[3][:, 0:64], D["IB"], D["CX" + x], True, False)] + [mm(wb[3][:, k:64:4], D["IB"], D["MR" + y], False, k == 3) for k in range(4)], [w_])
+        for q in range(1, 4):
+            v("CE" + x, "MO%s.%d" % (x, q), 64, lambda q=q: ts(MO[:, 128 * q:128 * q + 128], D["CE" + x], q + 1.0, None, A.is_equal))
+        for q in range(4):
+            v(w_ + ".3", "MV%s.%d" % (x, q), 64, lambda q=q: ts(MV[:, 64 * q:64 * q + 64], wb[3][:, 0:64], q + 5.0, None, A.is_equal), [w_])
+
+    def names2(t, b):
+        x, y = str(b), "%d%d" % (t, b)
+        wb, w_, PRO, PRV = WB[b], "W" + x, D["PRO" + x], D["PRV" + x]
+        v(w_ + ".0 C" + x, "PV.0", 128, lambda: tt(PV[:, 0], D["C" + x], wb[0], A.mult), [w_, "PV"])
+        v("PV.0 HI" + x, "N2" + x, 128, lambda: tt(D["N2" + x], D["HI" + x], PV[:, 0], A.add), ["PV"])
+        v("N2" + x, "N3" + x, 128, lambda: ts(D["N3" + x], D["N2" + x], 4095, None, A.bitwise_and))
+        v("N3%s P1%s" % (x, x), "PV.3", 128, lambda: tt(PV[:, 3], D["N3" + x], PV[:, 1 + b], A.add), ["PV"])
+        for q in range(4):
+            v("MV%s.%d PV.3" % (x, q), "PRV%s.%d" % (x, q), 64, lambda q=q: tt(PRV[:, 64 * q:64 * q + 64], D["MV" + x][:, 64 * q:64 * q + 64], PV[:, 3, :, 4:8], A.mult), ["PV"])
+        v(" ".join("PRV%s.%d" % (x, q) for q in range(4)) + " CRV", "OSV" + x, 256, lambda: sc(D["OSV" + x], D["CRV"], PRV, 0.0, A.mult, A.add))
+        for q in range(4):
+            if b:
+                s("OSV" + x, "SV%s.%d" % (y, q), 64, lambda q=q: act(D["SV" + y][:, :, q], D["OSV" + x][:, 64 * q + 3:64 * q + 64:4], F.Copy))
+                continue
+            gg("OSV" + x, "SV%s.%d" % (y, q), 0.21, lambda q=q: gcopy(D["SV" + y][:, :, q], D["OSV" + x][:, 64 * q + 3:64 * q + 64:4], 16))
+        sv = " ".join("SV%s.%d" % (y, q) for q in range(4))
+        for k in (0, 2):
+            for q in (k, k + 1):
+                v("MO%s.%d PV.3" % (x, q), "PRO%s.%d" % (x, q), 128, lambda q=q: tt(PRO[:, 128 * q:128 * q + 128], D["MO" + x][:, 128 * q:128 * q + 128], PV[:, 3], A.mult), ["PV"])
+            r = slice(128 * k, 128 * k + 256)
+            v("PRO%s.%d PRO%s.%d CRO" % (x, k, x, k + 1), "OSO%s.%d" % (x, k), 256, lambda r=r: sc(D["OSO" + x][:, r], D["CRO"][:, r], PRO[:, r], 0.0, A.mult, A.add))
+            for q in (k, k + 1):
+                s("KM OSO%s.%d" % (x, k), "SO%s.%d" % (y, q), 64, lambda q=q: act(D["SO" + y][:, :, q], D["OSO" + x][:, 128 * q + 7:128 * q + 128:8], F.Identity, bias=D["KM"]))
+        so = " ".join("SO%s.%d" % (y, q) for q in range(4))
+        if t < NV - 1:
+            i = op("g", so + " " + sv, "", 0.8, lambda: [send_pairs(y)], sem="none")
+            op("r", "", "RO%s RV%s" % (y, y), 0.0, None, sem="rx" + y, inc=len(pair_engines(prv, core, 0)) + len(pair_engines(pr2, prv, 1)), after=[i], lat=3.5)
+        else:
+            i = op("g", sv, "", 0.8, lambda: [send_last(y)], sem="none")
+            op("r", "", "RV" + y, 0.0, None, sem="rx" + y, inc=len(count_engines(prv, core)), after=[i], lat=3.5)
+
+    def join(t, b):
+        x, y, last = str(b), "%d%d" % (t, b), t == NV - 1
+        J, NM, DE = D["J" + x], D["NM" + x], D["DEAD" + x]
+        own, ov = D[("SO" if last else "RO") + y], D["RV" + y]
+        rd = "RV%s " % y + (" ".join("SO%s.%d" % (y, q) for q in range(4)) if last else "RO" + y)
+        if last:
+            v(rd, "J" + x, 128, lambda: tt(J, own, ov, A.add))
+            jt = "J" + x
+        else:
+            v(rd, "J%sa" % x, 112, lambda: tt(J[:, 2:16, :], own[:, 0:14, :], ov[:, 0:14, :], A.add))
+            v(rd, "J%sb" % x, 64, lambda: tt(J[:, 0:2, :], own[:, 14:16, :], ov[:, 14:16, :], A.add))
+            jt = "J%sa J%sb" % (x, x)
+        jm, jn = J, jt
+        if last:
+            jm, jn = D["JM" + x], "JM" + x
+            v(jt, jn, 64, lambda: ts(jm, J, 0.0, None, A.max))
+        v(jn, "NM%sa" % x, 64, lambda: ts(NM[:, :, 0::2], jm, 12, None, A.arith_shift_right))
+        v(jn, "NM" + x, 64, lambda: ts(NM[:, :, 1::2], jm, 4095, None, A.bitwise_and))
+        v("NM%s NM%sa" % (x, x), "NF" + x, 128, lambda: copy(D["NF" + x], NM))
+        p("NF%s IDF" % x, "PTN", 512, lambda: [P.transpose(PT[:, 128:256], D["NF" + x], D["IDF"])], ["PT"])
+        if not last:
+            v("PTN", "OFF" + x, 128, lambda: copy(D["OFF" + x], PT[:, 128:256]), ["PT"])
+            v(jt, "DE%sa" % x, 64, lambda: ts(DE[:, :, 0::2], J, 0.0, None, A.is_lt))
+            v(jt, "DEAD" + x, 64, lambda: ts(DE[:, :, 1::2], J, 0.0, None, A.is_lt))
+        else:
+            s("PTN", "YL" + x, 128, lambda: act(D["YL" + x], PT[:, 128:256], F.Copy), ["PT"])
+            ld("y", "yl" + x, T.yl[:, 128 * b:128 * b + 128], D["YL" + x], "YL" + x, "yl" + x, 2.5)
+            v(jt, "NA" + x, 64, lambda: ts(D["NA" + x], J, 0.0, 2.0, A.is_ge, A.mult))
+            v("NA" + x, "NC" + x, 64, lambda: tt(D["NC" + x], D["NA" + x][:, :, 0:2], D["NA" + x][:, :, 2:4], A.add))
+            v("NC" + x, "NN" + x, 64, lambda: tt(D["NN" + x], D["NC" + x][:, :, 0], D["NC" + x][:, :, 1], A.add))
+            p("NN%s IDF" % x, "LN" + x, 1024, lambda: [P.transpose(L[0][0:8, 256 * b + w1:256 * b + 256:2], D["NN" + x][:, w1::2], D["IDF"]) for w1 in (0, 1)], ["L0"])
+
+    def total(t):
+        p("ONES MX%d0 MX%d1" % (t, t), "PTA", 128, lambda: [mm(PT[:, 288:304], D["ONES"], D["MX%d0" % t], True, False), mm(PT[:, 288:304], D["ONES"], D["MX%d1" % t], False, True)], ["PT"])
+        v("PTA", "AR", 64, lambda: V.tensor_reduce(D["AR"], PT[:, 288:304], AxisListType.X, A.add), ["PT"])
+        v("AR", "AI", 64, lambda: copy(D["AI"], D["AR"]))
+        v("AI", "AI2", 64, lambda: ts(D["AI2"], D["AI"], 255, None, A.bitwise_and))
+        v("AI2", "A4", 64, lambda: ts(D["A4"], D["AI2"], 4.0, None, A.mult))
+
+    def count_engines(a, c):
+        return topo.engines(a, c)[0:8]
+
+    def pair_engines(a, c, k):
+        e = topo.engines(a, c)
+        return (e[8:16], e[0:8])[k] if len(e) == 16 else (e[0:4], e[4:8])[k]
+
+    def mask(es):
+        return sum(1 << e for e in es)
+    lsum = [0]
+
+    def send_one(dst, out, in_, sem):
+        es = count_engines(core, dst)
+        rid, pid, _ = topo.addr(dst)
+        lsum[0] += len(es)
+        g.remote_dma(D[out], D[in_], T.sem[sem], T.sem.ls, pid, rid, mask(es))
+
+    def send_counts(y):
+        send_one(prv, "MR" + y, "MX" + y, "rm" + y)
+
+    def send_last(y):
+        send_one(nxt, "RV" + y, "SV" + y, "rx" + y)
+
+    def send_pairs(y):
+        tr = []
+        for k, dst, o, i in ((0, nxt, "RO", "SO"), (1, nx2, "RV", "SV")):
+            es = pair_engines(core, nxt, k)
+            lsum[0] += len(es)
+            rid, pid, _ = topo.addr(dst)
+            tr.append(RemoteDMATransfer(dst_ids=[DstId(rid=rid, pnc=pid)], dma_engine_mask=mask(es), remote_sem=T.sem["rx" + y], srcs=[D[i + y]], dsts=[D[o + y]]))
+        g.remote_dma_fused(tr, local_sem=T.sem.ls)
+
+    def part(key, fn, *a):
+        cur[0] = key + "".join(str(k) for k in a[1:])
+        fn(*a)
+        cur[0] = ""
+
+    for t in range(NV):
+        for b in (0, 1):
+            part("phase1", phase1, t, b)
+            part("runs", runs, t, b)
+            part("upart", upart, t, b)
+            part("hpart", hpart, t, b)
+        if t == 0:
+            late_constants()
+        for b in (0, 1):
+            part("phase2", phase2, t, b)
+            part("first1", first1, t, b)
+            part("names1", names1, t, b)
+        part("first2", first2, t)
+        part("update", update, t)
+        if t == NV - 1:
+            ld("y", "yx", T.yx[:], X[:, 0:W], "X", "yx", 7.0)
+        for b in (0, 1):
+            part("dpart", dpart, t, b)
+            part("names2", names2, t, b)
+        if t < NV - 1:
+            total(t)
+        for b in (0, 1):
+            part("join", join, t, b)
+    v("LN0 LN1", "YN", 512, lambda: copy(D["YN"], L[0][0:8, :]), ["L0"])
+    ld("y", "yn", T.yn[:], D["YN"], "YN", "yn", 2.5)
+    emit(g, T, ops)
+    g.wait_ge(T.sem.ls, lsum[0])
+
+
+BOOST = {"runs1s": 258, "first2v": 246, "phase21p": -108, "names11v": -14, "phase10v": 32, "phase21s": -140, "upart1s": 138, "first11v": -82,
+         "first10v": -16, "runs0s": 196, "phase20p": -122, "first10p": -102, "phase11p": -84}
+
+
+def emit(g, T, ops):
+    deps = links(ops)
+    issue(g, T, ops, deps, arrange(ops, deps, BOOST, HOP)[0])
+
+
+def links(ops):
+    N = len(ops)
+    lastw, readers, banks = {}, {}, {}
+    deps = [dict() for _ in range(N)]
+
+    def add(i, j, hard):
+        if j != i:
+            deps[i][j] = deps[i].get(j, False) or hard
+    for i, o in enumerate(ops):
+        for k in o["r"]:
+            if k in lastw:
+                add(i, lastw[k], True)
+            readers.setdefault(k, []).append(i)
+        for k in o["w"]:
+            if k in lastw:
+                add(i, lastw[k], not (o["q"] == "p" and ops[lastw[k]]["q"] == "p"))
+            for j in readers.get(k, []):
+                add(i, j, True)
+            lastw[k] = i
+            readers[k] = []
+        for k in o["b"]:
+            for j in banks.get(k, []):
+                add(i, j, ops[j]["q"] != o["q"])
+            banks.setdefault(k, []).append(i)
+        for j in o["after"]:
+            add(i, j, False)
+    return deps
+
+
+def arrange(ops, deps, boost, hop):
+    N = len(ops)
+    succ = [[] for _ in range(N)]
+    for i in range(N):
+        for j in deps[i]:
+            succ[j].append(i)
+    prio = [0.0] * N
+    for i in range(N - 1, -1, -1):
+        o = ops[i]
+        prio[i] = o["cost"] + o["lat"] + max([prio[j] + hop for j in succ[i]] or [0.0])
+    prio = [prio[i] + boost.get(ops[i]["k"], 0.0) for i in range(N)]
+    left = [len(deps[i]) for i in range(N)]
+    ready = [0.0] * N
+    free, cand, order = {}, {}, []
+    for i in range(N):
+        if left[i] == 0:
+            cand.setdefault(ops[i]["q"], []).append(i)
+    while len(order) < N:
+        best = None
+        for q in sorted(cand):
+            if cand[q]:
+                st = max(free.get(q, 0.0), min(ready[i] for i in cand[q]))
+                if best is None or st < best[0]:
+                    best = (st, q)
+        st, q = best
+        i = max((i for i in cand[q] if ready[i] <= st + 1e-9), key=lambda i: (prio[i], -i))
+        cand[q].remove(i)
+        order.append(i)
+        end = st + ops[i]["cost"]
+        if q != "r":
+            free[q] = end
+        end += ops[i]["lat"]
+        for j in succ[i]:
+            ready[j] = max(ready[j], end + (hop if deps[j][i] and q != "r" else 0.0))
+            left[j] -= 1
+            if left[j] == 0:
+                cand.setdefault(ops[j]["q"], []).append(j)
+    return order, max(free.values())
+
+
+def issue(g, T, ops, deps, order):
+    queues = {"v": g.vector, "s": g.scalar, "d": g.scalar, "p": g.tensor, "g": g, "y": g.sync}
+    sems = {"v": "qv", "s": "qs", "p": "qp", "g": "qg"}
+    level, done, seen = {}, {}, {}
+    for i in order:
+        o = ops[i]
+        q = o["q"]
+        if q == "r":
+            level[o["sem"]] = level.get(o["sem"], 0) + o["inc"]
+            done[i] = (o["sem"], level[o["sem"]])
+            continue
+        qk = "s" if q == "d" else q
+        need = {}
+        for j, hard in deps[i].items():
+            if hard and done[j] is not None:
+                sm, c = done[j]
+                need[sm] = max(need.get(sm, 0), c)
+        for sm in sorted(need):
+            if seen.get((qk, sm), 0) < need[sm]:
+                seen[(qk, sm)] = need[sm]
+                queues[q].wait_ge(T.sem[sm], need[sm])
+        res = o["fn"]()
+        if o["sem"] == "none":
+            done[i] = None
+            continue
+        sm, inc = (o["sem"], o["inc"]) if o["sem"] else (sems[q], 1)
+        for r in res:
+            r.then_inc(T.sem[sm], inc)
+            level[sm] = level.get(sm, 0) + inc
+        done[i] = (sm, level[sm])
+    for sm in sorted(level):
+        if seen.get(("g", sm), 0) < level[sm]:
+            g.wait_ge(T.sem[sm], level[sm])

@@ -2,9 +2,13 @@ from concourse.bass import DstId, RemoteDMATransfer
 from concourse.mybir import dt, AluOpType, AxisListType, ActivationFunctionType
 
 NV, W = 3, 4096
-CALLS1 = [[("s", 0, 1), ("v", 1, 2), ("s", 2, 3), ("v", 3, 4)], [("s", 0, 2), ("s", 2, 4)]]
-CALLS2 = [[("s", 0, 2), ("s", 2, 4)], [("s", 0, 2), ("s", 2, 4)]]
-BFT, F32, I32, U16 = "bfloat16", "float32", "int32", "uint16"
+GATHER1 = [[("s", 0, 1), ("v", 1, 2), ("s", 2, 3), ("s", 3, 4)], [("s", 0, 2), ("s", 2, 4)]]
+GATHER2 = [[("s", 0, 2), ("v", 2, 3), ("s", 3, 4)], [("s", 0, 2), ("v", 2, 3), ("s", 3, 4)]]
+NEIGH = [[(0, 1), (1, 2), (2, 3), (3, 4)], [(0, 2), (2, 3), (3, 4)]]
+BYMAX = [2, 4]
+ABS2 = [[(0, 2), (2, 3), (3, 4)], [(0, 2), (2, 3), (3, 4)]]
+BFT, F32, I32, U16, F16 = "bfloat16", "float32", "int32", "uint16", "float16"
+BIG, BIG2, EMPTY = 2.0 ** 26, 2.0 ** 18, -2.0 ** 25
 SCRATCH = {}
 VIEWS = {}
 
@@ -18,34 +22,34 @@ def _sb(name, shape, ty):
 
 SCRATCH["X"] = ("sbuf", [128, 8192], BFT)
 SCRATCH["Z"] = ("sbuf", [128, 4096], BFT)
-for _n in ("L0", "L1", "L2", "PT", "W0", "W1", "UB"):
+SCRATCH["DD"] = ("sbuf", [128, 4096], BFT)
+for _n in ("L0", "L1", "TO", "TV", "W0", "W1", "UB"):
     SCRATCH[_n] = ("psum", [128, 512], F32)
-SCRATCH["PV"] = ("psum", [128, 4, 16, 8], F32)
+SCRATCH["D3"] = ("psum", [128, 4, 8, 16], F32)
+SCALED = (("NB32", "B", -128.0), ("B16", "B", 64.0), ("P4", "IB", 16384.0), ("NH", "IB", -0.5), ("I2", "IB", 2.0), ("N22", "IB", -2.0 ** 22),
+          ("CA", "IB", 9728.0), ("CB", "IB", 48.0), ("F2", "IB", 2 * BIG2), ("FN", "IB", -BIG2), ("T0", "IB", 2 * BIG), ("T1", "IB", 6 * BIG), ("T2", "IB", 10 * BIG),
+          ("T3", "IB", 14 * BIG), ("TN", "IB", -BIG), ("I120", "IB", 120.0))
+for _n, _a, _c in SCALED:
+    _sb(_n, [128, 128], BFT)
 for _n, _s, _t in (
-        ("ONES", [128, 128], BFT), ("B1", [128, 128], BFT), ("B", [128, 128], BFT), ("IB", [128, 128], BFT), ("NIB", [128, 128], BFT),
-        ("NB", [128, 128], BFT), ("N4", [128, 128], BFT), ("P4", [128, 128], BFT), ("P16", [128, 128], BFT), ("CL", [128, 128], BFT),
-        ("CR", [128, 512], BFT), ("IDF", [128, 128], F32), ("PR32", [128, 32], F32), ("E81", [8, 128], BFT), ("E8", [8, 128], BFT),
-        ("BIASC", [128, 16, 8], BFT), ("WM", [128, 8], BFT), ("KA0", [128, 16, 8], BFT), ("KA1", [128, 16, 8], BFT), ("KB", [128, 16, 8], BFT),
-        ("NK0", [128, 128], BFT), ("C129", [128, 16, 8], BFT), ("C128", [128, 16, 8], BFT),
-        ("FR", [128, 256], F32), ("CRO", [128, 512], F32), ("CRV", [128, 256], F32), ("THB", [8, 1], BFT), ("THF", [8, 1], F32), ("DT", [8, 8], BFT),
-        ("PID", [128, 1], I32), ("PI2", [128, 1], I32), ("WT", [128, 4], I32), ("AI", [128, 1], I32), ("AI2", [128, 1], I32), ("BX", [128, 1], I32), ("BY", [128, 1], I32),
-        ("NZ", [128, 1], F32), ("COEF", [128, 1], F32), ("WCOL", [128, 1], F32), ("AR", [128, 1], F32), ("A4", [128, 1], F32), ("CSQ", [128, 1], F32), ("CCT", [128, 1], F32),
-        ("K1", [128, 1], F32), ("K2", [128, 1], F32), ("KM", [128, 1], F32), ("KZ", [128, 1], F32), ("PF0", [128, 1], F32), ("PF1", [128, 1], F32), ("BA", [128, 1], F32), ("BB", [128, 1], F32), ("BC", [128, 1], F32),
-        ("BD", [128, 1], F32), ("BE", [128, 1], F32), ("TH", [8, 1], I32), ("WN", [8, 512], I32), ("WNF", [8, 512], F32), ("WL", [128, 256], I32),
-        ("BW1", [128, 32], I32), ("BW0", [128, 32], I32), ("L7", [128, 32], I32), ("FVM", [128, 256], F32), ("LI", [128, 64], I32), ("LQ", [128, 96], I32),
-        ("LOFF", [128, 96], U16), ("ZS", [128, 512], F32), ("ZX", [128, 512], BFT), ("ZI", [128, 512], BFT), ("YN", [8, 512], F32)):
+        ("ONES", [128, 128], BFT), ("B1", [128, 128], BFT), ("B", [128, 128], BFT), ("IB", [128, 128], BFT), ("CL", [128, 128], BFT),
+        ("IH", [128, 128], F16), ("H2K", [128, 128], F16), ("H8K", [128, 128], F16), ("ONEF", [128, 128], F32), ("F4K", [128, 128], F32),
+        ("CR", [128, 512], BFT), ("PR32", [128, 32], F32), ("E81", [8, 128], BFT), ("E8", [8, 128], BFT), ("TB", [8, 128], BFT), ("CK", [64, 1152], BFT),
+        ("WM", [128, 8], BFT), ("BW", [128, 128], BFT), ("NK0", [128, 128], BFT), ("C8", [128, 128], BFT), ("RSF", [128, 128], BFT), ("RS", [128, 512], BFT), ("RS4", [128, 256], BFT), ("M192", [128, 512], BFT),
+        ("THB", [8, 1], BFT), ("THC", [8, 1], F32), ("PID", [128, 1], I32), ("PI2", [128, 1], I32), ("WT", [128, 4], I32), ("AI", [128, 1], I32), ("AI2", [128, 1], I32),
+        ("BX", [128, 1], I32), ("BY", [128, 1], I32), ("NZ", [128, 1], F32), ("COEF", [128, 1], F32), ("WCOL", [128, 1], F32), ("A8", [128, 1], F32),
+        ("BA", [128, 1], F32), ("BE", [128, 1], F32), ("TH", [8, 1], I32), ("WN", [8, 512], I32), ("WNB", [8, 512], BFT), ("WL", [128, 256], I32),
+        ("BW1", [128, 32], I32), ("BASE", [128, 64], I32), ("FVM", [128, 128], F32), ("LI", [128, 32], I32), ("LR", [128, 64], I32), ("LQ", [128, 64], I32),
+        ("LOFF", [128, 64], U16), ("ZS", [128, 512], BFT), ("ZX", [128, 512], BFT), ("YN", [8, 512], F32)):
     _sb(_n, _s, _t)
 for _b in "01":
     for _n, _s, _t in (
-            ("V", [128, 2064], BFT), ("AD", [128, 2048], BFT), ("XH", [128, 2048], BFT), ("AE", [128, 2048], BFT),
-            ("OFF", [128, 128], U16), ("HOFF", [128, 128], U16), ("DEAD", [128, 16, 8], BFT), ("NM", [128, 16, 8], I32), ("NF", [128, 128], F32),
-            ("S", [128, 16, 9], BFT), ("NS", [128, 128], BFT), ("SP", [128, 128], BFT), ("C", [128, 128], BFT), ("CN", [128, 128], BFT), ("CE", [128, 16, 8], BFT),
-            ("CX", [128, 16, 4], BFT), ("SN", [128, 128], F32), ("AX", [128, 128], F32), ("T0", [128, 16, 8], F32), ("TI", [128, 16, 8], I32), ("TJ", [128, 16, 8], I32),
-            ("KP", [128, 16, 8], BFT), ("CT", [128, 16, 8], F32), ("WI", [128, 16, 8], I32), ("HI", [128, 16, 8], I32), ("HF", [128, 128], F32),
-            ("FS", [128, 256], F32), ("FO", [128, 256], F32),
-            ("MO", [128, 512], BFT), ("MV", [128, 256], BFT), ("N2", [128, 16, 8], I32), ("N3", [128, 16, 8], I32),
-            ("PRO", [128, 512], F32), ("PRV", [128, 256], F32), ("OSO", [128, 512], F32), ("OSV", [128, 256], F32),
-            ("J", [128, 16, 4], I32), ("JM", [128, 16, 4], I32), ("YL", [128, 128], F32), ("NA", [128, 16, 4], F32), ("NC", [128, 16, 2], F32), ("NN", [128, 16], F32)):
+            ("V", [128, 2064], BFT), ("M", [128, 2048], BFT), ("XH", [128, 2048], BFT), ("AE", [128, 2048], BFT),
+            ("OFF", [128, 128], U16), ("HOFF", [128, 128], U16), ("LE", [128, 16, 9], BFT), ("LP", [128, 16, 5], BFT), ("NM", [128, 16, 8], I32), ("NF", [128, 16, 8], F16),
+            ("SG", [128, 144], BFT), ("CS", [128, 128], BFT), ("C", [128, 16, 8], BFT), ("K", [128, 128], BFT), ("K2", [128, 128], BFT), ("KX", [128, 16, 8], BFT),
+            ("KY", [128, 64], BFT), ("KY2", [128, 64], BFT), ("AS", [128, 1], F32), ("TA", [128, 128], F32), ("TI", [128, 16, 8], I32), ("TJ", [128, 16, 8], I32), ("N1", [128, 16, 8], F16),
+            ("KP", [128, 128], BFT), ("SQ", [128, 128], F32), ("U", [128, 128], F32), ("WI", [128, 16, 8], I32), ("HI", [128, 16, 8], I32), ("HF", [128, 16, 8], F16), ("Q", [128, 16, 8], F16),
+            ("FO", [128, 128], F32), ("OSO", [128, 512], F32), ("OSV", [128, 256], F32), ("J", [128, 16, 4], I32), ("YL", [128, 128], F32)):
         _sb(_n + _b, _s, _t)
     for _i in range(NV):
         for _n in ("SO", "SV", "RO", "RV"):
@@ -55,9 +59,9 @@ for _b in "01":
 
 DMAS = ["xv", "wl", "wn", "wt", "th", "yx", "yl0", "yl1", "yn"]
 SEMAPHORES = ["qv", "qs", "qp", "qg", "ls"] + ["d_" + n for n in DMAS] + ["r%s%d%d" % (k, t, b) for k in "xm" for t in range(NV) for b in (0, 1)]
-CY = 0.00104
-PC = 0.00052
-HOP = 0.08
+CY = 0.00085
+PC = 0.00044
+HOP = 0.075
 
 
 def rank_program(g, core, T, topo):
@@ -69,7 +73,7 @@ def rank_program(g, core, T, topo):
     A, F = AluOpType, ActivationFunctionType
     V, S, P = g.vector, g.scalar, g.tensor
     D = {k: T[b][:, i] for k, (b, i) in VIEWS.items()}
-    X, Z, PT, PV, L = T.X, T.Z, T.PT, T.PV, [T.L0, T.L1, T.L2]
+    X, Z, DD, D3, TO, TV, L = T.X, T.Z, T.DD, T.D3, T.TO, T.TV, [T.L0, T.L1]
     tiles = [slice(128 * k, 128 * k + 128) for k in range(4)]
     UB, WB = [T.UB[:, k] for k in tiles], [[w[:, k] for k in tiles] for w in (T.W0, T.W1)]
     tt, mm, sc, act, mset, copy = V.tensor_tensor, P.matmul, V.tensor_tensor_scan, S.activation, V.memset, V.tensor_copy
@@ -80,10 +84,10 @@ def rank_program(g, core, T, topo):
         return len(ops) - 1
 
     def v(r, w, cyc, fn, b=()):
-        return op("v", r, w, 0.03 + CY * max(cyc, 64), lambda: [fn()], b)
+        return op("v", r, w, 0.05 + CY * max(cyc, 64), lambda: [fn()], b)
 
     def s(r, w, cyc, fn, b=()):
-        return op("s", r, w, 0.03 + CY * max(cyc, 64), lambda: [fn()], b)
+        return op("s", r, w, 0.065 + CY * max(cyc, 64), lambda: [fn()], b)
 
     def p(r, w, cyc, fn, b):
         return op("p", r, w, PC * cyc, fn, b)
@@ -102,282 +106,264 @@ def rank_program(g, core, T, topo):
     def gcopy(out, in_, n):
         return g.affine_select(out, in_, [[0, n]], A.is_equal, 0.0, 0, 0)
 
-    nl = [0]
+    def pcs(tok, a, e):
+        return " ".join("%s.%d" % (tok, i) for i in range(a, e))
 
-    def lane():
-        nl[0] += 1
-        return (nl[0] - 1) % len(L)
+    CKT, CKC, CKF, CKU, CKD, CKN = slice(0, 512), slice(512, 640), slice(640, 768), slice(768, 896), slice(896, 1024), slice(1024, 1152)
+
+    def const(out, cols):
+        return mm(out, D["ONES"][0:33, :], D["CK"][0:33, cols], True, False)
 
     ld("y", "wl", D["WL"], T.wl[:], "", "WL", 2.0)
-    ld("y", "xv", X[:, 0:W], T.xv[:], "", "X", 7.0)
+    ld("y", "xv", X[:, 0:W], T.xv[:], "", "X", 6.0)
     ld("d", "th", D["TH"], T.th[:], "", "TH", 2.0)
     ld("d", "wt", D["WT"][:, 0:1], T.wt[:], "", "WT", 2.0)
     ld("d", "wn", D["WN"], T.wn[:], "", "WN", 2.0)
     v("", "ONES", 64, lambda: mset(D["ONES"], 1.0))
-    gg("ONES", "B1", 0.5, lambda: g.affine_select(D["B1"], D["ONES"], [[-16, 8], [0, 16]], A.is_ge, 0.0, 0, 1))
-    gg("B1", "B", 0.5, lambda: g.affine_select(D["B"], D["B1"], [[16, 8], [0, 16]], A.is_ge, 0.0, 15, -1))
-    gg("ONES", "IB", 0.5, lambda: g.affine_select(D["IB"], D["ONES"], [[-1, 128]], A.is_equal, 0.0, 0, 1))
-    gg("ONES", "E81", 0.5, lambda: g.affine_select(D["E81"], T.b_128_128_bfloat16[0:8, VIEWS["ONES"][1]], [[1, 128]], A.is_ge, 0.0, 0, -16))
-    gg("E81", "E8", 0.5, lambda: g.affine_select(D["E8"], D["E81"], [[-1, 128]], A.is_ge, 0.0, 15, 16))
+    gg("ONES", "IB", 0.4, lambda: g.affine_select(D["IB"], D["ONES"], [[-1, 128]], A.is_equal, 0.0, 0, 1))
+    gg("ONES", "B1", 0.4, lambda: g.affine_select(D["B1"], D["ONES"], [[-16, 8], [0, 16]], A.is_ge, 0.0, 0, 1))
+    gg("B1", "B", 0.4, lambda: g.affine_select(D["B"], D["B1"], [[16, 8], [0, 16]], A.is_ge, 0.0, 15, -1))
+    gg("ONES", "E81", 0.4, lambda: g.affine_select(D["E81"], D["ONES"][0:8, :], [[1, 128]], A.is_ge, 0.0, 0, -16))
+    gg("E81", "E8", 0.4, lambda: g.affine_select(D["E8"], D["E81"], [[-1, 128]], A.is_ge, 0.0, 15, 16))
     gg("", "PID", 0.2, lambda: g.iota(D["PID"], [[0, 1]], 0, 1))
-    gg("", "BW1", 0.3, lambda: g.iota(D["BW1"], [[16, 32]], 0, 0))
+    gg("", "BW1", 0.2, lambda: g.iota(D["BW1"], [[16, 32]], 0, 0))
+    CK = D["CK"]
+    v("", "CK0", 576, lambda: mset(CK, 0.0))
+    gg("CK0", "CKF", 0.4, lambda: g.iota(CK[0:1, CKF], [[0, 16], [8192, 8]], -31 * 8192, 0, allow_small_or_imprecise_dtypes=True))
+    gg("CK0", "CKN", 0.4, lambda: g.iota(CK[0:1, CKN], [[0, 16], [-1, 8]], 0, 0, allow_small_or_imprecise_dtypes=True))
+    for q in range(4):
+        v("CK0", "CKT%d" % q, 64, lambda q=q: mset(CK[0:1, 128 * q:128 * q + 128], -BIG * (2 * q + 1) ** 2))
+    for k, r, cols, c in (("CKT", 32, CKT, 2048.0), ("CKC", 0, CKC, 32768.0), ("CKc", 32, CKC, 208.0), ("CKf", 32, CKF, 129.0 * 4096), ("CKD", 0, CKD, -120.0)):
+        v("CK0", k, 256 if k == "CKT" else 64, lambda r=r, cols=cols, c=c: mset(CK[r:r + 1, cols], c))
     for b in (0, 1):
-        v("WL", "OFF%d" % b, 128, lambda b=b: copy(D["OFF%d" % b], D["WL"][:, 128 * b:128 * b + 128]))
-        v("", "V%dz" % b, 64, lambda b=b: mset(D["V%d" % b][:, 0:16], 0.0))
-        v("", "S%d9" % b, 64, lambda b=b: mset(D["S%d" % b][:, :, 8], 1.0))
-    v("IB", "IDF", 128, lambda: copy(D["IDF"], D["IB"]))
-    for k, src, c in (("NIB", "IB", -1.0), ("NB", "B", -16.0), ("N4", "IB", -4096.0), ("P4", "IB", 4096.0), ("P16", "IB", 65536.0)):
+        x = str(b)
+        v("WL", "OFF" + x, 128, lambda b=b, x=x: copy(D["OFF" + x], D["WL"][:, 128 * b:128 * b + 128]))
+        v("WL", "NF" + x, 128, lambda b=b, x=x: ts(D["NF" + x], D["WL"][:, 128 * b:128 * b + 128], -2048.0, None, A.add))
+        v("", "V%sz" % x, 64, lambda x=x: mset(D["V" + x][:, 0:16], -32.0))
+        v("", "SGz" + x, 64, lambda x=x: mset(D["SG" + x][:, 128:144], -1.0))
+        v("", "LEz" + x, 64, lambda x=x: mset(D["LE" + x][:, :, 0], -0.5))
+        v("", "LPz" + x, 64, lambda x=x: mset(D["LP" + x][:, :, 0], -0.5))
+    for k, src, c in SCALED + (("F4K", "IB", 4096.0),):
+        s(src, k, 128, lambda k=k, src=src, c=c: act(D[k], D[src], F.Copy, scale=c))
+    for k, src, c in (("IH", "IB", 1.0), ("H2K", "IB", 2048.0), ("H8K", "IB", 8192.0)):
         v(src, k, 64, lambda k=k, src=src, c=c: ts(D[k], D[src], c, None, A.mult))
-    v("", "CRa", 256, lambda: mset(D["CR"], 1.0))
-    v("CRa", "CR", 64, lambda: mset(D["CR"][:, 0:512:8], -64.0))
+    for k, c, c0, st, w in (("CR", 4.0, -256.0, 8, 512), ("NK0", 1.0, 0.0, 8, 128), ("RSF", 2.0 ** 30, 4096.0, 8, 128), ("RS", 2.0 ** 30, EMPTY, 8, 512), ("RS4", 2.0 ** 30, EMPTY, 4, 256)):
+        v("", k + "a", w // 2, lambda k=k, c=c: mset(D[k], c))
+        v(k + "a", k, 64, lambda k=k, c0=c0, st=st: mset(D[k][:, 0::st], c0))
+    for k, c, w in (("C8", 0.125, 64), ("M192", -192.0, 256), ("ONEF", 1.0, 128), ("A8", 2.0 ** 24, 64), ("FVM", 0.0, 128)):
+        v("", k, w, lambda k=k, c=c: mset(D[k], c))
     v("TH", "THB", 64, lambda: copy(D["THB"], D["TH"]))
-    v("TH", "THF", 64, lambda: copy(D["THF"], D["TH"]))
+    v("TH", "THC", 64, lambda: ts(D["THC"], D["TH"], 64.0, -8192.0, A.mult, A.add))
     v("PID", "PI2", 64, lambda: ts(D["PI2"], D["PID"], 15, None, A.bitwise_and))
-    v("PI2", "NZ", 64, lambda: ts(D["NZ"], D["PI2"], 0.0, None, A.is_gt))
-    p("E8 THB", "PTth", 64, lambda: [mm(PT[:, 304:305], D["E8"], D["THB"], True, True)], ["PT"])
-    v("PTth NZ", "COEF", 64, lambda: tt(D["COEF"], PT[:, 304:305], D["NZ"], A.add), ["PT"])
+    v("PI2", "NZ", 64, lambda: ts(D["NZ"], D["PI2"], 0.0, None, A.is_equal))
+    p("E8 THB", "UF0", 64, lambda: [mm(T.UB[:, 304:305], D["E8"], D["THB"], True, True)], ["UB"])
+    v("UF0 NZ", "COEF", 64, lambda: tt(D["COEF"], T.UB[:, 304:305], D["NZ"], A.add), ["UB"])
     v("B COEF", "CL", 64, lambda: ts(D["CL"], D["B"], D["COEF"], None, A.mult))
-    v("THF IB", "DT", 64, lambda: ts(D["DT"], D["IB"][0:8, 0:8], D["THF"], None, A.mult))
-    p("ONES DT", "W0.0", 1024, lambda: [mm(WB[0][0][:, m:128:16], D["ONES"][0:8, :], D["DT"], True, True) for m in range(16)], ["W0"])
-    v("W0.0", "BIa", 128, lambda: ts(D["BIASC"], WB[0][0], -1.0, None, A.mult), ["W0"])
-    v("BIa", "BIASC", 64, lambda: mset(D["BIASC"][:, :, 0], 8192.0))
+    v("THC E8", "TBa", 64, lambda: ts(D["TB"], D["E8"], D["THC"], None, A.mult))
+    v("TBa", "TB", 64, lambda: mset(D["TB"][:, 0::8], -16384.0))
     v("WT", "WCOL", 64, lambda: copy(D["WCOL"], D["WT"][:, 0:1]))
-    v("B WCOL", "WM", 64, lambda: ts(D["WM"], D["B"][:, 0:128:16], D["WCOL"], None, A.mult))
-    for k, c in (("C129", 129.0), ("C128", 128.0), ("A4", 0.0), ("CSQ", 4096.0 + 592.0), ("CCT", -360240.0), ("K1", 1.0), ("K2", 2.0), ("KM", -1.0), ("KZ", 257.5)):
-        v("", k, 64, lambda k=k, c=c: mset(D[k], c))
-    v("", "NKa", 64, lambda: mset(D["NK0"], 1.0))
-    v("NKa", "NK0", 64, lambda: mset(D["NK0"][:, 0::8], 0.0))
-    v("WN", "WNF", 512, lambda: copy(D["WNF"], D["WN"]))
+    v("B WCOL", "WM", 64, lambda: ts(D["WM"], D["B"][:, 0:128:16], D["WCOL"], 1.0 / 4096, A.mult, A.mult))
+    v("B WCOL", "BW", 64, lambda: ts(D["BW"], D["B"], D["WCOL"], 32.0 / 4096, A.mult, A.mult))
+    for q in range(4):
+        v("IB", "PR%d" % q, 64, lambda q=q: copy(D["PR32"][32 * q:32 * q + 32, :], D["IB"][32 * q:32 * q + 32, 32 * q:32 * q + 32]))
+    v("PID", "BX", 64, lambda: ts(D["BX"], D["PID"], 7, None, A.bitwise_and))
+    v("PID", "BY", 64, lambda: ts(D["BY"], D["PID"], 8, None, A.bitwise_and))
+    v("BX", "BA", 64, lambda: ts(D["BA"], D["BX"], 512.0, None, A.mult))
+    v("BY BA", "BE", 64, lambda: ts(D["BE"], D["BY"], D["BA"], None, A.add))
+    v("BW1 BE", "BASEa", 64, lambda: ts(D["BASE"][:, 0:32], D["BW1"], D["BE"], -1.0, A.add, A.add))
+    v("BW1 BE", "BASE", 64, lambda: ts(D["BASE"][:, 32:64], D["BW1"], D["BE"], None, A.add))
+    v("WN", "WNB", 512, lambda: copy(D["WNB"], D["WN"]))
     for b in (0, 1):
-        p("WNF IDF", "PTn%d" % b, 512, lambda b=b: [P.transpose(PT[:, 320 + 16 * b + w1:336 + 16 * b:2], D["WNF"][:, 256 * b + w1:256 * b + 256:2], D["IDF"][0:8, 0:8]) for w1 in (0, 1)], ["PT"])
-        for k in range(8):
-            v("PTn%d" % b + (" " + " ".join("DE%d%d" % (b, i) for i in range(7)) if k == 7 else ""), "DEAD%d" % b if k == 7 else "DE%d%d" % (b, k), 64,
-              lambda b=b, k=k: ts(D["DEAD%d" % b][:, :, k], PT[:, 320 + 16 * b:336 + 16 * b], float(k), None, A.is_le), ["PT"])
-        v("WL", "NF%d" % b, 128, lambda b=b: copy(D["NF%d" % b], D["WL"][:, 128 * b:128 * b + 128]))
-        p("NF%d IDF" % b, "PTN", 512, lambda b=b: [P.transpose(PT[:, 128:256], D["NF%d" % b], D["IDF"])], ["PT"])
-        v("PTN", "NM%d" % b, 128, lambda b=b: copy(D["NM%d" % b], PT[:, 128:256]), ["PT"])
-
-    def late_constants():
-        v("", "FRa", 256, lambda: mset(D["FR"], 1.0))
-        v("FRa", "FR", 64, lambda: mset(D["FR"][:, 0::8], 0.0))
-        v("", "CROa", 512, lambda: mset(D["CRO"], 1.0))
-        v("CROa", "CRO", 64, lambda: mset(D["CRO"][:, 0::8], 0.0))
-        v("", "CRVa", 256, lambda: mset(D["CRV"], 1.0))
-        v("CRVa", "CRV", 64, lambda: mset(D["CRV"][:, 0::4], 0.0))
-        v("", "FVM", 256, lambda: mset(D["FVM"], 0.0))
-        v("PID", "PF0", 64, lambda: copy(D["PF0"], D["PID"]))
-        v("PF0", "PF1", 64, lambda: ts(D["PF1"], D["PF0"], 128.0, None, A.add))
-        for b in (0, 1):
-            v("PF%d C129" % b, "KA%d" % b, 64, lambda b=b: ts(D["KA%d" % b], D["C129"], 0.0, D["PF%d" % b], A.mult, A.add))
-        for k in range(16):
-            v("", "KB.%d" % k, 64, lambda k=k: mset(D["KB"][:, k // 8::2, k % 8], float(k)))
-        for q in range(4):
-            v("IDF", "PR%d" % q, 64, lambda q=q: copy(D["PR32"][32 * q:32 * q + 32, :], D["IDF"][32 * q:32 * q + 32, 32 * q:32 * q + 32]))
-        v("PI2", "BX", 64, lambda: ts(D["BX"], D["PI2"], 3, None, A.bitwise_and))
-        v("PI2", "BY", 64, lambda: ts(D["BY"], D["PI2"], 2, 1, A.arith_shift_right, A.bitwise_and))
-        v("BX", "BA", 64, lambda: ts(D["BA"], D["BX"], 512.0, None, A.mult))
-        v("BY", "BB", 64, lambda: ts(D["BB"], D["BY"], 2048.0, None, A.mult))
-        v("BA BB", "BC", 64, lambda: tt(D["BC"], D["BA"], D["BB"], A.add))
-        v("PI2", "BD", 64, lambda: ts(D["BD"], D["PI2"], 8.0, 8.0, A.is_ge, A.mult))
-        v("BC BD", "BE", 64, lambda: tt(D["BE"], D["BC"], D["BD"], A.add))
-        v("BW1 BE", "BW0", 64, lambda: ts(D["BW0"], D["BW1"], D["BE"], None, A.add))
-
-    def gather(out, base, off, r, tok, calls):
-        for q, a, e in calls:
-            w = " ".join("%s.%d" % (tok, i) for i in range(a, e))
-            o, x = out[:, base + 512 * a:base + 512 * e], off[:, 32 * a:32 * e]
-            if q == "s":
-                s(r, w, (e - a) * 512 * 1.5, lambda o=o, x=x: act(o, X[:, 0:W].indirect(x), F.Copy))
-            else:
-                v(r, w, (e - a) * 512 * 1.5, lambda o=o, x=x: copy(o, X[:, 0:W].indirect(x)))
-
-    def lanesum(wb, k, m, src, mov, start, stop, o=0):
-        return mm(wb[k][:, m:128:16], src[:, o + m:o + 2048:16], mov, start, stop)
+        p("WNB E8 ONES CKN", "D3.%d" % (2 + b), 256, lambda b=b: [const(D3[:, 2 + b], CKN)] + [
+            mm(D3[:, 2 + b, :, 8 * w1:8 * w1 + 8], D["WNB"][:, 256 * b + w1:256 * b + 256:2], D["E8"][:, 0:128:2], False, w1 == 1) for w1 in (0, 1)], ["D3"])
+        v("D3.%d" % (2 + b), "LA%d" % b, 128, lambda b=b: ts(D["LE%d" % b][:, :, 1:9], D3[:, 2 + b], 0.0, -0.5, A.is_gt, A.add), ["D3"])
 
     def phase1(t, b):
-        x = str(b)
-        Vb, AD, wb, w_ = D["V" + x], D["AD" + x], WB[b], "W" + x
-        gather(Vb, 16, D["OFF" + x], "X OFF" + x, "V" + x, CALLS1[b])
+        x, nm = str(b), BYMAX[b]
+        Vb, M, y = D["V" + x], D["M" + x], D3[:, b]
+        for q, a, e in GATHER1[b]:
+            o, w = Vb[:, 16 + 512 * a:16 + 512 * e], X[:, 0:W].indirect(D["OFF" + x][:, 32 * a:32 * e])
+            if q == "s":
+                s("X OFF" + x, pcs("V" + x, a, e), (e - a) * 512 * 1.56, lambda o=o, w=w: act(o, w, F.Identity, bias=-32.0))
+            else:
+                v("X OFF" + x, pcs("V" + x, a, e), (e - a) * 512 * 1.56, lambda o=o, w=w: ts(o, w, -32.0, None, A.add))
+
+        def before(c):
+            return "V%sz" % x if c == 0 else "V%s.%d" % (x, c - 1)
+        for a, e in NEIGH[b]:
+            r, v0, v1 = slice(512 * a, 512 * e), Vb[:, 15 + 512 * a:15 + 512 * e], Vb[:, 16 + 512 * a:16 + 512 * e]
+            rd = before(a) + " " + pcs("V" + x, a, e)
+            if a < nm:
+                v(rd, pcs("M" + x, a, e), 256 * (e - a), lambda r=r, v0=v0, v1=v1: sc(M[:, r], v0, v1, 0.0, A.min, A.max))
+            else:
+                v(rd, pcs("XH" + x, a, e), 256 * (e - a), lambda r=r, v0=v0, v1=v1: sc(D["XH" + x][:, r], v1, v0, 0.0, A.min, A.subtract))
+                s(pcs("XH" + x, a, e), pcs("M" + x, a, e), 512 * (e - a), lambda r=r: act(M[:, r], D["XH" + x][:, r], F.Abs, scale=0.5))
         for c in range(4):
-            j = 512 * c
-            i = lane()
-            p("V%s.%d %s IB NIB" % (x, c, "V%sz" % x if c == 0 else "V%s.%d" % (x, c - 1)), "L%d" % i, 1024,
-              lambda j=j, i=i: [mm(L[i][:], D["IB"], Vb[:, 16 + j:528 + j], True, False), mm(L[i][:], D["NIB"], Vb[:, 15 + j:527 + j], False, True)], ["L%d" % i])
-            s("L%d" % i, "AD%s.%d" % (x, c), 512, lambda j=j, i=i: act(AD[:, j:j + 512], L[i][:], F.Abs), ["L%d" % i])
-            i = lane()
-            p("CL CR", "L%d" % i, 512, lambda i=i: [mm(L[i][:], D["CL"], D["CR"], True, False)], ["L%d" % i])
-            p("AD%s.%d NB" % (x, c), "L%d" % i, 512, lambda j=j, i=i: [mm(L[i][:], D["NB"], AD[:, j:j + 512], False, True)], ["L%d" % i])
-            v("L%d V%s.%d" % (i, x, c), "Z%s.%d" % (x, c), 512, lambda j=j, i=i: sc(Z[:, 2048 * b + j:2048 * b + j + 512], L[i][:], Vb[:, 16 + j:528 + j], 0.0, A.min, A.max), ["L%d" % i])
-        p("IB BIASC P4 DEAD%s DE%sa" % (x, x), w_ + ".0", 256, lambda: [mm(wb[0], D["IB"], D["BIASC"], True, False), mm(wb[0], D["P4"], D["DEAD" + x], False, False)], [w_])
-        p(" ".join("AD%s.%d" % (x, c) for c in range(4)) + " B", w_ + ".0", 1024,
-          lambda: [lanesum(wb, 0, m, AD, D["B"][:, 0:128:16], False, m == 15) for m in range(16)], [w_])
-        v(w_ + ".0", "S" + x, 128, lambda: ts(D["S" + x][:, :, 0:8], wb[0], 0.0, None, A.is_gt), [w_])
-        p("S%s S%s9 DEAD%s DE%sa IB NIB" % (x, x, x, x), w_ + ".1", 256, lambda: [mm(wb[1], D["IB"], D["S" + x][:, :, 1:9], True, False), mm(wb[1], D["NIB"], D["DEAD" + x], False, True)], [w_])
+            j, i = 512 * c, c % 2
+            k = "L%d" % i
+            p("CL CR", k, 512, lambda i=i: [mm(L[i][:], D["CL"], D["CR"], True, False)], [k])
+            if c < nm:
+                p("V%s.%d %s B16" % (x, c, before(c)), k, 1024, lambda j=j, i=i: [mm(L[i][:], D["B16"], Vb[:, o + j:o + 512 + j], False, False) for o in (15, 16)], [k])
+            p("M%s.%d NB32" % (x, c), k, 512, lambda j=j, i=i: [mm(L[i][:], D["NB32"], M[:, j:j + 512], False, True)], [k])
+            v("%s V%s.%d" % (k, x, c), "Z%s.%d" % (x, c), 512, lambda j=j, i=i: sc(Z[:, 2048 * b + j:2048 * b + j + 512], L[i][:], Vb[:, 16 + j:528 + j], 0.0, A.min, A.max), [k])
+        LE, LP, ym, end = D["LE" + x], D["LP" + x], y[0:32 * nm] if nm else None, 16 + 512 * nm
+        p("ONES TB P4 LA%s B16 %s" % (x, pcs("V" + x, 0, nm)), "D3." + x, 256 + 16 * min(64, 32 * nm),
+          lambda: [mm(y, D["ONES"][0:8, :], D["TB"], True, False)]
+          + ([mm(y, D["P4"], LE[:, :, 1:9], False, False)] if t == 0 else [mm(y[:, :, o::2], D["P4"], LP[:, :, 1:5], False, False) for o in (0, 1)])
+          + [mm(ym[:, :, m:m + 2], Vb[:, 16 + m:end:16], D["B16"][:, 0:128:8], False, False) for m in range(15 if nm else 0)]
+          + ([mm(ym[:, :, 15], Vb[:, 31:end:16], D["B16"][:, 0:128:16], False, False)] if nm else []), ["D3"])
+        p(pcs("M" + x, 0, 4) + " NB32", "D3." + x, 1024, lambda: [mm(y[:, :, m], M[:, m:2048:16], D["NB32"][:, 0:128:16], False, m == 15) for m in range(16)], ["D3"])
+        s("D3." + x, "SG" + x, 128, lambda: act(D["SG" + x][:, 0:128], y, F.Sign, bias=8.0), ["D3"])
 
     def runs(t, b):
         x, y = str(b), "%d%d" % (t, b)
-        wb, w_, Sx = WB[b], "W" + x, D["S" + x][:, :, 0:8]
-        s("S%s K1" % x, "NS" + x, 128, lambda: act(D["NS" + x], Sx, F.Identity, bias=D["K1"], scale=-1.0))
-        s("S%s K2" % x, "SP" + x, 128, lambda: act(D["SP" + x], Sx, F.Identity, bias=D["K2"]))
-        v("NS%s SP%s" % (x, x), "C" + x, 64, lambda: sc(D["C" + x], D["NS" + x], D["SP" + x], 0.0, A.mult, A.add))
-        s("C%s CCT" % x, "CT" + x, 128, lambda: act(D["CT" + x], D["C" + x], F.Identity, bias=D["CCT"], scale=9776.0))
-        v(w_ + ".1 NK0", "CN" + x, 128, lambda: sc(D["CN" + x], D["NK0"], wb[1], 0.0, A.mult, A.add), [w_])
-        s("CN" + x, "MX" + y, 16, lambda: act(D["MX" + y], D["CN" + x][:, 7::8], F.Copy))
+        wb, w_, SG, LE, LP, K = WB[b], "W" + x, D["SG" + x], D["LE" + x], D["LP" + x], D["K" + x]
+        v("SG%s C8" % x, "CS" + x, 64, lambda: sc(D["CS" + x], SG[:, 0:128], D["C8"], 0.0, A.min, A.add))
+        s("CS" + x, "C" + x, 128, lambda: act(D["C" + x], D["CS" + x], F.Identity, bias=17.0, scale=16.0))
+        lam = [(wb[0], "IB", LE[:, :, 1:9]), (wb[0], "IB", LE[:, :, 0:8])] if t == 0 else \
+              [(wb[0][:, 0::2], "IB", LP[:, :, 1:5]), (wb[0][:, 0::2], "IB", LP[:, :, 0:4]), (wb[0][:, 1::2], "I2", LP[:, :, 1:5])]
+        p("SG%s SGz%s LA%s LEz%s LPz%s NH IB I2" % (x, x, x, x, x), w_ + ".0", 448,
+          lambda: [mm(wb[0], D["NH"], SG[:, 1:129], True, False), mm(wb[0], D["NH"], SG[:, 0:128], False, False)]
+          + [mm(o, D[k], m, False, i == len(lam) - 1) for i, (o, k, m) in enumerate(lam)], [w_])
+        v(w_ + ".0 NK0", "K" + x, 128, lambda: sc(K, D["NK0"], wb[0], 0.0, A.mult, A.add), [w_])
+        p("K%s LA%s IB" % (x, x), w_ + ".0", 128, lambda: [mm(wb[0][:, 0:16], D["IB"], K[:, 7::8], True, False), mm(wb[0][:, 0:16], D["IB"], LE[:, :, 8] if t == 0 else LP[:, :, 4], False, True)], [w_])
+        s(w_ + ".0", "MX%s AS%s" % (y, x), 64, lambda: act(D["MX" + y], wb[0][:, 0:16], F.Identity, bias=0.5, accum_out=D["AS" + x]), [w_])
         i = op("g", "MX" + y, "", 0.8, lambda: [send_counts(y)], sem="none")
         op("r", "", "MR" + y, 0.0, None, sem="rm" + y, inc=len(count_engines(nxt, core)), after=[i], lat=3.0)
+        s("K" + x, "K2" + x, 128, lambda: act(D["K2" + x], K, F.Square))
+        s("K" + x, "KX" + x, 128, lambda: act(D["KX" + x], K, F.Relu, bias=-8.0))
 
     def upart(t, b):
         x = str(b)
-        wb, w_ = WB[b], "W" + x
-        zs = " ".join("Z%s.%d" % (x, c) for c in range(4))
-        zo = 2048 * b
-        p(zs + " P4 C129 WM", w_ + ".2", 1200, lambda: [mm(wb[2], D["P4"], D["C129"], True, False)] + [lanesum(wb, 2, m, Z[:, zo:zo + 2048], D["WM"], False, m == 15) for m in range(16)], [w_])
-        p(zs + " P4 C128 WM", "UB%sa" % x, 1200, lambda: [mm(UB[b], D["P4"], D["C128"], True, False)] + [lanesum(UB, b, m, Z[:, zo:zo + 2048], D["WM"], False, False) for m in range(16)], ["UB"])
-        v(w_ + ".2", "KP" + x, 128, lambda: ts(D["KP" + x], wb[2], 1.0 / 4096, -0.5 + 1.0 / 8192, A.mult, A.add), [w_])
-        p("KP%s N4 UB%sa" % (x, x), "UB%s UB%sa" % (x, x), 128, lambda: [mm(UB[b], D["N4"], D["KP" + x], False, True)], ["UB"])
-        s("UB%s CSQ" % x, "SQ" + x, 128, lambda: act(UB[2 + b], UB[b], F.Square, bias=D["CSQ"]), ["UB"])
-
-    def hpart(t, b):
-        x = str(b)
-        v("SQ%s CT%s" % (x, x), "WI" + x, 128, lambda: tt(D["WI" + x], D["CT" + x], UB[2 + b], A.add), ["UB"])
-        v("WI" + x, "HI" + x, 128, lambda: ts(D["HI" + x], D["WI" + x], 5, 4095, A.arith_shift_right, A.bitwise_and))
-        v("HI" + x, "HF" + x, 128, lambda: copy(D["HF" + x], D["HI" + x]))
-        p("HF%s IDF" % x, "PTH", 512, lambda: [P.transpose(PT[:, 0:128], D["HF" + x], D["IDF"])], ["PT"])
-        v("PTH", "HOFF" + x, 128, lambda: copy(D["HOFF" + x], PT[:, 0:128]), ["PT"])
+        u, zo = UB[b], 2048 * b
+        p("ONES BW", "UB" + x, 128, lambda: [mm(u, D["ONES"], D["BW"], True, False)], ["UB"])
+        p(pcs("Z" + x, 0, 4) + " WM", "UB" + x, 1024, lambda: [mm(u[:, m:128:16], Z[:, zo + m:zo + 2048:16], D["WM"], False, m == 15) for m in range(16)], ["UB"])
+        s("UB" + x, "KP" + x, 128, lambda: act(D["KP" + x], u, F.Identity, bias=128.5 + 1.0 / 8192), ["UB"])
+        v("KP%s UB%s" % (x, x), "U" + x, 128, lambda: tt(D["U" + x], u, D["KP" + x], A.subtract), ["UB"])
+        s("U" + x, "SQ" + x, 128, lambda: act(D["SQ" + x], D["U" + x], F.Square, bias=592.0 + 129 * 4096, scale=4096.0))
 
     def first1(t, b):
         x = str(b)
-        wb, w_, FS, M0 = WB[b], "W" + x, D["FS" + x], D["MO" + x][:, 0:128]
-        v("CN%s %s.1" % (x, w_), "CE" + x, 128, lambda: tt(D["CE" + x], D["CN" + x], wb[1], A.mult), [w_])
-        v("CE" + x, "MO%s.0" % x, 64, lambda: ts(M0, D["CE" + x], 1.0, None, A.is_equal))
-        v("MO%s.0 UB%s" % (x, x), "FS%sc" % x, 128, lambda: tt(FS[:, 128:256], M0, UB[b], A.mult), ["UB"])
-        p("HF%s IDF P16 P4 KA%s " % (x, x) + " ".join("KB.%d" % k for k in range(16)), w_ + ".2", 768,
-          lambda: [mm(wb[2], D["IDF"], D["HF" + x], True, False), mm(wb[2], D["P16"], D["KA" + x], False, False), mm(wb[2], D["P4"], D["KB"], False, True)], [w_])
-        v("MO%s.0 %s.2" % (x, w_), "FS%sa" % x, 128, lambda: tt(FS[:, 0:128], M0, wb[2], A.mult), [w_])
-        v("FR FS%sa FS%sc" % (x, x), "FO" + x, 256, lambda: sc(D["FO" + x], D["FR"], FS, 0.0, A.mult, A.add))
+        fs, w_ = WB[b][3], "W" + x
+        p("ONES CKF CKf F2 FN F4K U%s K%s K2%s" % (x, x, x), w_ + ".3", 896,
+          lambda: [const(fs, CKF), mm(fs, D["F4K"], D["U" + x], False, False), mm(fs, D["F2"], D["K" + x], False, False), mm(fs, D["FN"], D["K2" + x], False, True)], [w_])
+        v("RSF %s.3" % w_, "FO" + x, 128, lambda: sc(D["FO" + x], D["RSF"], fs, 4096.0, A.min, A.max), [w_])
         for q in range(4):
             r = slice(32 * q, 32 * q + 32)
-            gg("FVM FO" + x, "FV%s%d" % (x, q), 0.24, lambda r=r, q=q: gcopy(D["FVM"][r, 4 * b + q::8], D["FO" + x][r, 7::8], 32))
+            gg("FVM FO" + x, "FV%s%d" % (x, q), 0.2, lambda r=r, q=q: gcopy(D["FVM"][r, 4 * b + q::8], D["FO" + x][r, 7::8], 16))
 
-    def first2(t):
-        p(" ".join("FV%d%d" % (b, q) for b in (0, 1) for q in range(4)) + " ".join(" PR%d" % q for q in range(4)) + " P4 ONES", "PTL", 640,
-          lambda: [mm(PT[:, 256:288], D["FVM"][:, 0:128], D["PR32"], True, True), mm(PT[:, 288:320], D["P4"], D["ONES"][:, 0:32], True, False),
-                   mm(PT[:, 288:320], D["FVM"][:, 128:256], D["PR32"], False, True)], ["PT"])
-        LI, LQ = D["LI"], D["LQ"]
-        v("PTL", "LI", 64, lambda: copy(LI, PT[:, 256:320]), ["PT"])
-        v("LI", "L7", 64, lambda: ts(D["L7"], LI[:, 32:64], 4096 + 7, None, A.bitwise_and))
-        v("LI", "LQa", 64, lambda: ts(LQ[:, 0:32], LI[:, 0:32], 4095, None, A.bitwise_and))
-        v("LI", "LQb", 64, lambda: ts(LQ[:, 32:64], LI[:, 0:32], 12, None, A.arith_shift_right))
-        v("L7 BW0", "LQc", 64, lambda: tt(LQ[:, 64:96], D["L7"], D["BW0"], A.add))
-        v("LQa LQb LQc", "LOFF", 96, lambda: copy(D["LOFF"], LQ))
-
-    def update(t):
-        zs = " ".join("Z%d.%d" % (b, c) for b in (0, 1) for c in range(4))
-        s(zs + " LOFF KZ", "ZS", 512 * 1.5, lambda: act(D["ZS"], Z[:].indirect(D["LOFF"][:, 32:64]), F.Identity, bias=D["KZ"]))
-        v("X LOFF ZS", "ZX", 512 * 1.5, lambda: tt(D["ZX"], X[:, 0:W].indirect(D["LOFF"][:, 0:32]), D["ZS"], A.add))
-        v("ZX", "ZI", 256, lambda: ts(D["ZI"], D["ZX"], 0.5, -129.0, A.mult, A.add))
-        v("ZI LOFF", "X", 512 * 3.5, lambda: copy(X[:].indirect(D["LOFF"][:, 64:96]), D["ZI"]))
-
-    def phase2(t, b):
+    def hpart(t, b):
         x = str(b)
-        XH, AE = D["XH" + x], D["AE" + x]
-        gather(XH, 0, D["HOFF" + x], "X HOFF" + x, "XH" + x, CALLS2[b])
-        for c in range(4):
-            j = 512 * c
-            i = lane()
-            p("Z%s.%d NIB" % (x, c), "L%d" % i, 512, lambda j=j, i=i: [mm(L[i][:], D["NIB"], Z[:, 2048 * b + j:2048 * b + j + 512], True, False)], ["L%d" % i])
-            p("XH%s.%d IB" % (x, c), "L%d" % i, 512, lambda j=j, i=i: [mm(L[i][:], D["IB"], XH[:, j:j + 512], False, True)], ["L%d" % i])
-            s("L%d" % i, "AE%s.%d" % (x, c), 512, lambda j=j, i=i: act(AE[:, j:j + 512], L[i][:], F.Abs), ["L%d" % i])
-
-    def dpart(t, b):
-        x = str(b)
-        p(" ".join("AE%s.%d" % (x, c) for c in range(4)) + " B", "W%s.0" % x, 1024, lambda: [lanesum(WB[b], 0, m, D["AE" + x], D["B"][:, 0:128:16], True, True) for m in range(16)], ["W" + x])
+        wb, w_ = WB[b], "W" + x
+        p("ONES CKC CKc CA CB C" + x, w_ + ".3", 384, lambda: [const(wb[3], CKC), mm(wb[3], D["CA"], D["C" + x], False, False), mm(wb[3], D["CB"], D["C" + x], False, True)], [w_])
+        v("SQ%s %s.3" % (x, w_), "WI" + x, 128, lambda: tt(D["WI" + x], D["SQ" + x], wb[3], A.add), [w_])
+        v("WI" + x, "HI" + x, 128, lambda: ts(D["HI" + x], D["WI" + x], 5, 4095, A.arith_shift_right, A.bitwise_and))
+        v("HI" + x, "HF" + x, 128, lambda: ts(D["HF" + x], D["HI" + x], -2048.0, None, A.add))
+        p("HF%s IH" % x, w_ + ".0", 128, lambda: [mm(wb[0], D["HF" + x], D["IH"], True, True)], [w_])
+        v(w_ + ".0", "HOFF" + x, 128, lambda: ts(D["HOFF" + x], wb[0], 2048.0, None, A.add), [w_])
 
     def names1(t, b):
         x, y = str(b), "%d%d" % (t, b)
-        wb, w_, MO, MV = WB[b], "W" + x, D["MO" + x], D["MV" + x]
-        v("S%s NM%s NM%sa" % (x, x, x), "SN" + x, 256, lambda: tt(D["SN" + x], D["S" + x][:, :, 0:8], D["NM" + x], A.mult))
-        v("NS%s SN%s" % (x, x), "AX" + x, 128, lambda: sc(D["AX" + x], D["NS" + x], D["SN" + x], 0.0, A.mult, A.add))
-        v("AX%s C%s" % (x, x), "T0" + x, 256, lambda: tt(D["T0" + x], D["C" + x], D["AX" + x], A.mult))
-        v("T0%s A4" % x, "TI" + x, 128, lambda: ts(D["TI" + x], D["T0" + x], D["A4"], 1024.0, A.add, A.mult))
-        v("TI" + x, "TJ" + x, 128, lambda: ts(D["TJ" + x], D["TI" + x], 4095 << 12, None, A.bitwise_and))
-        v("TJ" + x, "P1" + x, 128, lambda: ts(PV[:, 1 + b], D["TJ" + x], 1.0, None, A.add), ["PV"])
-        v("CE" + x, "CX" + x, 64, lambda: ts(D["CX" + x], D["CE" + x][:, :, 4:8], 4.5, None, A.max))
-        p("CX%s MR%s IB" % (x, y), w_ + ".3", 320, lambda: [mm(wb[3][:, 0:64], D["IB"], D["CX" + x], True, False)] + [mm(wb[3][:, k:64:4], D["IB"], D["MR" + y], False, k == 3) for k in range(4)], [w_])
-        for q in range(1, 4):
-            v("CE" + x, "MO%s.%d" % (x, q), 64, lambda q=q: ts(MO[:, 128 * q:128 * q + 128], D["CE" + x], q + 1.0, None, A.is_equal))
-        for q in range(4):
-            v(w_ + ".3", "MV%s.%d" % (x, q), 64, lambda q=q: ts(MV[:, 64 * q:64 * q + 64], wb[3][:, 0:64], q + 5.0, None, A.is_equal), [w_])
+        wb, w_, SG, NF = WB[b], "W" + x, D["SG" + x], D["NF" + x]
+        p("NF%s H2K N22 SG%s" % (x, x), w_ + ".1", 256,
+          lambda: [mm(wb[1], NF, D["H2K"], True, False) if t == 0 else mm(wb[1], D["H2K"], NF, True, False), mm(wb[1], D["N22"], SG[:, 0:128], False, True)], [w_])
+        v("SG%s %s.1" % (x, w_), w_ + ".2", 128, lambda: sc(wb[2], SG[:, 0:128], wb[1], 0.0, A.mult, A.max), [w_])
+        v("C%s %s.2" % (x, w_), "TA" + x, 128, lambda: tt(D["TA" + x], D["C" + x], wb[2], A.mult), [w_])
+        v("TA%s A8" % x, "TI" + x, 128, lambda: ts(D["TI" + x], D["TA" + x], D["A8"], None, A.add))
+        v("TI" + x, "TJ" + x, 128, lambda: ts(D["TJ" + x], D["TI" + x], 13, 4095, A.arith_shift_right, A.bitwise_and))
+        v("TJ" + x, "N1" + x, 128, lambda: ts(D["N1" + x], D["TJ" + x], -2048.0, None, A.add))
+        ky = wb[3][:, 0:64]
+        p("KX%s MR%s IB" % (x, y), w_ + ".3", 320, lambda: [mm(ky, D["IB"], D["KX" + x][:, :, 4:8], True, False)] + [mm(ky[:, k:64:4], D["IB"], D["MR" + y], False, k == 3) for k in range(4)], [w_])
+        s(w_ + ".3", "KY" + x, 64, lambda: act(D["KY" + x], ky, F.Copy), [w_])
+        s(w_ + ".3", "KY2" + x, 64, lambda: act(D["KY2" + x], ky, F.Square), [w_])
+
+    def phase2(t, b):
+        x = str(b)
+        XH, AE, zo = D["XH" + x], D["AE" + x], 2048 * b
+        for q, a, e in GATHER2[b]:
+            r, zr, w = slice(512 * a, 512 * e), slice(zo + 512 * a, zo + 512 * e), X[:, 0:W].indirect(D["HOFF" + x][:, 32 * a:32 * e])
+            if q == "v":
+                v("X HOFF%s %s" % (x, pcs("Z" + x, a, e)), pcs("DD" + x, a, e), (e - a) * 512 * 1.56, lambda zr=zr, w=w: tt(DD[:, zr], w, Z[:, zr], A.subtract))
+                continue
+            s("X HOFF" + x, pcs("XH" + x, a, e), (e - a) * 512 * 1.56, lambda r=r, w=w: act(XH[:, r], w, F.Copy))
+            v(pcs("Z" + x, a, e) + " " + pcs("XH" + x, a, e), pcs("DD" + x, a, e), 256 * (e - a), lambda r=r, zr=zr: sc(DD[:, zr], XH[:, r], Z[:, zr], 64.0, A.min, A.subtract))
+        for a, e in ABS2[b]:
+            r, zr = slice(512 * a, 512 * e), slice(zo + 512 * a, zo + 512 * e)
+            s(pcs("DD" + x, a, e), pcs("AE" + x, a, e), 512 * (e - a), lambda r=r, zr=zr: act(AE[:, r], DD[:, zr], F.Abs, bias=-32.0))
+
+    def first2(t):
+        LI, LR = D["LI"], D["LR"]
+        p(" ".join("FV%d%d" % (b, q) for b in (0, 1) for q in range(4)) + " PR0 PR1 PR2 PR3", "UF0", 256, lambda: [mm(UB[2][:, 0:32], D["FVM"], D["PR32"], True, True)], ["UB"])
+        v("UF0", "LI", 64, lambda: copy(LI, UB[2][:, 0:32]), ["UB"])
+        v("LI", "LRa", 64, lambda: ts(LR[:, 0:32], LI, 13, None, A.arith_shift_right))
+        v("LI", "LRb", 64, lambda: ts(LR[:, 32:64], LI, 4096 + 7, None, A.bitwise_and))
+        v("LRa LRb BASE BASEa", "LQ", 128, lambda: tt(D["LQ"], LR, D["BASE"], A.add))
+        v("LQ", "LOFF", 64, lambda: copy(D["LOFF"], D["LQ"]))
+
+    def update(t):
+        pos, col = D["LOFF"][:, 0:32], D["LOFF"][:, 32:64]
+        s(pcs("DD0", 0, 4) + " " + pcs("DD1", 0, 4) + " LOFF", "ZS", 512 * 1.56, lambda: act(D["ZS"], DD[:].indirect(pos), F.Identity, bias=207.75, scale=0.5))
+        v(pcs("Z0", 0, 4) + " " + pcs("Z1", 0, 4) + " LOFF ZS", "ZX", 512 * 1.56, lambda: tt(D["ZX"], Z[:].indirect(pos), D["ZS"], A.add))
+        v("ZX M192 LOFF", "X", 512 * 3.8, lambda: tt(X[:].indirect(col), D["ZX"], D["M192"], A.add))
 
     def names2(t, b):
         x, y = str(b), "%d%d" % (t, b)
-        wb, w_, PRO, PRV = WB[b], "W" + x, D["PRO" + x], D["PRV" + x]
-        v(w_ + ".0 C" + x, "PV.0", 128, lambda: tt(PV[:, 0], D["C" + x], wb[0], A.mult), [w_, "PV"])
-        v("PV.0 HI" + x, "N2" + x, 128, lambda: tt(D["N2" + x], D["HI" + x], PV[:, 0], A.add), ["PV"])
-        v("N2" + x, "N3" + x, 128, lambda: ts(D["N3" + x], D["N2" + x], 4095, None, A.bitwise_and))
-        v("N3%s P1%s" % (x, x), "PV.3", 128, lambda: tt(PV[:, 3], D["N3" + x], PV[:, 1 + b], A.add), ["PV"])
+        d = D3[:, 2 + b]
+        p("ONES CKD", "D3.%d" % (2 + b), 128, lambda: [const(d, CKD)], ["D3"])
+        p(pcs("AE" + x, 0, 4) + " B", "D3.%d" % (2 + b), 1024, lambda: [mm(d[:, :, m], D["AE" + x][:, m:2048:16], D["B"][:, 0:128:16], False, m == 15) for m in range(16)], ["D3"])
+        v("D3.%d C%s" % (2 + b, x), "Q" + x, 128, lambda: tt(D["Q" + x], D["C" + x], d, A.mult), ["D3"])
+        for bank, tok, w, cols, key, lo, rs, out in ((TV, "TV", 64, slice(0, 512, 2), "KY", 4, "RS4", "OSV"), (TO, "TO", 128, CKT, "K", 0, "RS", "OSO")):
+            def terms(pairs, stop, bank=bank, w=w):
+                return [mm(bank[:, w * q:w * q + w], D[k] if k != "T" else D["T%d" % q], m, False, stop and q == 3) for k, m in pairs for q in range(4)]
+            p("ONES CKT CKT0 CKT1 CKT2 CKT3 T0 T1 T2 T3 TN %s%s %s2%s" % (key, x, key, x), tok, 12 * w,
+              lambda bank=bank, w=w, cols=cols, key=key, terms=terms: [const(bank[:, 0:4 * w], cols)] + terms([("T", D[key + x]), ("TN", D[key + "2" + x])], False), [tok])
+            p("I120 H8K IH C%s N1%s HF%s" % (x, x, x), tok, 12 * w,
+              lambda lo=lo, terms=terms: terms([("I120", D["C" + x][:, :, lo:8]), ("H8K", D["N1" + x][:, :, lo:8]), ("IH", D["HF" + x][:, :, lo:8])], False), [tok])
+            p("IH Q" + x, tok, 4 * w, lambda lo=lo, terms=terms: terms([("IH", D["Q" + x][:, :, lo:8])], True), [tok])
+            v("%s %s" % (tok, rs), out + x, 4 * w, lambda bank=bank, w=w, rs=rs, out=out: sc(D[out + x], D[rs], bank[:, 0:4 * w], 0.0, A.min, A.max), [tok])
         for q in range(4):
-            v("MV%s.%d PV.3" % (x, q), "PRV%s.%d" % (x, q), 64, lambda q=q: tt(PRV[:, 64 * q:64 * q + 64], D["MV" + x][:, 64 * q:64 * q + 64], PV[:, 3, :, 4:8], A.mult), ["PV"])
-        v(" ".join("PRV%s.%d" % (x, q) for q in range(4)) + " CRV", "OSV" + x, 256, lambda: sc(D["OSV" + x], D["CRV"], PRV, 0.0, A.mult, A.add))
-        for q in range(4):
-            if b:
-                s("OSV" + x, "SV%s.%d" % (y, q), 64, lambda q=q: act(D["SV" + y][:, :, q], D["OSV" + x][:, 64 * q + 3:64 * q + 64:4], F.Copy))
-                continue
-            gg("OSV" + x, "SV%s.%d" % (y, q), 0.21, lambda q=q: gcopy(D["SV" + y][:, :, q], D["OSV" + x][:, 64 * q + 3:64 * q + 64:4], 16))
-        sv = " ".join("SV%s.%d" % (y, q) for q in range(4))
-        for k in (0, 2):
-            for q in (k, k + 1):
-                v("MO%s.%d PV.3" % (x, q), "PRO%s.%d" % (x, q), 128, lambda q=q: tt(PRO[:, 128 * q:128 * q + 128], D["MO" + x][:, 128 * q:128 * q + 128], PV[:, 3], A.mult), ["PV"])
-            r = slice(128 * k, 128 * k + 256)
-            v("PRO%s.%d PRO%s.%d CRO" % (x, k, x, k + 1), "OSO%s.%d" % (x, k), 256, lambda r=r: sc(D["OSO" + x][:, r], D["CRO"][:, r], PRO[:, r], 0.0, A.mult, A.add))
-            for q in (k, k + 1):
-                s("KM OSO%s.%d" % (x, k), "SO%s.%d" % (y, q), 64, lambda q=q: act(D["SO" + y][:, :, q], D["OSO" + x][:, 128 * q + 7:128 * q + 128:8], F.Identity, bias=D["KM"]))
-        so = " ".join("SO%s.%d" % (y, q) for q in range(4))
+            gg("OSV" + x, "SV%s.%d" % (y, q), 0.2, lambda q=q: gcopy(D["SV" + y][:, :, q], D["OSV" + x][:, 64 * q + 3:64 * q + 64:4], 16))
+            s("OSO" + x, "SO%s.%d" % (y, q), 64, lambda q=q: act(D["SO" + y][:, :, q], D["OSO" + x][:, 128 * q + 7:128 * q + 128:8], F.Copy))
+        so, sv = pcs("SO" + y, 0, 4), pcs("SV" + y, 0, 4)
         if t < NV - 1:
             i = op("g", so + " " + sv, "", 0.8, lambda: [send_pairs(y)], sem="none")
-            op("r", "", "RO%s RV%s" % (y, y), 0.0, None, sem="rx" + y, inc=len(pair_engines(prv, core, 0)) + len(pair_engines(pr2, prv, 1)), after=[i], lat=3.5)
+            op("r", "", "RO%s RV%s" % (y, y), 0.0, None, sem="rx" + y, inc=len(pair_engines(prv, core, 0)) + len(pair_engines(pr2, prv, 1)), after=[i], lat=3.0)
         else:
             i = op("g", sv, "", 0.8, lambda: [send_last(y)], sem="none")
-            op("r", "", "RV" + y, 0.0, None, sem="rx" + y, inc=len(count_engines(prv, core)), after=[i], lat=3.5)
+            op("r", "", "RV" + y, 0.0, None, sem="rx" + y, inc=len(count_engines(prv, core)), after=[i], lat=3.0)
 
     def join(t, b):
         x, y, last = str(b), "%d%d" % (t, b), t == NV - 1
-        J, NM, DE = D["J" + x], D["NM" + x], D["DEAD" + x]
+        J, NM, LP, wb, w_ = D["J" + x], D["NM" + x], D["LP" + x], WB[b], "W" + x
         own, ov = D[("SO" if last else "RO") + y], D["RV" + y]
-        rd = "RV%s " % y + (" ".join("SO%s.%d" % (y, q) for q in range(4)) if last else "RO" + y)
+        rd = "RV%s " % y + (pcs("SO" + y, 0, 4) if last else "RO" + y)
         if last:
-            v(rd, "J" + x, 128, lambda: tt(J, own, ov, A.add))
+            v(rd, "J" + x, 128, lambda: tt(J, own, ov, A.max))
             jt = "J" + x
         else:
-            v(rd, "J%sa" % x, 112, lambda: tt(J[:, 2:16, :], own[:, 0:14, :], ov[:, 0:14, :], A.add))
-            v(rd, "J%sb" % x, 64, lambda: tt(J[:, 0:2, :], own[:, 14:16, :], ov[:, 14:16, :], A.add))
+            v(rd, "J%sa" % x, 112, lambda: tt(J[:, 2:16, :], own[:, 0:14, :], ov[:, 0:14, :], A.max))
+            v(rd, "J%sb" % x, 64, lambda: tt(J[:, 0:2, :], own[:, 14:16, :], ov[:, 14:16, :], A.max))
             jt = "J%sa J%sb" % (x, x)
-        jm, jn = J, jt
-        if last:
-            jm, jn = D["JM" + x], "JM" + x
-            v(jt, jn, 64, lambda: ts(jm, J, 0.0, None, A.max))
-        v(jn, "NM%sa" % x, 64, lambda: ts(NM[:, :, 0::2], jm, 12, None, A.arith_shift_right))
-        v(jn, "NM" + x, 64, lambda: ts(NM[:, :, 1::2], jm, 4095, None, A.bitwise_and))
-        v("NM%s NM%sa" % (x, x), "NF" + x, 128, lambda: copy(D["NF" + x], NM))
-        p("NF%s IDF" % x, "PTN", 512, lambda: [P.transpose(PT[:, 128:256], D["NF" + x], D["IDF"])], ["PT"])
+        v(jt, "NM%sa" % x, 64, lambda: ts(NM[:, :, 0::2], J, 13, 4095, A.arith_shift_right, A.bitwise_and))
+        v(jt, "NM" + x, 64, lambda: ts(NM[:, :, 1::2], J, 4095, None, A.bitwise_and))
+        v("NM%s NM%sa" % (x, x), "NF" + x, 128, lambda: ts(D["NF" + x], NM, -2048.0, None, A.add))
+        p("NF%s IH" % x, w_ + ".0", 128, lambda: [mm(wb[0], D["NF" + x], D["IH"], True, True)], [w_])
         if not last:
-            v("PTN", "OFF" + x, 128, lambda: copy(D["OFF" + x], PT[:, 128:256]), ["PT"])
-            v(jt, "DE%sa" % x, 64, lambda: ts(DE[:, :, 0::2], J, 0.0, None, A.is_lt))
-            v(jt, "DEAD" + x, 64, lambda: ts(DE[:, :, 1::2], J, 0.0, None, A.is_lt))
+            v(w_ + ".0", "OFF" + x, 128, lambda: ts(D["OFF" + x], wb[0], 2048.0, None, A.add), [w_])
         else:
-            s("PTN", "YL" + x, 128, lambda: act(D["YL" + x], PT[:, 128:256], F.Copy), ["PT"])
+            s(w_ + ".0", "YL" + x, 128, lambda: act(D["YL" + x], wb[0], F.Identity, bias=2048.0), [w_])
             ld("y", "yl" + x, T.yl[:, 128 * b:128 * b + 128], D["YL" + x], "YL" + x, "yl" + x, 2.5)
-            v(jt, "NA" + x, 64, lambda: ts(D["NA" + x], J, 0.0, 2.0, A.is_ge, A.mult))
-            v("NA" + x, "NC" + x, 64, lambda: tt(D["NC" + x], D["NA" + x][:, :, 0:2], D["NA" + x][:, :, 2:4], A.add))
-            v("NC" + x, "NN" + x, 64, lambda: tt(D["NN" + x], D["NC" + x][:, :, 0], D["NC" + x][:, :, 1], A.add))
-            p("NN%s IDF" % x, "LN" + x, 1024, lambda: [P.transpose(L[0][0:8, 256 * b + w1:256 * b + 256:2], D["NN" + x][:, w1::2], D["IDF"]) for w1 in (0, 1)], ["L0"])
+        v(jt, "LA" + x, 64, lambda: ts(LP[:, :, 1:5], J, 0.75 * EMPTY, -0.5, A.is_ge, A.add))
+        if last:
+            p("LA%s I2" % x, "L0", 1024, lambda: [mm(L[0][0:8, 256 * b + w1:256 * b + 256:2], LP[:, w1::2, 1 + j], D["I2"], j == 0, j == 3) for w1 in (0, 1) for j in range(4)], ["L0"])
+            s("L0", "YN" + x, 256, lambda: act(D["YN"][:, 256 * b:256 * b + 256], L[0][0:8, 256 * b:256 * b + 256], F.Identity, bias=4.0), ["L0"])
 
     def total(t):
-        p("ONES MX%d0 MX%d1" % (t, t), "PTA", 128, lambda: [mm(PT[:, 288:304], D["ONES"], D["MX%d0" % t], True, False), mm(PT[:, 288:304], D["ONES"], D["MX%d1" % t], False, True)], ["PT"])
-        v("PTA", "AR", 64, lambda: V.tensor_reduce(D["AR"], PT[:, 288:304], AxisListType.X, A.add), ["PT"])
-        v("AR", "AI", 64, lambda: copy(D["AI"], D["AR"]))
-        v("AI", "AI2", 64, lambda: ts(D["AI2"], D["AI"], 255, None, A.bitwise_and))
-        v("AI2", "A4", 64, lambda: ts(D["A4"], D["AI2"], 4.0, None, A.mult))
+        a = UB[3][:, 0:1]
+        p("ONEF AS0 AS1", "UF1", 512, lambda: [mm(a, D["ONEF"], D["AS0"], True, False), mm(a, D["ONEF"], D["AS1"], False, True)], ["UB"])
+        v("UF1", "AI", 64, lambda: copy(D["AI"], a), ["UB"])
+        v("AI", "AI2", 64, lambda: ts(D["AI2"], D["AI"], 510, None, A.bitwise_and))
+        v("AI2", "A8", 64, lambda: ts(D["A8"], D["AI2"], 4096.0, 2.0 ** 24, A.mult, A.add))
 
     def count_engines(a, c):
         return topo.engines(a, c)[0:8]
@@ -422,31 +408,27 @@ def rank_program(g, core, T, topo):
             part("runs", runs, t, b)
             part("upart", upart, t, b)
             part("hpart", hpart, t, b)
-        if t == 0:
-            late_constants()
-        for b in (0, 1):
-            part("phase2", phase2, t, b)
             part("first1", first1, t, b)
+        for b in (0, 1):
             part("names1", names1, t, b)
+            part("phase2", phase2, t, b)
         part("first2", first2, t)
         part("update", update, t)
         if t == NV - 1:
-            ld("y", "yx", T.yx[:], X[:, 0:W], "X", "yx", 7.0)
+            ld("y", "yx", T.yx[:], X[:, 0:W], "X", "yx", 6.0)
         for b in (0, 1):
-            part("dpart", dpart, t, b)
             part("names2", names2, t, b)
         if t < NV - 1:
-            total(t)
+            part("total", total, t)
         for b in (0, 1):
             part("join", join, t, b)
-    v("LN0 LN1", "YN", 512, lambda: copy(D["YN"], L[0][0:8, :]), ["L0"])
-    ld("y", "yn", T.yn[:], D["YN"], "YN", "yn", 2.5)
+    ld("y", "yn", T.yn[:], D["YN"], "YN0 YN1", "yn", 2.5)
     emit(g, T, ops)
     g.wait_ge(T.sem.ls, lsum[0])
 
 
-BOOST = {"runs1s": 258, "first2v": 246, "phase21p": -108, "names11v": -14, "phase10v": 32, "phase21s": -140, "upart1s": 138, "first11v": -82,
-         "first10v": -16, "runs0s": 196, "phase20p": -122, "first10p": -102, "phase11p": -84}
+BOOST = {'phase11p': -2.8, 'phase10p': -1.3, 'hpart0v': 4, 'hpart0p': 24, 'phase20v': 95, 'upart1p': -1, 'names10s': -3, 'phase11s': -1, 'names21s': -5.5, 'first10p': -1,
+         'upart0s': 6, 'join0v': -1.4, 'runs0s': 2, 'phase21v': 2, 'first2p': -2, 'updates': -3}
 
 
 def emit(g, T, ops):
@@ -489,44 +471,41 @@ def arrange(ops, deps, boost, hop):
     for i in range(N):
         for j in deps[i]:
             succ[j].append(i)
-    prio = [0.0] * N
+    way = [0.0] * N
     for i in range(N - 1, -1, -1):
-        o = ops[i]
-        prio[i] = o["cost"] + o["lat"] + max([prio[j] + hop for j in succ[i]] or [0.0])
-    prio = [prio[i] + boost.get(ops[i]["k"], 0.0) for i in range(N)]
-    left = [len(deps[i]) for i in range(N)]
-    ready = [0.0] * N
-    free, cand, order = {}, {}, []
-    for i in range(N):
-        if left[i] == 0:
-            cand.setdefault(ops[i]["q"], []).append(i)
-    while len(order) < N:
-        best = None
-        for q in sorted(cand):
-            if cand[q]:
-                st = max(free.get(q, 0.0), min(ready[i] for i in cand[q]))
-                if best is None or st < best[0]:
-                    best = (st, q)
-        st, q = best
-        i = max((i for i in cand[q] if ready[i] <= st + 1e-9), key=lambda i: (prio[i], -i))
-        cand[q].remove(i)
-        order.append(i)
-        end = st + ops[i]["cost"]
+        way[i] = ops[i]["cost"] + ops[i]["lat"] + max([way[j] + hop for j in succ[i]] or [0.0])
+    key = [way[i] + boost.get(ops[i]["k"], 0.0) for i in range(N)]
+    left = [len(d) for d in deps]
+    cand = [i for i in range(N) if left[i] == 0]
+    start, end, taken = [0.0] * N, [0.0] * N, {}
+    while cand:
+        i = max(cand, key=lambda i: (key[i], -i))
+        cand.remove(i)
+        q, c = ops[i]["q"], ops[i]["cost"]
+        st = max([end[j] + (hop if hard else 0.0) for j, hard in deps[i].items()] or [0.0])
         if q != "r":
-            free[q] = end
-        end += ops[i]["lat"]
+            iv = taken.setdefault("s" if q == "d" else q, [])
+            k = len(iv)
+            while k > 0 and iv[k - 1][0] >= st:
+                k -= 1
+            if k > 0:
+                st = max(st, iv[k - 1][1])
+            while k < len(iv) and st + c > iv[k][0] + 1e-9:
+                st = iv[k][1]
+                k += 1
+            iv.insert(k, (st, st + c))
+        start[i], end[i] = st, st + c + ops[i]["lat"]
         for j in succ[i]:
-            ready[j] = max(ready[j], end + (hop if deps[j][i] and q != "r" else 0.0))
             left[j] -= 1
             if left[j] == 0:
-                cand.setdefault(ops[j]["q"], []).append(j)
-    return order, max(free.values())
+                cand.append(j)
+    return sorted(range(N), key=lambda i: (start[i], i)), max(end)
 
 
 def issue(g, T, ops, deps, order):
     queues = {"v": g.vector, "s": g.scalar, "d": g.scalar, "p": g.tensor, "g": g, "y": g.sync}
     sems = {"v": "qv", "s": "qs", "p": "qp", "g": "qg"}
-    level, done, seen = {}, {}, {}
+    level, done, seen, last_some = {}, {}, {}, [False]
     for i in order:
         o = ops[i]
         q = o["q"]
@@ -540,6 +519,11 @@ def issue(g, T, ops, deps, order):
             if hard and done[j] is not None:
                 sm, c = done[j]
                 need[sm] = max(need.get(sm, 0), c)
+        if q == "g" and not o["sem"]:
+            some = o["w"][0].startswith("FV") and o["w"][0] != "FVM"
+            if some != last_some[0]:
+                need["qg"] = level.get("qg", 0)
+            last_some[0] = some
         for sm in sorted(need):
             if seen.get((qk, sm), 0) < need[sm]:
                 seen[(qk, sm)] = need[sm]

@@ -2,11 +2,14 @@ from concourse.bass import DstId, RemoteDMATransfer
 from concourse.mybir import dt, AluOpType, AxisListType, ActivationFunctionType
 
 NV, W = 3, 4096
-GATHER1 = [[("s", 0, 1), ("v", 1, 2), ("s", 2, 3), ("s", 3, 4)], [("s", 0, 2), ("s", 2, 4)]]
-GATHER2 = [[("s", 0, 2), ("v", 2, 3), ("s", 3, 4)], [("s", 0, 2), ("v", 2, 3), ("s", 3, 4)]]
-NEIGH = [[(0, 1), (1, 2), (2, 3), (3, 4)], [(0, 2), (2, 3), (3, 4)]]
-BYMAX = [2, 4]
-ABS2 = [[(0, 2), (2, 3), (3, 4)], [(0, 2), (2, 3), (3, 4)]]
+GATHER1 = [[(q, i, i + 1) for i, q in enumerate(x)] for x in ("svss", "ssss")]
+GATHER2 = [[(q, i, i + 1) for i, q in enumerate(x)] for x in ("ssvs", "svsv")]
+NEIGH = [[(0, 1), (1, 2), (2, 3), (3, 4)], [(0, 1), (1, 2), (2, 3), (3, 4)]]
+BYMAX = [(0, 2), (0, 2)]
+ABS2 = [[(0, 1), (1, 2), (2, 3), (3, 4)], [(0, 1), (1, 2), (2, 3), (3, 4)]]
+EARLY = [0, 0]
+COPY = ["ggggssss", "ggggssss"]
+KPQ = "ss"
 BFT, F32, I32, U16, F16 = "bfloat16", "float32", "int32", "uint16", "float16"
 BIG, BIG2, EMPTY = 2.0 ** 26, 2.0 ** 18, -2.0 ** 25
 SCRATCH = {}
@@ -20,12 +23,14 @@ def _sb(name, shape, ty):
     VIEWS[name] = (buf, k)
 
 
-SCRATCH["X"] = ("sbuf", [128, 8192], BFT)
+SCRATCH["X0"] = ("sbuf", [128, 8192], BFT)
+SCRATCH["X1"] = ("sbuf", [128, 8192], BFT)
 SCRATCH["Z"] = ("sbuf", [128, 4096], BFT)
 SCRATCH["DD"] = ("sbuf", [128, 4096], BFT)
-for _n in ("L0", "L1", "TO", "TV", "W0", "W1", "UB"):
+for _n in ("L0", "L1", "TO", "TV", "W0", "W1"):
     SCRATCH[_n] = ("psum", [128, 512], F32)
-SCRATCH["D3"] = ("psum", [128, 4, 8, 16], F32)
+for _n in ("Y0", "Y1"):
+    SCRATCH[_n] = ("psum", [128, 4, 8, 16], F32)
 SCALED = (("NB32", "B", -128.0), ("B16", "B", 64.0), ("P4", "IB", 16384.0), ("NH", "IB", -0.5), ("I2", "IB", 2.0), ("N22", "IB", -2.0 ** 22),
           ("CA", "IB", 9728.0), ("CB", "IB", 48.0), ("F2", "IB", 2 * BIG2), ("FN", "IB", -BIG2), ("T0", "IB", 2 * BIG), ("T1", "IB", 6 * BIG), ("T2", "IB", 10 * BIG),
           ("T3", "IB", 14 * BIG), ("TN", "IB", -BIG), ("I120", "IB", 120.0))
@@ -35,12 +40,12 @@ for _n, _s, _t in (
         ("ONES", [128, 128], BFT), ("B1", [128, 128], BFT), ("B", [128, 128], BFT), ("IB", [128, 128], BFT), ("CL", [128, 128], BFT),
         ("IH", [128, 128], F16), ("H2K", [128, 128], F16), ("H8K", [128, 128], F16), ("ONEF", [128, 128], F32), ("F4K", [128, 128], F32),
         ("CR", [128, 512], BFT), ("PR32", [128, 32], F32), ("E81", [8, 128], BFT), ("E8", [8, 128], BFT), ("TB", [8, 128], BFT), ("CK", [64, 1152], BFT),
-        ("WM", [128, 8], BFT), ("BW", [128, 128], BFT), ("NK0", [128, 128], BFT), ("C8", [128, 128], BFT), ("RSF", [128, 128], BFT), ("RS", [128, 512], BFT), ("RS4", [128, 256], BFT), ("M192", [128, 512], BFT),
+        ("WM", [128, 8], BFT), ("BW", [128, 128], BFT), ("NK0", [128, 128], BFT), ("C8", [128, 128], BFT), ("RSF", [128, 256], BFT), ("RS", [128, 512], BFT), ("RS4", [128, 256], BFT), ("M192", [128, 512], BFT),
         ("THB", [8, 1], BFT), ("THC", [8, 1], F32), ("PID", [128, 1], I32), ("PI2", [128, 1], I32), ("WT", [128, 4], I32), ("AI", [128, 1], I32), ("AI2", [128, 1], I32),
         ("BX", [128, 1], I32), ("BY", [128, 1], I32), ("NZ", [128, 1], F32), ("COEF", [128, 1], F32), ("WCOL", [128, 1], F32), ("A8", [128, 1], F32),
         ("BA", [128, 1], F32), ("BE", [128, 1], F32), ("TH", [8, 1], I32), ("WN", [8, 512], I32), ("WNB", [8, 512], BFT), ("WL", [128, 256], I32),
-        ("BW1", [128, 32], I32), ("BASE", [128, 64], I32), ("FVM", [128, 128], F32), ("LI", [128, 32], I32), ("LR", [128, 64], I32), ("LQ", [128, 64], I32),
-        ("LOFF", [128, 64], U16), ("ZS", [128, 512], BFT), ("ZX", [128, 512], BFT), ("YN", [8, 512], F32)):
+        ("BW1", [128, 32], I32), ("BASE", [128, 64], I32), ("FVM", [128, 256], F32), ("LI", [128, 32], I32), ("LR", [128, 64], I32), ("LQ", [128, 64], I32),
+        ("LOFF", [128, 64], U16), ("LH", [128, 32], U16), ("ZS", [128, 512], BFT), ("ZH", [128, 512], BFT), ("ZX", [128, 512], BFT), ("YN", [8, 512], F32)):
     _sb(_n, _s, _t)
 for _b in "01":
     for _n, _s, _t in (
@@ -49,7 +54,7 @@ for _b in "01":
             ("SG", [128, 144], BFT), ("CS", [128, 128], BFT), ("C", [128, 16, 8], BFT), ("K", [128, 128], BFT), ("K2", [128, 128], BFT), ("KX", [128, 16, 8], BFT),
             ("KY", [128, 64], BFT), ("KY2", [128, 64], BFT), ("AS", [128, 1], F32), ("TA", [128, 128], F32), ("TI", [128, 16, 8], I32), ("TJ", [128, 16, 8], I32), ("N1", [128, 16, 8], F16),
             ("KP", [128, 128], BFT), ("SQ", [128, 128], F32), ("U", [128, 128], F32), ("WI", [128, 16, 8], I32), ("HI", [128, 16, 8], I32), ("HF", [128, 16, 8], F16), ("Q", [128, 16, 8], F16),
-            ("FO", [128, 128], F32), ("OSO", [128, 512], F32), ("OSV", [128, 256], F32), ("J", [128, 16, 4], I32), ("YL", [128, 128], F32)):
+            ("FO", [128, 256], F32), ("OSO", [128, 512], F32), ("OSV", [128, 256], F32), ("J", [128, 16, 4], I32), ("YL", [128, 128], F32)):
         _sb(_n + _b, _s, _t)
     for _i in range(NV):
         for _n in ("SO", "SV", "RO", "RV"):
@@ -57,11 +62,11 @@ for _b in "01":
         for _n in ("MX", "MR"):
             _sb("%s%d%s" % (_n, _i, _b), [128, 16], BFT)
 
-DMAS = ["xv", "wl", "wn", "wt", "th", "yx", "yl0", "yl1", "yn"]
+DMAS = ["xv", "xc0", "xc1", "xc2", "wl", "wn", "wt", "th", "yx", "yl0", "yl1", "yn"]
 SEMAPHORES = ["qv", "qs", "qp", "qg", "ls"] + ["d_" + n for n in DMAS] + ["r%s%d%d" % (k, t, b) for k in "xm" for t in range(NV) for b in (0, 1)]
-CY = 0.00085
-PC = 0.00044
-HOP = 0.075
+CY = 0.00083
+PC = 0.00046
+HOP = 0.09
 
 
 def rank_program(g, core, T, topo):
@@ -73,21 +78,25 @@ def rank_program(g, core, T, topo):
     A, F = AluOpType, ActivationFunctionType
     V, S, P = g.vector, g.scalar, g.tensor
     D = {k: T[b][:, i] for k, (b, i) in VIEWS.items()}
-    X, Z, DD, D3, TO, TV, L = T.X, T.Z, T.DD, T.D3, T.TO, T.TV, [T.L0, T.L1]
+    XS, Z, DD, Y, TO, TV, L = [T.X0, T.X1], T.Z, T.DD, [T.Y0, T.Y1], T.TO, T.TV, [T.L0, T.L1]
     tiles = [slice(128 * k, 128 * k + 128) for k in range(4)]
-    UB, WB = [T.UB[:, k] for k in tiles], [[w[:, k] for k in tiles] for w in (T.W0, T.W1)]
+    WB = [[w[:, k] for k in tiles] for w in (T.W0, T.W1)]
     tt, mm, sc, act, mset, copy = V.tensor_tensor, P.matmul, V.tensor_tensor_scan, S.activation, V.memset, V.tensor_copy
-    ops, cur = [], [""]
+    ops, cur, visit, seen = [], [""], [0], {}
 
     def op(q, r, w, cost, fn, b=(), sem=None, inc=0, after=(), lat=0.0):
-        ops.append({"k": cur[0] + q if cur[0] else "", "q": q, "r": r.split(), "w": w.split(), "cost": cost, "fn": fn, "b": list(b), "sem": sem, "inc": inc, "after": list(after), "lat": lat})
+        k = (w.split() or ["send"])[0]
+        k = q + (k[:2] + k[3:] if k[:2] in ("MX", "MR", "SO", "SV", "RO", "RV") else "X" if cur[0] and k in ("X0", "X1") else k + "a" if k in ("J0", "J1") else k) + ("" if cur[0] else "!")
+        seen[(k, visit[0])] = seen.get((k, visit[0]), 0) + 1
+        k += "" if seen[(k, visit[0])] == 1 else "#%d" % seen[(k, visit[0])]
+        ops.append({"name": k, "t": visit[0], "k": cur[0] + q if cur[0] else "", "q": q, "r": r.split(), "w": w.split(), "cost": cost, "fn": fn, "b": list(b), "sem": sem, "inc": inc, "after": list(after), "lat": lat})
         return len(ops) - 1
 
     def v(r, w, cyc, fn, b=()):
-        return op("v", r, w, 0.05 + CY * max(cyc, 64), lambda: [fn()], b)
+        return op("v", r, w, 0.035 + CY * max(cyc, 64), lambda: [fn()], b)
 
     def s(r, w, cyc, fn, b=()):
-        return op("s", r, w, 0.065 + CY * max(cyc, 64), lambda: [fn()], b)
+        return op("s", r, w, 0.05 + CY * max(cyc, 64), lambda: [fn()], b)
 
     def p(r, w, cyc, fn, b):
         return op("p", r, w, PC * cyc, fn, b)
@@ -109,13 +118,14 @@ def rank_program(g, core, T, topo):
     def pcs(tok, a, e):
         return " ".join("%s.%d" % (tok, i) for i in range(a, e))
 
-    CKT, CKC, CKF, CKU, CKD, CKN = slice(0, 512), slice(512, 640), slice(640, 768), slice(768, 896), slice(896, 1024), slice(1024, 1152)
+    CKT, CKC, CKF, CKH, CKD, CKN = slice(0, 512), slice(512, 640), slice(640, 768), slice(768, 896), slice(896, 1024), slice(1024, 1152)
 
     def const(out, cols):
         return mm(out, D["ONES"][0:33, :], D["CK"][0:33, cols], True, False)
 
     ld("y", "wl", D["WL"], T.wl[:], "", "WL", 2.0)
-    ld("y", "xv", X[:, 0:W], T.xv[:], "", "X", 6.0)
+    ld("y", "xv", XS[0][:, 0:W], T.xv[:], "", "X0", 7.0)
+    ld("y", "xc0", XS[1][:, 0:W], T.xv[:], "X0", "X1", 7.0)
     ld("d", "th", D["TH"], T.th[:], "", "TH", 2.0)
     ld("d", "wt", D["WT"][:, 0:1], T.wt[:], "", "WT", 2.0)
     ld("d", "wn", D["WN"], T.wn[:], "", "WN", 2.0)
@@ -133,7 +143,7 @@ def rank_program(g, core, T, topo):
     gg("CK0", "CKN", 0.4, lambda: g.iota(CK[0:1, CKN], [[0, 16], [-1, 8]], 0, 0, allow_small_or_imprecise_dtypes=True))
     for q in range(4):
         v("CK0", "CKT%d" % q, 64, lambda q=q: mset(CK[0:1, 128 * q:128 * q + 128], -BIG * (2 * q + 1) ** 2))
-    for k, r, cols, c in (("CKT", 32, CKT, 2048.0), ("CKC", 0, CKC, 32768.0), ("CKc", 32, CKC, 208.0), ("CKf", 32, CKF, 129.0 * 4096), ("CKD", 0, CKD, -120.0)):
+    for k, r, cols, c in (("CKT", 32, CKT, 2048.0), ("CKC", 0, CKC, 32768.0), ("CKc", 32, CKC, 208.0), ("CKf", 32, CKF, 129.0 * 4096), ("CKH", 0, CKH, -BIG2), ("CKh", 32, CKH, 6144.0), ("CKD", 0, CKD, -120.0)):
         v("CK0", k, 256 if k == "CKT" else 64, lambda r=r, cols=cols, c=c: mset(CK[r:r + 1, cols], c))
     for b in (0, 1):
         x = str(b)
@@ -147,17 +157,17 @@ def rank_program(g, core, T, topo):
         s(src, k, 128, lambda k=k, src=src, c=c: act(D[k], D[src], F.Copy, scale=c))
     for k, src, c in (("IH", "IB", 1.0), ("H2K", "IB", 2048.0), ("H8K", "IB", 8192.0)):
         v(src, k, 64, lambda k=k, src=src, c=c: ts(D[k], D[src], c, None, A.mult))
-    for k, c, c0, st, w in (("CR", 4.0, -256.0, 8, 512), ("NK0", 1.0, 0.0, 8, 128), ("RSF", 2.0 ** 30, 4096.0, 8, 128), ("RS", 2.0 ** 30, EMPTY, 8, 512), ("RS4", 2.0 ** 30, EMPTY, 4, 256)):
+    for k, c, c0, st, w in (("CR", 4.0, -256.0, 8, 512), ("NK0", 1.0, 0.0, 8, 128), ("RSF", 2.0 ** 30, 4096.0, 8, 256), ("RS", 2.0 ** 30, EMPTY, 8, 512), ("RS4", 2.0 ** 30, EMPTY, 4, 256)):
         v("", k + "a", w // 2, lambda k=k, c=c: mset(D[k], c))
         v(k + "a", k, 64, lambda k=k, c0=c0, st=st: mset(D[k][:, 0::st], c0))
-    for k, c, w in (("C8", 0.125, 64), ("M192", -192.0, 256), ("ONEF", 1.0, 128), ("A8", 2.0 ** 24, 64), ("FVM", 0.0, 128)):
+    for k, c, w in (("C8", 0.125, 64), ("M192", -192.0, 256), ("ONEF", 1.0, 128), ("A8", 2.0 ** 24, 64), ("FVM", 0.0, 256)):
         v("", k, w, lambda k=k, c=c: mset(D[k], c))
     v("TH", "THB", 64, lambda: copy(D["THB"], D["TH"]))
     v("TH", "THC", 64, lambda: ts(D["THC"], D["TH"], 64.0, -8192.0, A.mult, A.add))
     v("PID", "PI2", 64, lambda: ts(D["PI2"], D["PID"], 15, None, A.bitwise_and))
     v("PI2", "NZ", 64, lambda: ts(D["NZ"], D["PI2"], 0.0, None, A.is_equal))
-    p("E8 THB", "UF0", 64, lambda: [mm(T.UB[:, 304:305], D["E8"], D["THB"], True, True)], ["UB"])
-    v("UF0 NZ", "COEF", 64, lambda: tt(D["COEF"], T.UB[:, 304:305], D["NZ"], A.add), ["UB"])
+    p("E8 THB", "TO", 64, lambda: [mm(TO[:, 0:1], D["E8"], D["THB"], True, True)], ["TO"])
+    v("TO NZ", "COEF", 64, lambda: tt(D["COEF"], TO[:, 0:1], D["NZ"], A.add), ["TO"])
     v("B COEF", "CL", 64, lambda: ts(D["CL"], D["B"], D["COEF"], None, A.mult))
     v("THC E8", "TBa", 64, lambda: ts(D["TB"], D["E8"], D["THC"], None, A.mult))
     v("TBa", "TB", 64, lambda: mset(D["TB"][:, 0::8], -16384.0))
@@ -174,26 +184,26 @@ def rank_program(g, core, T, topo):
     v("BW1 BE", "BASE", 64, lambda: ts(D["BASE"][:, 32:64], D["BW1"], D["BE"], None, A.add))
     v("WN", "WNB", 512, lambda: copy(D["WNB"], D["WN"]))
     for b in (0, 1):
-        p("WNB E8 ONES CKN", "D3.%d" % (2 + b), 256, lambda b=b: [const(D3[:, 2 + b], CKN)] + [
-            mm(D3[:, 2 + b, :, 8 * w1:8 * w1 + 8], D["WNB"][:, 256 * b + w1:256 * b + 256:2], D["E8"][:, 0:128:2], False, w1 == 1) for w1 in (0, 1)], ["D3"])
-        v("D3.%d" % (2 + b), "LA%d" % b, 128, lambda b=b: ts(D["LE%d" % b][:, :, 1:9], D3[:, 2 + b], 0.0, -0.5, A.is_gt, A.add), ["D3"])
+        p("WNB E8 ONES CKN", "Y%d.2" % b, 256, lambda b=b: [const(Y[b][:, 2], CKN)] + [
+            mm(Y[b][:, 2, :, 8 * w1:8 * w1 + 8], D["WNB"][:, 256 * b + w1:256 * b + 256:2], D["E8"][:, 0:128:2], False, w1 == 1) for w1 in (0, 1)], ["Y%d" % b])
+        v("Y%d.2" % b, "LA%d" % b, 128, lambda b=b: ts(D["LE%d" % b][:, :, 1:9], Y[b][:, 2], 0.0, -0.5, A.is_gt, A.add), ["Y%d" % b])
 
     def phase1(t, b):
-        x, nm = str(b), BYMAX[b]
-        Vb, M, y = D["V" + x], D["M" + x], D3[:, b]
+        x, (m0, m1) = str(b), BYMAX[b]
+        Vb, M, y = D["V" + x], D["M" + x], Y[b][:, 0]
         for q, a, e in GATHER1[b]:
-            o, w = Vb[:, 16 + 512 * a:16 + 512 * e], X[:, 0:W].indirect(D["OFF" + x][:, 32 * a:32 * e])
+            o, w = Vb[:, 16 + 512 * a:16 + 512 * e], XS[t % 2][:, 0:W].indirect(D["OFF" + x][:, 32 * a:32 * e])
             if q == "s":
-                s("X OFF" + x, pcs("V" + x, a, e), (e - a) * 512 * 1.56, lambda o=o, w=w: act(o, w, F.Identity, bias=-32.0))
+                s("X%d OFF%s" % (t % 2, x), pcs("V" + x, a, e), (e - a) * 512 * 1.56, lambda o=o, w=w: act(o, w, F.Identity, bias=-32.0))
             else:
-                v("X OFF" + x, pcs("V" + x, a, e), (e - a) * 512 * 1.56, lambda o=o, w=w: ts(o, w, -32.0, None, A.add))
+                v("X%d OFF%s" % (t % 2, x), pcs("V" + x, a, e), (e - a) * 512 * 1.56, lambda o=o, w=w: ts(o, w, -32.0, None, A.add))
 
         def before(c):
             return "V%sz" % x if c == 0 else "V%s.%d" % (x, c - 1)
         for a, e in NEIGH[b]:
             r, v0, v1 = slice(512 * a, 512 * e), Vb[:, 15 + 512 * a:15 + 512 * e], Vb[:, 16 + 512 * a:16 + 512 * e]
             rd = before(a) + " " + pcs("V" + x, a, e)
-            if a < nm:
+            if m0 <= a < m1:
                 v(rd, pcs("M" + x, a, e), 256 * (e - a), lambda r=r, v0=v0, v1=v1: sc(M[:, r], v0, v1, 0.0, A.min, A.max))
             else:
                 v(rd, pcs("XH" + x, a, e), 256 * (e - a), lambda r=r, v0=v0, v1=v1: sc(D["XH" + x][:, r], v1, v0, 0.0, A.min, A.subtract))
@@ -202,18 +212,19 @@ def rank_program(g, core, T, topo):
             j, i = 512 * c, c % 2
             k = "L%d" % i
             p("CL CR", k, 512, lambda i=i: [mm(L[i][:], D["CL"], D["CR"], True, False)], [k])
-            if c < nm:
+            if m0 <= c < m1:
                 p("V%s.%d %s B16" % (x, c, before(c)), k, 1024, lambda j=j, i=i: [mm(L[i][:], D["B16"], Vb[:, o + j:o + 512 + j], False, False) for o in (15, 16)], [k])
             p("M%s.%d NB32" % (x, c), k, 512, lambda j=j, i=i: [mm(L[i][:], D["NB32"], M[:, j:j + 512], False, True)], [k])
             v("%s V%s.%d" % (k, x, c), "Z%s.%d" % (x, c), 512, lambda j=j, i=i: sc(Z[:, 2048 * b + j:2048 * b + j + 512], L[i][:], Vb[:, 16 + j:528 + j], 0.0, A.min, A.max), [k])
-        LE, LP, ym, end = D["LE" + x], D["LP" + x], y[0:32 * nm] if nm else None, 16 + 512 * nm
-        p("ONES TB P4 LA%s B16 %s" % (x, pcs("V" + x, 0, nm)), "D3." + x, 256 + 16 * min(64, 32 * nm),
+        nm = m1 - m0
+        LE, LP, ym, beg, end = D["LE" + x], D["LP" + x], y[32 * m0:32 * m1] if nm else None, 16 + 512 * m0, 16 + 512 * m1
+        p("ONES TB P4 LA%s B16 %s" % (x, pcs("V" + x, m0, m1)), "D3." + x, 256 + 16 * min(64, 32 * nm),
           lambda: [mm(y, D["ONES"][0:8, :], D["TB"], True, False)]
           + ([mm(y, D["P4"], LE[:, :, 1:9], False, False)] if t == 0 else [mm(y[:, :, o::2], D["P4"], LP[:, :, 1:5], False, False) for o in (0, 1)])
-          + [mm(ym[:, :, m:m + 2], Vb[:, 16 + m:end:16], D["B16"][:, 0:128:8], False, False) for m in range(15 if nm else 0)]
-          + ([mm(ym[:, :, 15], Vb[:, 31:end:16], D["B16"][:, 0:128:16], False, False)] if nm else []), ["D3"])
-        p(pcs("M" + x, 0, 4) + " NB32", "D3." + x, 1024, lambda: [mm(y[:, :, m], M[:, m:2048:16], D["NB32"][:, 0:128:16], False, m == 15) for m in range(16)], ["D3"])
-        s("D3." + x, "SG" + x, 128, lambda: act(D["SG" + x][:, 0:128], y, F.Sign, bias=8.0), ["D3"])
+          + [mm(ym[:, :, m:m + 2], Vb[:, beg + m:end:16], D["B16"][:, 0:128:8], False, False) for m in range(15 if nm else 0)]
+          + ([mm(ym[:, :, 15], Vb[:, beg + 15:end:16], D["B16"][:, 0:128:16], False, False)] if nm else []), ["Y" + x])
+        p(pcs("M" + x, 0, 4) + " NB32", "D3." + x, 1024, lambda: [mm(y[:, :, m], M[:, m:2048:16], D["NB32"][:, 0:128:16], False, m == 15) for m in range(16)], ["Y" + x])
+        s("D3." + x, "SG" + x, 128, lambda: act(D["SG" + x][:, 0:128], y, F.Sign, bias=8.0), ["Y" + x])
 
     def runs(t, b):
         x, y = str(b), "%d%d" % (t, b)
@@ -228,29 +239,33 @@ def rank_program(g, core, T, topo):
         v(w_ + ".0 NK0", "K" + x, 128, lambda: sc(K, D["NK0"], wb[0], 0.0, A.mult, A.add), [w_])
         p("K%s LA%s IB" % (x, x), w_ + ".0", 128, lambda: [mm(wb[0][:, 0:16], D["IB"], K[:, 7::8], True, False), mm(wb[0][:, 0:16], D["IB"], LE[:, :, 8] if t == 0 else LP[:, :, 4], False, True)], [w_])
         s(w_ + ".0", "MX%s AS%s" % (y, x), 64, lambda: act(D["MX" + y], wb[0][:, 0:16], F.Identity, bias=0.5, accum_out=D["AS" + x]), [w_])
-        i = op("g", "MX" + y, "", 0.8, lambda: [send_counts(y)], sem="none")
+        i = op("g", "MX" + y, "", 0.7 if t + b else 2.7, lambda: [send_counts(y)], sem="none")
         op("r", "", "MR" + y, 0.0, None, sem="rm" + y, inc=len(count_engines(nxt, core)), after=[i], lat=3.0)
         s("K" + x, "K2" + x, 128, lambda: act(D["K2" + x], K, F.Square))
         s("K" + x, "KX" + x, 128, lambda: act(D["KX" + x], K, F.Relu, bias=-8.0))
 
     def upart(t, b):
         x = str(b)
-        u, zo = UB[b], 2048 * b
-        p("ONES BW", "UB" + x, 128, lambda: [mm(u, D["ONES"], D["BW"], True, False)], ["UB"])
-        p(pcs("Z" + x, 0, 4) + " WM", "UB" + x, 1024, lambda: [mm(u[:, m:128:16], Z[:, zo + m:zo + 2048:16], D["WM"], False, m == 15) for m in range(16)], ["UB"])
-        s("UB" + x, "KP" + x, 128, lambda: act(D["KP" + x], u, F.Identity, bias=128.5 + 1.0 / 8192), ["UB"])
-        v("KP%s UB%s" % (x, x), "U" + x, 128, lambda: tt(D["U" + x], u, D["KP" + x], A.subtract), ["UB"])
+        u, zo, bk = Y[b][:, 1], 2048 * b, ["Y" + x]
+        p("ONES BW", "UB" + x, 128, lambda: [mm(u, D["ONES"], D["BW"], True, False)], bk)
+        p(pcs("Z" + x, 0, 4) + " WM", "UB" + x, 1024, lambda: [mm(u[:, :, m], Z[:, zo + m:zo + 2048:16], D["WM"], False, m == 15) for m in range(16)], bk)
+        if KPQ[b] == "s":
+            s("UB" + x, "KP" + x, 128, lambda: act(D["KP" + x], u, F.Identity, bias=128.5 + 1.0 / 8192), bk)
+        else:
+            v("UB" + x, "KP" + x, 128, lambda: ts(D["KP" + x], u, 128.5 + 1.0 / 8192, None, A.add), bk)
+        v("KP%s UB%s" % (x, x), "U" + x, 128, lambda: tt(D["U" + x], u, D["KP" + x], A.subtract), bk)
         s("U" + x, "SQ" + x, 128, lambda: act(D["SQ" + x], D["U" + x], F.Square, bias=592.0 + 129 * 4096, scale=4096.0))
 
     def first1(t, b):
         x = str(b)
-        fs, w_ = WB[b][3], "W" + x
-        p("ONES CKF CKf F2 FN F4K U%s K%s K2%s" % (x, x, x), w_ + ".3", 896,
-          lambda: [const(fs, CKF), mm(fs, D["F4K"], D["U" + x], False, False), mm(fs, D["F2"], D["K" + x], False, False), mm(fs, D["FN"], D["K2" + x], False, True)], [w_])
-        v("RSF %s.3" % w_, "FO" + x, 128, lambda: sc(D["FO" + x], D["RSF"], fs, 4096.0, A.min, A.max), [w_])
+        fs, both, w_ = WB[b][2:4], (T.W0, T.W1)[b][:, 256:512], "W" + x
+        p("ONES CKF CKf CKH CKh F2 FN F4K IH U%s HF%s K%s K2%s" % (x, x, x, x), "%s.2 %s.3" % (w_, w_), 1408,
+          lambda: [const(both, slice(CKF.start, CKH.stop)), mm(fs[0], D["F4K"], D["U" + x], False, False), mm(fs[1], D["IH"], D["HF" + x], False, False)]
+          + [mm(fs[i], D[k], D[m + x], False, i == 1 and k == "FN") for k, m in (("F2", "K"), ("FN", "K2")) for i in (0, 1)], [w_])
+        v("RSF %s.2 %s.3" % (w_, w_), "FO" + x, 256, lambda: sc(D["FO" + x], D["RSF"], both, 4096.0, A.min, A.max), [w_])
         for q in range(4):
             r = slice(32 * q, 32 * q + 32)
-            gg("FVM FO" + x, "FV%s%d" % (x, q), 0.2, lambda r=r, q=q: gcopy(D["FVM"][r, 4 * b + q::8], D["FO" + x][r, 7::8], 16))
+            gg("FVM FO" + x, "FV%s%d" % (x, q), 0.23, lambda r=r, q=q: gcopy(D["FVM"][r, 4 * b + q::8], D["FO" + x][r, 7::8], 32))
 
     def hpart(t, b):
         x = str(b)
@@ -272,6 +287,10 @@ def rank_program(g, core, T, topo):
         v("TA%s A8" % x, "TI" + x, 128, lambda: ts(D["TI" + x], D["TA" + x], D["A8"], None, A.add))
         v("TI" + x, "TJ" + x, 128, lambda: ts(D["TJ" + x], D["TI" + x], 13, 4095, A.arith_shift_right, A.bitwise_and))
         v("TJ" + x, "N1" + x, 128, lambda: ts(D["N1" + x], D["TJ" + x], -2048.0, None, A.add))
+
+    def keys(t, b):
+        x, y = str(b), "%d%d" % (t, b)
+        wb, w_ = WB[b], "W" + x
         ky = wb[3][:, 0:64]
         p("KX%s MR%s IB" % (x, y), w_ + ".3", 320, lambda: [mm(ky, D["IB"], D["KX" + x][:, :, 4:8], True, False)] + [mm(ky[:, k:64:4], D["IB"], D["MR" + y], False, k == 3) for k in range(4)], [w_])
         s(w_ + ".3", "KY" + x, 64, lambda: act(D["KY" + x], ky, F.Copy), [w_])
@@ -281,11 +300,11 @@ def rank_program(g, core, T, topo):
         x = str(b)
         XH, AE, zo = D["XH" + x], D["AE" + x], 2048 * b
         for q, a, e in GATHER2[b]:
-            r, zr, w = slice(512 * a, 512 * e), slice(zo + 512 * a, zo + 512 * e), X[:, 0:W].indirect(D["HOFF" + x][:, 32 * a:32 * e])
+            r, zr, w = slice(512 * a, 512 * e), slice(zo + 512 * a, zo + 512 * e), XS[t % 2][:, 0:W].indirect(D["HOFF" + x][:, 32 * a:32 * e])
             if q == "v":
-                v("X HOFF%s %s" % (x, pcs("Z" + x, a, e)), pcs("DD" + x, a, e), (e - a) * 512 * 1.56, lambda zr=zr, w=w: tt(DD[:, zr], w, Z[:, zr], A.subtract))
+                v("X%d HOFF%s %s" % (t % 2, x, pcs("Z" + x, a, e)), pcs("DD" + x, a, e), (e - a) * 512 * 1.56, lambda zr=zr, w=w: tt(DD[:, zr], w, Z[:, zr], A.subtract))
                 continue
-            s("X HOFF" + x, pcs("XH" + x, a, e), (e - a) * 512 * 1.56, lambda r=r, w=w: act(XH[:, r], w, F.Copy))
+            s("X%d HOFF%s" % (t % 2, x), pcs("XH" + x, a, e), (e - a) * 512 * 1.56, lambda r=r, w=w: act(XH[:, r], w, F.Copy))
             v(pcs("Z" + x, a, e) + " " + pcs("XH" + x, a, e), pcs("DD" + x, a, e), 256 * (e - a), lambda r=r, zr=zr: sc(DD[:, zr], XH[:, r], Z[:, zr], 64.0, A.min, A.subtract))
         for a, e in ABS2[b]:
             r, zr = slice(512 * a, 512 * e), slice(zo + 512 * a, zo + 512 * e)
@@ -293,25 +312,28 @@ def rank_program(g, core, T, topo):
 
     def first2(t):
         LI, LR = D["LI"], D["LR"]
-        p(" ".join("FV%d%d" % (b, q) for b in (0, 1) for q in range(4)) + " PR0 PR1 PR2 PR3", "UF0", 256, lambda: [mm(UB[2][:, 0:32], D["FVM"], D["PR32"], True, True)], ["UB"])
-        v("UF0", "LI", 64, lambda: copy(LI, UB[2][:, 0:32]), ["UB"])
+        p(" ".join("FV%d%d" % (b, q) for b in (0, 1) for q in range(4)) + " PR0 PR1 PR2 PR3", "UF0", 512,
+          lambda: [mm(Y[1][:, 3, 2 * i:2 * i + 2], D["FVM"][:, 128 * i:128 * i + 128], D["PR32"], True, True) for i in (0, 1)], ["Y1"])
+        v("UF0", "LH", 64, lambda: ts(D["LH"], Y[1][:, 3, 2:4], -4096.0, None, A.add), ["Y1"])
+        v("UF0", "LI", 64, lambda: copy(LI, Y[1][:, 3, 0:2]), ["Y1"])
         v("LI", "LRa", 64, lambda: ts(LR[:, 0:32], LI, 13, None, A.arith_shift_right))
         v("LI", "LRb", 64, lambda: ts(LR[:, 32:64], LI, 4096 + 7, None, A.bitwise_and))
         v("LRa LRb BASE BASEa", "LQ", 128, lambda: tt(D["LQ"], LR, D["BASE"], A.add))
         v("LQ", "LOFF", 64, lambda: copy(D["LOFF"], D["LQ"]))
 
     def update(t):
-        pos, col = D["LOFF"][:, 0:32], D["LOFF"][:, 32:64]
-        s(pcs("DD0", 0, 4) + " " + pcs("DD1", 0, 4) + " LOFF", "ZS", 512 * 1.56, lambda: act(D["ZS"], DD[:].indirect(pos), F.Identity, bias=207.75, scale=0.5))
+        pos, col, old, new = D["LOFF"][:, 0:32], D["LOFF"][:, 32:64], t % 2, 1 - t % 2
+        s("X%d LH" % old, "ZS", 512 * 1.56, lambda: act(D["ZS"], XS[old][:, 0:W].indirect(D["LH"]), F.Copy))
         v(pcs("Z0", 0, 4) + " " + pcs("Z1", 0, 4) + " LOFF ZS", "ZX", 512 * 1.56, lambda: tt(D["ZX"], Z[:].indirect(pos), D["ZS"], A.add))
-        v("ZX M192 LOFF", "X", 512 * 3.8, lambda: tt(X[:].indirect(col), D["ZX"], D["M192"], A.add))
+        s("ZX", "ZH", 512, lambda: act(D["ZH"], D["ZX"], F.Identity, bias=207.75, scale=0.5))
+        v("ZH M192 LOFF", "X%d" % new, 512 * 3.8, lambda: tt(XS[new][:].indirect(col), D["ZH"], D["M192"], A.add))
 
     def names2(t, b):
         x, y = str(b), "%d%d" % (t, b)
-        d = D3[:, 2 + b]
-        p("ONES CKD", "D3.%d" % (2 + b), 128, lambda: [const(d, CKD)], ["D3"])
-        p(pcs("AE" + x, 0, 4) + " B", "D3.%d" % (2 + b), 1024, lambda: [mm(d[:, :, m], D["AE" + x][:, m:2048:16], D["B"][:, 0:128:16], False, m == 15) for m in range(16)], ["D3"])
-        v("D3.%d C%s" % (2 + b, x), "Q" + x, 128, lambda: tt(D["Q" + x], D["C" + x], d, A.mult), ["D3"])
+        d, bk = Y[b][:, 2], ["Y" + x]
+        p("ONES CKD", "Y%s.2" % x, 128, lambda: [const(d, CKD)], bk)
+        p(pcs("AE" + x, 0, 4) + " B", "Y%s.2" % x, 1024, lambda: [mm(d[:, :, m], D["AE" + x][:, m:2048:16], D["B"][:, 0:128:16], False, m == 15) for m in range(16)], bk)
+        v("Y%s.2 C%s" % (x, x), "Q" + x, 128, lambda: tt(D["Q" + x], D["C" + x], d, A.mult), bk)
         for bank, tok, w, cols, key, lo, rs, out in ((TV, "TV", 64, slice(0, 512, 2), "KY", 4, "RS4", "OSV"), (TO, "TO", 128, CKT, "K", 0, "RS", "OSO")):
             def terms(pairs, stop, bank=bank, w=w):
                 return [mm(bank[:, w * q:w * q + w], D[k] if k != "T" else D["T%d" % q], m, False, stop and q == 3) for k, m in pairs for q in range(4)]
@@ -322,15 +344,21 @@ def rank_program(g, core, T, topo):
             p("IH Q" + x, tok, 4 * w, lambda lo=lo, terms=terms: terms([("IH", D["Q" + x][:, :, lo:8])], True), [tok])
             v("%s %s" % (tok, rs), out + x, 4 * w, lambda bank=bank, w=w, rs=rs, out=out: sc(D[out + x], D[rs], bank[:, 0:4 * w], 0.0, A.min, A.max), [tok])
         for q in range(4):
-            gg("OSV" + x, "SV%s.%d" % (y, q), 0.2, lambda q=q: gcopy(D["SV" + y][:, :, q], D["OSV" + x][:, 64 * q + 3:64 * q + 64:4], 16))
-            s("OSO" + x, "SO%s.%d" % (y, q), 64, lambda q=q: act(D["SO" + y][:, :, q], D["OSO" + x][:, 128 * q + 7:128 * q + 128:8], F.Copy))
+            for k, src, w, e in (("SV", "OSV", 4, COPY[b][q]), ("SO", "OSO", 8, COPY[b][4 + q])):
+                o, i, tok = D[k + y][:, :, q], D[src + x][:, 16 * w * q + w - 1:16 * w * (q + 1):w], "%s%s.%d" % (k, y, q)
+                if e == "g":
+                    gg(src + x, tok, 0.2, lambda o=o, i=i: gcopy(o, i, 16))
+                elif e == "s":
+                    s(src + x, tok, 64, lambda o=o, i=i: act(o, i, F.Copy))
+                else:
+                    v(src + x, tok, 64, lambda o=o, i=i: copy(o, i))
         so, sv = pcs("SO" + y, 0, 4), pcs("SV" + y, 0, 4)
         if t < NV - 1:
             i = op("g", so + " " + sv, "", 0.8, lambda: [send_pairs(y)], sem="none")
-            op("r", "", "RO%s RV%s" % (y, y), 0.0, None, sem="rx" + y, inc=len(pair_engines(prv, core, 0)) + len(pair_engines(pr2, prv, 1)), after=[i], lat=3.0)
+            op("r", "", "RO%s RV%s" % (y, y), 0.0, None, sem="rx" + y, inc=len(pair_engines(prv, core, 0)) + len(pair_engines(pr2, prv, 1)), after=[i], lat=3.5)
         else:
             i = op("g", sv, "", 0.8, lambda: [send_last(y)], sem="none")
-            op("r", "", "RV" + y, 0.0, None, sem="rx" + y, inc=len(count_engines(prv, core)), after=[i], lat=3.0)
+            op("r", "", "RV" + y, 0.0, None, sem="rx" + y, inc=len(count_engines(prv, core)), after=[i], lat=3.5)
 
     def join(t, b):
         x, y, last = str(b), "%d%d" % (t, b), t == NV - 1
@@ -359,9 +387,9 @@ def rank_program(g, core, T, topo):
             s("L0", "YN" + x, 256, lambda: act(D["YN"][:, 256 * b:256 * b + 256], L[0][0:8, 256 * b:256 * b + 256], F.Identity, bias=4.0), ["L0"])
 
     def total(t):
-        a = UB[3][:, 0:1]
-        p("ONEF AS0 AS1", "UF1", 512, lambda: [mm(a, D["ONEF"], D["AS0"], True, False), mm(a, D["ONEF"], D["AS1"], False, True)], ["UB"])
-        v("UF1", "AI", 64, lambda: copy(D["AI"], a), ["UB"])
+        a = Y[1][:, 3, 4, 0:1]
+        p("ONEF AS0 AS1", "UF1", 512, lambda: [mm(a, D["ONEF"], D["AS0"], True, False), mm(a, D["ONEF"], D["AS1"], False, True)], ["Y1"])
+        v("UF1", "AI", 64, lambda: copy(D["AI"], a), ["Y1"])
         v("AI", "AI2", 64, lambda: ts(D["AI2"], D["AI"], 510, None, A.bitwise_and))
         v("AI2", "A8", 64, lambda: ts(D["A8"], D["AI2"], 4096.0, 2.0 ** 24, A.mult, A.add))
 
@@ -403,25 +431,32 @@ def rank_program(g, core, T, topo):
         cur[0] = ""
 
     for t in range(NV):
+        visit[0] = t
         for b in (0, 1):
             part("phase1", phase1, t, b)
             part("runs", runs, t, b)
+            if EARLY[b]:
+                part("names1", names1, t, b)
             part("upart", upart, t, b)
             part("hpart", hpart, t, b)
             part("first1", first1, t, b)
         for b in (0, 1):
-            part("names1", names1, t, b)
+            if not EARLY[b]:
+                part("names1", names1, t, b)
+            part("keys", keys, t, b)
             part("phase2", phase2, t, b)
         part("first2", first2, t)
         part("update", update, t)
         if t == NV - 1:
-            ld("y", "yx", T.yx[:], X[:, 0:W], "X", "yx", 6.0)
+            ld("y", "yx", T.yx[:], XS[NV % 2][:, 0:W], "X%d" % (NV % 2), "yx", 7.0)
         for b in (0, 1):
             part("names2", names2, t, b)
         if t < NV - 1:
             part("total", total, t)
         for b in (0, 1):
             part("join", join, t, b)
+        if t < NV - 1:
+            part("copy", lambda t: ld("y", "xc%d" % (t + 1), XS[t % 2][:, 0:W], XS[1 - t % 2][:, 0:W], "X%d RO%d1" % (1 - t % 2, t), "X%d" % (t % 2), 7.0), t)
     ld("y", "yn", T.yn[:], D["YN"], "YN0 YN1", "yn", 2.5)
     emit(g, T, ops)
     g.wait_ge(T.sem.ls, lsum[0])
@@ -429,6 +464,11 @@ def rank_program(g, core, T, topo):
 
 BOOST = {'phase11p': -2.8, 'phase10p': -1.3, 'hpart0v': 4, 'hpart0p': 24, 'phase20v': 95, 'upart1p': -1, 'names10s': -3, 'phase11s': -1, 'names21s': -5.5, 'first10p': -1,
          'upart0s': 6, 'join0v': -1.4, 'runs0s': 2, 'phase21v': 2, 'first2p': -2, 'updates': -3}
+
+
+ORDER = """
+pL0#7 pL0#12+ sSQ1 vRS4! yyn!+ vCKC!- vBA! gFV12 vXH0.2 sV1.0 vM0.0 sN22! vZ0.3 pL0#2 vONEF! vXH0.3 pL1#3 pL1#2 sKP0 pD3.0 vZ0.0 vNF1+ vBASEa! vZ0.1 pUF1+ pL0#4 pL0#8 sYN1+ pD3.0#2 vA8! yX1! pL1#4 vCKh! pTO#2 vSGz1! sV1.1 sV1.2 vCS0 sMX0 pTO#5 pUB0 pL0#11+ vNM1+ sSO1.2+ vOFF1+ pL0#5 vJ1b+ vDD0.0 pL1#5 sT1! vK0 pL1#6 vXH1.2 sSO1.3+ pY1.2#2 vJ1a+ sC0 pW0.0 vM1.0 vNM1a+ vU0 vZ1.1 pUB0#2 vHF0 gSV0.3 yX+ yyl1+ pTV#4 pW0.0#2 sSO0.2 pL1#7 sV1.3 vZ1.0 sM1.3 sAE0.1 vM1.1 pL1#8 pW0.3#2 pW0.3 pW0.1 pD3.1 pW0.2 vWI0 pL0#6 vHI0 vBASE! pL0#9 sKX0 vZ1.3 sM1.2 vTI1 vHOFF0 sM0.2- vCKT2! gFV00 vDD0.2 pL1#9 pW0.0#3 vXH1.3 pL0#10 pL1#10 pD3.1#2 sK20 sXH0.1 sKP1 vHF1 sXH0.0 gFV01 pW1.0 pUB1 sSG1 vBX!- sYL0+ sMX1 vCS1 pUB1#2 pY0.2#2 pW1.3 vU1 gSV0.1 pTO#4 vFO0 sKY0 vK1 pL1- pW1.0#2 gFV02 vDD0.3 gSV0.0 sXH0.3 vDD0.1 vZX vTA0 vX rMR0 sKY20 sC1 vWI1 pW1.1 pY1.2 sAE0.0 gPID!- pTO pTV gFV13 vM192!- vW0.2 pW1.2 rMR1 vHOFF1 pW1.0#3 gFV10 pTO#6 gFV03 gBW1!- vOSV1 vHI1 sK21 yyl0+ pY0.2 sAE0.2 gE8!- vQ0 vTI0 vOSV0 vTHB!- pUF0 vTJ0 vWNB!- sAE0.3 sYL1+ gFV11 gsend vNK0!- vSGz0!- vOSO0 dTH!- vDD1.1 vDD1.3 pTV#6 vTBa!- pTV#5 vCKH!- sSO0.3 sXH1.0 vCR!- gsend#3 sXH1.2 gE81!- sAE1.1 sI120!- vTHC!- sKX1 gSV0.2 sSO0.0 vV0z!- vCKc!- vPR2!- vN10 vONES!- vC8!- vDD1.0 vN11 dWN!- gB!- pTV#2 sV0.0- gB1!- sSO0.1 sSQ0- vOSO1 vV1z!- vCRa!- vCKT0!- sAE1.3 vDD1.2 sAE1.0 vLH dWT!- sNH!- pTV#3 vCKf!- pTO!- pW1.3#2 pTO#3 sI2!- vLEz1!- vOFF1!- vAI pY0.2!- vWM!- vLI sAE1.2 sF4K!- vW1.2 vLA0!- rRO0 rRV0 vLRa vFO1 vLPz1!- vNZ!- rRO1 vTA1 vCOEF!- sF2!- sZS vLRb vOFF0!- vH8K!- vIH!- sKY1 vLQ sV0.2- sT2!- vCKT1!- sFN!- vQ1 gIB!- sT0!- sSG0- pW0.0#4 pW1.0#4 pY1.2!- pL0- vCKT!- yX0!- sM0.3- sV0.3- sTN!- vAI2 vRS!- vZ1.2- vRSFa!- vA8 vTJ1 vCKD!- vTB!- vCK0!- sCA!- gCKF!- sP4!- sB16!- sT3!- vCKT3!- sKY21 vBW!- vLOFF sCB!- sZH gSV1.2 vNM0 vRS4a!- vLA1!- vPR0!- gCKN!- gSV1.3 vNF0!- vCL!- vNK0a!- vNF1!- vRSa!- vZ0.2- gSV1.0 vFVM!- vNF0 vRSF!- vPR3!- vPI2!- vLPz0!- gsend#4 yWL!- yyx! vH2K!- vM0.1- gsend#2- gSV1.1 rRV1 vLA1 vWCOL!- vLEz0!- sYN0 vBY!- vJ0a vNM0a vJ0b vV0.1- pL0#3- sNB32!- vBE!- vOFF0 sSO1.0 vLA0 sSO1.1 vPR1!-
+"""
 
 
 def emit(g, T, ops):
@@ -475,6 +515,10 @@ def arrange(ops, deps, boost, hop):
     for i in range(N - 1, -1, -1):
         way[i] = ops[i]["cost"] + ops[i]["lat"] + max([way[j] + hop for j in succ[i]] or [0.0])
     key = [way[i] + boost.get(ops[i]["k"], 0.0) for i in range(N)]
+    if ORDER:
+        names = ORDER.split()
+        at = {x.rstrip("+-"): i + len(names) * (x.count("+") - x.count("-")) for i, x in enumerate(names)}
+        key = [-at[o["name"]] - len(names) * o["t"] for o in ops]
     left = [len(d) for d in deps]
     cand = [i for i in range(N) if left[i] == 0]
     start, end, taken = [0.0] * N, [0.0] * N, {}

from concourse.bass import DstId, RemoteDMATransfer
from concourse.mybir import dt, AluOpType, AxisListType, ActivationFunctionType

NV, W = 3, 4096
GATHER1 = [[(q, i, i + 1) for i, q in enumerate(x)] for x in ("svss", "ssss")]
GATHER2 = [[(q, i, i + 1) for i, q in enumerate(x)] for x in ("ssvs", "svsv")]
NEIGH = [[(0, 1), (1, 2), (2, 3), (3, 4)], [(0, 1), (1, 2), (2, 3), (3, 4)]]
BYMAX = [(0, 2), (0, 2)]
ABS2 = [[(0, 1), (1, 2), (2, 3), (3, 4)], [(0, 1), (1, 2), (2, 3), (3, 4)]]
EARLY = [0, 0]
COPY = ["ggggssss", "ggggssss"]
KPQ = "ss"
BFT, F32, I32, U16, F16 = "bfloat16", "float32", "int32", "uint16", "float16"
BIG, BIG2, EMPTY = 2.0 ** 26, 2.0 ** 18, -2.0 ** 25
SCRATCH = {}
VIEWS = {}


def _sb(name, shape, ty):
    buf = "b_" + "_".join(str(n) for n in shape) + "_" + ty
    k = SCRATCH[buf][1][1] if buf in SCRATCH else 0
    SCRATCH[buf] = ("sbuf", [shape[0], k + 1] + shape[1:], ty)
    VIEWS[name] = (buf, k)


SCRATCH["X0"] = ("sbuf", [128, 8192], BFT)
SCRATCH["X1"] = ("sbuf", [128, 8192], BFT)
SCRATCH["Z"] = ("sbuf", [128, 4096], BFT)
SCRATCH["DD"] = ("sbuf", [128, 4096], BFT)
for _n in ("L0", "L1", "TO", "TV", "W0", "W1"):
    SCRATCH[_n] = ("psum", [128, 512], F32)
for _n in ("Y0", "Y1"):
    SCRATCH[_n] = ("psum", [128, 4, 8, 16], F32)
SCALED = (("NB32", "B", -128.0), ("B16", "B", 64.0), ("P4", "IB", 16384.0), ("NH", "IB", -0.5), ("I2", "IB", 2.0), ("N22", "IB", -2.0 ** 22),
          ("CA", "IB", 9728.0), ("CB", "IB", 48.0), ("F2", "IB", 2 * BIG2), ("FN", "IB", -BIG2), ("T0", "IB", 2 * BIG), ("T1", "IB", 6 * BIG), ("T2", "IB", 10 * BIG),
          ("T3", "IB", 14 * BIG), ("TN", "IB", -BIG), ("I120", "IB", 120.0))
for _n, _a, _c in SCALED:
    _sb(_n, [128, 128], BFT)
for _n, _s, _t in (
        ("ONES", [128, 128], BFT), ("B1", [128, 128], BFT), ("B", [128, 128], BFT), ("IB", [128, 128], BFT), ("CL", [128, 128], BFT),
        ("IH", [128, 128], F16), ("H2K", [128, 128], F16), ("H8K", [128, 128], F16), ("ONEF", [128, 128], F32), ("F4K", [128, 128], F32),
        ("CR", [128, 512], BFT), ("PR32", [128, 32], F32), ("E81", [8, 128], BFT), ("E8", [8, 128], BFT), ("TB", [8, 128], BFT), ("CK", [64, 1152], BFT),
        ("WM", [128, 8], BFT), ("BW", [128, 128], BFT), ("NK0", [128, 128], BFT), ("C8", [128, 128], BFT), ("RSF", [128, 256], BFT), ("RS", [128, 512], BFT), ("RS4", [128, 256], BFT), ("M192", [128, 512], BFT),
        ("THB", [8, 1], BFT), ("THC", [8, 1], F32), ("PID", [128, 1], I32), ("PI2", [128, 1], I32), ("WT", [128, 4], I32), ("AI", [128, 1], I32), ("AI2", [128, 1], I32),
        ("BX", [128, 1], I32), ("BY", [128, 1], I32), ("NZ", [128, 1], F32), ("COEF", [128, 1], F32), ("WCOL", [128, 1], F32), ("A8", [128, 1], F32),
        ("BA", [128, 1], F32), ("BE", [128, 1], F32), ("TH", [8, 1], I32), ("WN", [8, 512], I32), ("WNB", [8, 512], BFT), ("WL", [128, 256], I32),
        ("BW1", [128, 32], I32), ("BASE", [128, 64], I32), ("FVM", [128, 256], F32), ("LI", [128, 32], I32), ("LR", [128, 64], I32), ("LQ", [128, 64], I32),
        ("LOFF", [128, 64], U16), ("LH", [128, 32], U16), ("ZS", [128, 512], BFT), ("ZH", [128, 512], BFT), ("ZX", [128, 512], BFT), ("YN", [8, 512], F32)):
    _sb(_n, _s, _t)
for _b in "01":
    for _n, _s, _t in (
            ("V", [128, 2064], BFT), ("M", [128, 2048], BFT), ("XH", [128, 2048], BFT), ("AE", [128, 2048], BFT),
            ("OFF", [128, 128], U16), ("HOFF", [128, 128], U16), ("LE", [128, 16, 9], BFT), ("LP", [128, 16, 5], BFT), ("NM", [128, 16, 8], I32), ("NF", [128, 16, 8], F16),
            ("SG", [128, 144], BFT), ("CS", [128, 128], BFT), ("C", [128, 16, 8], BFT), ("K", [128, 128], BFT), ("K2", [128, 128], BFT), ("KX", [128, 16, 8], BFT),
            ("KY", [128, 64], BFT), ("KY2", [128, 64], BFT), ("AS", [128, 1], F32), ("TA", [128, 128], F32), ("TI", [128, 16, 8], I32), ("TJ", [128, 16, 8], I32), ("N1", [128, 16, 8], F16),
            ("KP", [128, 128], BFT), ("SQ", [128, 128], F32), ("U", [128, 128], F32), ("WI", [128, 16, 8], I32), ("HI", [128, 16, 8], I32), ("HF", [128, 16, 8], F16), ("Q", [128, 16, 8], F16),
            ("FO", [128, 256], F32), ("OSO", [128, 512], F32), ("OSV", [128, 256], F32), ("J", [128, 16, 4], I32), ("YL", [128, 128], F32)):
        _sb(_n + _b, _s, _t)
    for _i in range(NV):
        for _n in ("SO", "SV", "RO", "RV"):
            _sb("%s%d%s" % (_n, _i, _b), [128, 16, 4], F32)
        for _n in ("MX", "MR"):
            _sb("%s%d%s" % (_n, _i, _b), [128, 16], BFT)

DMAS = ["xv", "xc0", "xc1", "xc2", "wl", "wn", "wt", "th", "yx", "yl0", "yl1", "yn"]
SEMAPHORES = ["qv", "qs", "qp", "qg", "ls"] + ["d_" + n for n in DMAS] + ["r%s%d%d" % (k, t, b) for k in "xm" for t in range(NV) for b in (0, 1)]
CY = 0.00083
PC = 0.00046
HOP = 0.09


def rank_program(g, core, T, topo):
    rank = T.rank_of(core)
    if rank is None:
        return
    n = len(T.cores)
    nxt, nx2, prv, pr2 = [T.cores[(rank + k) % n] for k in (1, 2, -1, -2)]
    A, F = AluOpType, ActivationFunctionType
    V, S, P = g.vector, g.scalar, g.tensor
    D = {k: T[b][:, i] for k, (b, i) in VIEWS.items()}
    XS, Z, DD, Y, TO, TV, L = [T.X0, T.X1], T.Z, T.DD, [T.Y0, T.Y1], T.TO, T.TV, [T.L0, T.L1]
    tiles = [slice(128 * k, 128 * k + 128) for k in range(4)]
    WB = [[w[:, k] for k in tiles] for w in (T.W0, T.W1)]
    tt, mm, sc, act, mset, copy = V.tensor_tensor, P.matmul, V.tensor_tensor_scan, S.activation, V.memset, V.tensor_copy
    ops, cur, visit, seen = [], [""], [0], {}

    def op(q, r, w, cost, fn, b=(), sem=None, inc=0, after=(), lat=0.0):
        k = (w.split() or ["send"])[0]
        k = q + (k[:2] + k[3:] if k[:2] in ("MX", "MR", "SO", "SV", "RO", "RV") else "X" if cur[0] and k in ("X0", "X1") else k + "a" if k in ("J0", "J1") else k) + ("" if cur[0] else "!")
        seen[(k, visit[0])] = seen.get((k, visit[0]), 0) + 1
        k += "" if seen[(k, visit[0])] == 1 else "#%d" % seen[(k, visit[0])]
        ops.append({"name": k, "t": visit[0], "k": cur[0] + q if cur[0] else "", "q": q, "r": r.split(), "w": w.split(), "cost": cost, "fn": fn, "b": list(b), "sem": sem, "inc": inc, "after": list(after), "lat": lat})
        return len(ops) - 1

    def v(r, w, cyc, fn, b=()):
        return op("v", r, w, 0.035 + CY * max(cyc, 64), lambda: [fn()], b)

    def s(r, w, cyc, fn, b=()):
        return op("s", r, w, 0.05 + CY * max(cyc, 64), lambda: [fn()], b)

    def p(r, w, cyc, fn, b):
        return op("p", r, w, PC * cyc, fn, b)

    def gg(r, w, cost, fn):
        return op("g", r, w, cost, lambda: [fn()])

    def ld(q, name, out, in_, r, w, cost):
        return op(q, r, w, 0.06, lambda: [(g.sync if q == "y" else S).dma_start(out, in_)], sem="d_" + name, inc=16, lat=cost)

    def ts(out, in0, s1, s2, o0, o1=None):
        if o1 is None:
            return V.tensor_scalar(out, in0, s1, None, o0)
        return V.tensor_scalar(out, in0, s1, s2, o0, o1)

    def gcopy(out, in_, n):
        return g.affine_select(out, in_, [[0, n]], A.is_equal, 0.0, 0, 0)

    def pcs(tok, a, e):
        return " ".join("%s.%d" % (tok, i) for i in range(a, e))

    CKT, CKC, CKF, CKH, CKD, CKN = slice(0, 512), slice(512, 640), slice(640, 768), slice(768, 896), slice(896, 1024), slice(1024, 1152)

    def const(out, cols):
        return mm(out, D["ONES"][0:33, :], D["CK"][0:33, cols], True, False)

    ld("y", "wl", D["WL"], T.wl[:], "", "WL", 2.0)
    ld("y", "xv", XS[0][:, 0:W], T.xv[:], "", "X0", 7.0)
    ld("y", "xc0", XS[1][:, 0:W], T.xv[:], "X0", "X1", 7.0)
    ld("d", "th", D["TH"], T.th[:], "", "TH", 2.0)
    ld("d", "wt", D["WT"][:, 0:1], T.wt[:], "", "WT", 2.0)
    ld("d", "wn", D["WN"], T.wn[:], "", "WN", 2.0)
    v("", "ONES", 64, lambda: mset(D["ONES"], 1.0))
    gg("ONES", "IB", 0.4, lambda: g.affine_select(D["IB"], D["ONES"], [[-1, 128]], A.is_equal, 0.0, 0, 1))
    gg("ONES", "B1", 0.4, lambda: g.affine_select(D["B1"], D["ONES"], [[-16, 8], [0, 16]], A.is_ge, 0.0, 0, 1))
    gg("B1", "B", 0.4, lambda: g.affine_select(D["B"], D["B1"], [[16, 8], [0, 16]], A.is_ge, 0.0, 15, -1))
    gg("ONES", "E81", 0.4, lambda: g.affine_select(D["E81"], D["ONES"][0:8, :], [[1, 128]], A.is_ge, 0.0, 0, -16))
    gg("E81", "E8", 0.4, lambda: g.affine_select(D["E8"], D["E81"], [[-1, 128]], A.is_ge, 0.0, 15, 16))
    gg("", "PID", 0.2, lambda: g.iota(D["PID"], [[0, 1]], 0, 1))
    gg("", "BW1", 0.2, lambda: g.iota(D["BW1"], [[16, 32]], 0, 0))
    CK = D["CK"]
    v("", "CK0", 576, lambda: mset(CK, 0.0))
    gg("CK0", "CKF", 0.4, lambda: g.iota(CK[0:1, CKF], [[0, 16], [8192, 8]], -31 * 8192, 0, allow_small_or_imprecise_dtypes=True))
    gg("CK0", "CKN", 0.4, lambda: g.iota(CK[0:1, CKN], [[0, 16], [-1, 8]], 0, 0, allow_small_or_imprecise_dtypes=True))
    for q in range(4):
        v("CK0", "CKT%d" % q, 64, lambda q=q: mset(CK[0:1, 128 * q:128 * q + 128], -BIG * (2 * q + 1) ** 2))
    for k, r, cols, c in (("CKT", 32, CKT, 2048.0), ("CKC", 0, CKC, 32768.0), ("CKc", 32, CKC, 208.0), ("CKf", 32, CKF, 129.0 * 4096), ("CKH", 0, CKH, -BIG2), ("CKh", 32, CKH, 6144.0), ("CKD", 0, CKD, -120.0)):
        v("CK0", k, 256 if k == "CKT" else 64, lambda r=r, cols=cols, c=c: mset(CK[r:r + 1, cols], c))
    for b in (0, 1):
        x = str(b)
        v("WL", "OFF" + x, 128, lambda b=b, x=x: copy(D["OFF" + x], D["WL"][:, 128 * b:128 * b + 128]))
        v("WL", "NF" + x, 128, lambda b=b, x=x: ts(D["NF" + x], D["WL"][:, 128 * b:128 * b + 128], -2048.0, None, A.add))
        v("", "V%sz" % x, 64, lambda x=x: mset(D["V" + x][:, 0:16], -32.0))
        v("", "SGz" + x, 64, lambda x=x: mset(D["SG" + x][:, 128:144], -1.0))
        v("", "LEz" + x, 64, lambda x=x: mset(D["LE" + x][:, :, 0], -0.5))
        v("", "LPz" + x, 64, lambda x=x: mset(D["LP" + x][:, :, 0], -0.5))
    for k, src, c in SCALED + (("F4K", "IB", 4096.0),):
        s(src, k, 128, lambda k=k, src=src, c=c: act(D[k], D[src], F.Copy, scale=c))
    for k, src, c in (("IH", "IB", 1.0), ("H2K", "IB", 2048.0), ("H8K", "IB", 8192.0)):
        v(src, k, 64, lambda k=k, src=src, c=c: ts(D[k], D[src], c, None, A.mult))
    for k, c, c0, st, w in (("CR", 4.0, -256.0, 8, 512), ("NK0", 1.0, 0.0, 8, 128), ("RSF", 2.0 ** 30, 4096.0, 8, 256), ("RS", 2.0 ** 30, EMPTY, 8, 512), ("RS4", 2.0 ** 30, EMPTY, 4, 256)):
        v("", k + "a", w // 2, lambda k=k, c=c: mset(D[k], c))
        v(k + "a", k, 64, lambda k=k, c0=c0, st=st: mset(D[k][:, 0::st], c0))
    for k, c, w in (("C8", 0.125, 64), ("M192", -192.0, 256), ("ONEF", 1.0, 128), ("A8", 2.0 ** 24, 64), ("FVM", 0.0, 256)):
        v("", k, w, lambda k=k, c=c: mset(D[k], c))
    v("TH", "THB", 64, lambda: copy(D["THB"], D["TH"]))
    v("TH", "THC", 64, lambda: ts(D["THC"], D["TH"], 64.0, -8192.0, A.mult, A.add))
    v("PID", "PI2", 64, lambda: ts(D["PI2"], D["PID"], 15, None, A.bitwise_and))
    v("PI2", "NZ", 64, lambda: ts(D["NZ"], D["PI2"], 0.0, None, A.is_equal))
    p("E8 THB", "TO", 64, lambda: [mm(TO[:, 0:1], D["E8"], D["THB"], True, True)], ["TO"])
    v("TO NZ", "COEF", 64, lambda: tt(D["COEF"], TO[:, 0:1], D["NZ"], A.add), ["TO"])
    v("B COEF", "CL", 64, lambda: ts(D["CL"], D["B"], D["COEF"], None, A.mult))
    v("THC E8", "TBa", 64, lambda: ts(D["TB"], D["E8"], D["THC"], None, A.mult))
    v("TBa", "TB", 64, lambda: mset(D["TB"][:, 0::8], -16384.0))
    v("WT", "WCOL", 64, lambda: copy(D["WCOL"], D["WT"][:, 0:1]))
    v("B WCOL", "WM", 64, lambda: ts(D["WM"], D["B"][:, 0:128:16], D["WCOL"], 1.0 / 4096, A.mult, A.mult))
    v("B WCOL", "BW", 64, lambda: ts(D["BW"], D["B"], D["WCOL"], 32.0 / 4096, A.mult, A.mult))
    for q in range(4):
        v("IB", "PR%d" % q, 64, lambda q=q: copy(D["PR32"][32 * q:32 * q + 32, :], D["IB"][32 * q:32 * q + 32, 32 * q:32 * q + 32]))
    v("PID", "BX", 64, lambda: ts(D["BX"], D["PID"], 7, None, A.bitwise_and))
    v("PID", "BY", 64, lambda: ts(D["BY"], D["PID"], 8, None, A.bitwise_and))
    v("BX", "BA", 64, lambda: ts(D["BA"], D["BX"], 512.0, None, A.mult))
    v("BY BA", "BE", 64, lambda: ts(D["BE"], D["BY"], D["BA"], None, A.add))
    v("BW1 BE", "BASEa", 64, lambda: ts(D["BASE"][:, 0:32], D["BW1"], D["BE"], -1.0, A.add, A.add))
    v("BW1 BE", "BASE", 64, lambda: ts(D["BASE"][:, 32:64], D["BW1"], D["BE"], None, A.add))
    v("WN", "WNB", 512, lambda: copy(D["WNB"], D["WN"]))
    for b in (0, 1):
        p("WNB E8 ONES CKN", "Y%d.2" % b, 256, lambda b=b: [const(Y[b][:, 2], CKN)] + [
            mm(Y[b][:, 2, :, 8 * w1:8 * w1 + 8], D["WNB"][:, 256 * b + w1:256 * b + 256:2], D["E8"][:, 0:128:2], False, w1 == 1) for w1 in (0, 1)], ["Y%d" % b])
        v("Y%d.2" % b, "LA%d" % b, 128, lambda b=b: ts(D["LE%d" % b][:, :, 1:9], Y[b][:, 2], 0.0, -0.5, A.is_gt, A.add), ["Y%d" % b])

    def phase1(t, b):
        x, (m0, m1) = str(b), BYMAX[b]
        Vb, M, y = D["V" + x], D["M" + x], Y[b][:, 0]
        for q, a, e in GATHER1[b]:
            o, w = Vb[:, 16 + 512 * a:16 + 512 * e], XS[t % 2][:, 0:W].indirect(D["OFF" + x][:, 32 * a:32 * e])
            if q == "s":
                s("X%d OFF%s" % (t % 2, x), pcs("V" + x, a, e), (e - a) * 512 * 1.56, lambda o=o, w=w: act(o, w, F.Identity, bias=-32.0))
            else:
                v("X%d OFF%s" % (t % 2, x), pcs("V" + x, a, e), (e - a) * 512 * 1.56, lambda o=o, w=w: ts(o, w, -32.0, None, A.add))

        def before(c):
            return "V%sz" % x if c == 0 else "V%s.%d" % (x, c - 1)
        for a, e in NEIGH[b]:
            r, v0, v1 = slice(512 * a, 512 * e), Vb[:, 15 + 512 * a:15 + 512 * e], Vb[:, 16 + 512 * a:16 + 512 * e]
            rd = before(a) + " " + pcs("V" + x, a, e)
            if m0 <= a < m1:
                v(rd, pcs("M" + x, a, e), 256 * (e - a), lambda r=r, v0=v0, v1=v1: sc(M[:, r], v0, v1, 0.0, A.min, A.max))
            else:
                v(rd, pcs("XH" + x, a, e), 256 * (e - a), lambda r=r, v0=v0, v1=v1: sc(D["XH" + x][:, r], v1, v0, 0.0, A.min, A.subtract))
                s(pcs("XH" + x, a, e), pcs("M" + x, a, e), 512 * (e - a), lambda r=r: act(M[:, r], D["XH" + x][:, r], F.Abs, scale=0.5))
        for c in range(4):
            j, i = 512 * c, c % 2
            k = "L%d" % i
            p("CL CR", k, 512, lambda i=i: [mm(L[i][:], D["CL"], D["CR"], True, False)], [k])
            if m0 <= c < m1:
                p("V%s.%d %s B16" % (x, c, before(c)), k, 1024, lambda j=j, i=i: [mm(L[i][:], D["B16"], Vb[:, o + j:o + 512 + j], False, False) for o in (15, 16)], [k])
            p("M%s.%d NB32" % (x, c), k, 512, lambda j=j, i=i: [mm(L[i][:], D["NB32"], M[:, j:j + 512], False, True)], [k])
            v("%s V%s.%d" % (k, x, c), "Z%s.%d" % (x, c), 512, lambda j=j, i=i: sc(Z[:, 2048 * b + j:2048 * b + j + 512], L[i][:], Vb[:, 16 + j:528 + j], 0.0, A.min, A.max), [k])
        nm = m1 - m0
        LE, LP, ym, beg, end = D["LE" + x], D["LP" + x], y[32 * m0:32 * m1] if nm else None, 16 + 512 * m0, 16 + 512 * m1
        p("ONES TB P4 LA%s B16 %s" % (x, pcs("V" + x, m0, m1)), "D3." + x, 256 + 16 * min(64, 32 * nm),
          lambda: [mm(y, D["ONES"][0:8, :], D["TB"], True, False)]
          + ([mm(y, D["P4"], LE[:, :, 1:9], False, False)] if t == 0 else [mm(y[:, :, o::2], D["P4"], LP[:, :, 1:5], False, False) for o in (0, 1)])
          + [mm(ym[:, :, m:m + 2], Vb[:, beg + m:end:16], D["B16"][:, 0:128:8], False, False) for m in range(15 if nm else 0)]
          + ([mm(ym[:, :, 15], Vb[:, beg + 15:end:16], D["B16"][:, 0:128:16], False, False)] if nm else []), ["Y" + x])
        p(pcs("M" + x, 0, 4) + " NB32", "D3." + x, 1024, lambda: [mm(y[:, :, m], M[:, m:2048:16], D["NB32"][:, 0:128:16], False, m == 15) for m in range(16)], ["Y" + x])
        s("D3." + x, "SG" + x, 128, lambda: act(D["SG" + x][:, 0:128], y, F.Sign, bias=8.0), ["Y" + x])

    def runs(t, b):
        x, y = str(b), "%d%d" % (t, b)
        wb, w_, SG, LE, LP, K = WB[b], "W" + x, D["SG" + x], D["LE" + x], D["LP" + x], D["K" + x]
        v("SG%s C8" % x, "CS" + x, 64, lambda: sc(D["CS" + x], SG[:, 0:128], D["C8"], 0.0, A.min, A.add))
        s("CS" + x, "C" + x, 128, lambda: act(D["C" + x], D["CS" + x], F.Identity, bias=17.0, scale=16.0))
        lam = [(wb[0], "IB", LE[:, :, 1:9]), (wb[0], "IB", LE[:, :, 0:8])] if t == 0 else \
              [(wb[0][:, 0::2], "IB", LP[:, :, 1:5]), (wb[0][:, 0::2], "IB", LP[:, :, 0:4]), (wb[0][:, 1::2], "I2", LP[:, :, 1:5])]
        p("SG%s SGz%s LA%s LEz%s LPz%s NH IB I2" % (x, x, x, x, x), w_ + ".0", 448,
          lambda: [mm(wb[0], D["NH"], SG[:, 1:129], True, False), mm(wb[0], D["NH"], SG[:, 0:128], False, False)]
          + [mm(o, D[k], m, False, i == len(lam) - 1) for i, (o, k, m) in enumerate(lam)], [w_])
        v(w_ + ".0 NK0", "K" + x, 128, lambda: sc(K, D["NK0"], wb[0], 0.0, A.mult, A.add), [w_])
        p("K%s LA%s IB" % (x, x), w_ + ".0", 128, lambda: [mm(wb[0][:, 0:16], D["IB"], K[:, 7::8], True, False), mm(wb[0][:, 0:16], D["IB"], LE[:, :, 8] if t == 0 else LP[:, :, 4], False, True)], [w_])
        s(w_ + ".0", "MX%s AS%s" % (y, x), 64, lambda: act(D["MX" + y], wb[0][:, 0:16], F.Identity, bias=0.5, accum_out=D["AS" + x]), [w_])
        i = op("g", "MX" + y, "", 0.7 if t + b else 2.7, lambda: [send_counts(y)], sem="none")
        op("r", "", "MR" + y, 0.0, None, sem="rm" + y, inc=len(count_engines(nxt, core)), after=[i], lat=3.0)
        s("K" + x, "K2" + x, 128, lambda: act(D["K2" + x], K, F.Square))
        s("K" + x, "KX" + x, 128, lambda: act(D["KX" + x], K, F.Relu, bias=-8.0))

    def upart(t, b):
        x = str(b)
        u, zo, bk = Y[b][:, 1], 2048 * b, ["Y" + x]
        p("ONES BW", "UB" + x, 128, lambda: [mm(u, D["ONES"], D["BW"], True, False)], bk)
        p(pcs("Z" + x, 0, 4) + " WM", "UB" + x, 1024, lambda: [mm(u[:, :, m], Z[:, zo + m:zo + 2048:16], D["WM"], False, m == 15) for m in range(16)], bk)
        if KPQ[b] == "s":
            s("UB" + x, "KP" + x, 128, lambda: act(D["KP" + x], u, F.Identity, bias=128.5 + 1.0 / 8192), bk)
        else:
            v("UB" + x, "KP" + x, 128, lambda: ts(D["KP" + x], u, 128.5 + 1.0 / 8192, None, A.add), bk)
        v("KP%s UB%s" % (x, x), "U" + x, 128, lambda: tt(D["U" + x], u, D["KP" + x], A.subtract), bk)
        s("U" + x, "SQ" + x, 128, lambda: act(D["SQ" + x], D["U" + x], F.Square, bias=592.0 + 129 * 4096, scale=4096.0))

    def first1(t, b):
        x = str(b)
        fs, both, w_ = WB[b][2:4], (T.W0, T.W1)[b][:, 256:512], "W" + x
        p("ONES CKF CKf CKH CKh F2 FN F4K IH U%s HF%s K%s K2%s" % (x, x, x, x), "%s.2 %s.3" % (w_, w_), 1408,
          lambda: [const(both, slice(CKF.start, CKH.stop)), mm(fs[0], D["F4K"], D["U" + x], False, False), mm(fs[1], D["IH"], D["HF" + x], False, False)]
          + [mm(fs[i], D[k], D[m + x], False, i == 1 and k == "FN") for k, m in (("F2", "K"), ("FN", "K2")) for i in (0, 1)], [w_])
        v("RSF %s.2 %s.3" % (w_, w_), "FO" + x, 256, lambda: sc(D["FO" + x], D["RSF"], both, 4096.0, A.min, A.max), [w_])
        for q in range(4):
            r = slice(32 * q, 32 * q + 32)
            gg("FVM FO" + x, "FV%s%d" % (x, q), 0.23, lambda r=r, q=q: gcopy(D["FVM"][r, 4 * b + q::8], D["FO" + x][r, 7::8], 32))

    def hpart(t, b):
        x = str(b)
        wb, w_ = WB[b], "W" + x
        p("ONES CKC CKc CA CB C" + x, w_ + ".3", 384, lambda: [const(wb[3], CKC), mm(wb[3], D["CA"], D["C" + x], False, False), mm(wb[3], D["CB"], D["C" + x], False, True)], [w_])
        v("SQ%s %s.3" % (x, w_), "WI" + x, 128, lambda: tt(D["WI" + x], D["SQ" + x], wb[3], A.add), [w_])
        v("WI" + x, "HI" + x, 128, lambda: ts(D["HI" + x], D["WI" + x], 5, 4095, A.arith_shift_right, A.bitwise_and))
        v("HI" + x, "HF" + x, 128, lambda: ts(D["HF" + x], D["HI" + x], -2048.0, None, A.add))
        p("HF%s IH" % x, w_ + ".0", 128, lambda: [mm(wb[0], D["HF" + x], D["IH"], True, True)], [w_])
        v(w_ + ".0", "HOFF" + x, 128, lambda: ts(D["HOFF" + x], wb[0], 2048.0, None, A.add), [w_])

    def names1(t, b):
        x, y = str(b), "%d%d" % (t, b)
        wb, w_, SG, NF = WB[b], "W" + x, D["SG" + x], D["NF" + x]
        p("NF%s H2K N22 SG%s" % (x, x), w_ + ".1", 256,
          lambda: [mm(wb[1], NF, D["H2K"], True, False) if t == 0 else mm(wb[1], D["H2K"], NF, True, False), mm(wb[1], D["N22"], SG[:, 0:128], False, True)], [w_])
        v("SG%s %s.1" % (x, w_), w_ + ".2", 128, lambda: sc(wb[2], SG[:, 0:128], wb[1], 0.0, A.mult, A.max), [w_])
        v("C%s %s.2" % (x, w_), "TA" + x, 128, lambda: tt(D["TA" + x], D["C" + x], wb[2], A.mult), [w_])
        v("TA%s A8" % x, "TI" + x, 128, lambda: ts(D["TI" + x], D["TA" + x], D["A8"], None, A.add))
        v("TI" + x, "TJ" + x, 128, lambda: ts(D["TJ" + x], D["TI" + x], 13, 4095, A.arith_shift_right, A.bitwise_and))
        v("TJ" + x, "N1" + x, 128, lambda: ts(D["N1" + x], D["TJ" + x], -2048.0, None, A.add))

    def keys(t, b):
        x, y = str(b), "%d%d" % (t, b)
        wb, w_ = WB[b], "W" + x
        ky = wb[3][:, 0:64]
        p("KX%s MR%s IB" % (x, y), w_ + ".3", 320, lambda: [mm(ky, D["IB"], D["KX" + x][:, :, 4:8], True, False)] + [mm(ky[:, k:64:4], D["IB"], D["MR" + y], False, k == 3) for k in range(4)], [w_])
        s(w_ + ".3", "KY" + x, 64, lambda: act(D["KY" + x], ky, F.Copy), [w_])
        s(w_ + ".3", "KY2" + x, 64, lambda: act(D["KY2" + x], ky, F.Square), [w_])

    def phase2(t, b):
        x = str(b)
        XH, AE, zo = D["XH" + x], D["AE" + x], 2048 * b
        for q, a, e in GATHER2[b]:
            r, zr, w = slice(512 * a, 512 * e), slice(zo + 512 * a, zo + 512 * e), XS[t % 2][:, 0:W].indirect(D["HOFF" + x][:, 32 * a:32 * e])
            if q == "v":
                v("X%d HOFF%s %s" % (t % 2, x, pcs("Z" + x, a, e)), pcs("DD" + x, a, e), (e - a) * 512 * 1.56, lambda zr=zr, w=w: tt(DD[:, zr], w, Z[:, zr], A.subtract))
                continue
            s("X%d HOFF%s" % (t % 2, x), pcs("XH" + x, a, e), (e - a) * 512 * 1.56, lambda r=r, w=w: act(XH[:, r], w, F.Copy))
            v(pcs("Z" + x, a, e) + " " + pcs("XH" + x, a, e), pcs("DD" + x, a, e), 256 * (e - a), lambda r=r, zr=zr: sc(DD[:, zr], XH[:, r], Z[:, zr], 64.0, A.min, A.subtract))
        for a, e in ABS2[b]:
            r, zr = slice(512 * a, 512 * e), slice(zo + 512 * a, zo + 512 * e)
            s(pcs("DD" + x, a, e), pcs("AE" + x, a, e), 512 * (e - a), lambda r=r, zr=zr: act(AE[:, r], DD[:, zr], F.Abs, bias=-32.0))

    def first2(t):
        LI, LR = D["LI"], D["LR"]
        p(" ".join("FV%d%d" % (b, q) for b in (0, 1) for q in range(4)) + " PR0 PR1 PR2 PR3", "UF0", 512,
          lambda: [mm(Y[1][:, 3, 2 * i:2 * i + 2], D["FVM"][:, 128 * i:128 * i + 128], D["PR32"], True, True) for i in (0, 1)], ["Y1"])
        v("UF0", "LH", 64, lambda: ts(D["LH"], Y[1][:, 3, 2:4], -4096.0, None, A.add), ["Y1"])
        v("UF0", "LI", 64, lambda: copy(LI, Y[1][:, 3, 0:2]), ["Y1"])
        v("LI", "LRa", 64, lambda: ts(LR[:, 0:32], LI, 13, None, A.arith_shift_right))
        v("LI", "LRb", 64, lambda: ts(LR[:, 32:64], LI, 4096 + 7, None, A.bitwise_and))
        v("LRa LRb BASE BASEa", "LQ", 128, lambda: tt(D["LQ"], LR, D["BASE"], A.add))
        v("LQ", "LOFF", 64, lambda: copy(D["LOFF"], D["LQ"]))

    def update(t):
        pos, col, old, new = D["LOFF"][:, 0:32], D["LOFF"][:, 32:64], t % 2, 1 - t % 2
        s("X%d LH" % old, "ZS", 512 * 1.56, lambda: act(D["ZS"], XS[old][:, 0:W].indirect(D["LH"]), F.Copy))
        v(pcs("Z0", 0, 4) + " " + pcs("Z1", 0, 4) + " LOFF ZS", "ZX", 512 * 1.56, lambda: tt(D["ZX"], Z[:].indirect(pos), D["ZS"], A.add))
        s("ZX", "ZH", 512, lambda: act(D["ZH"], D["ZX"], F.Identity, bias=207.75, scale=0.5))
        v("ZH M192 LOFF", "X%d" % new, 512 * 3.8, lambda: tt(XS[new][:].indirect(col), D["ZH"], D["M192"], A.add))

    def names2(t, b):
        x, y = str(b), "%d%d" % (t, b)
        d, bk = Y[b][:, 2], ["Y" + x]
        p("ONES CKD", "Y%s.2" % x, 128, lambda: [const(d, CKD)], bk)
        p(pcs("AE" + x, 0, 4) + " B", "Y%s.2" % x, 1024, lambda: [mm(d[:, :, m], D["AE" + x][:, m:2048:16], D["B"][:, 0:128:16], False, m == 15) for m in range(16)], bk)
        v("Y%s.2 C%s" % (x, x), "Q" + x, 128, lambda: tt(D["Q" + x], D["C" + x], d, A.mult), bk)
        for bank, tok, w, cols, key, lo, rs, out in ((TV, "TV", 64, slice(0, 512, 2), "KY", 4, "RS4", "OSV"), (TO, "TO", 128, CKT, "K", 0, "RS", "OSO")):
            def terms(pairs, stop, bank=bank, w=w):
                return [mm(bank[:, w * q:w * q + w], D[k] if k != "T" else D["T%d" % q], m, False, stop and q == 3) for k, m in pairs for q in range(4)]
            p("ONES CKT CKT0 CKT1 CKT2 CKT3 T0 T1 T2 T3 TN %s%s %s2%s" % (key, x, key, x), tok, 12 * w,
              lambda bank=bank, w=w, cols=cols, key=key, terms=terms: [const(bank[:, 0:4 * w], cols)] + terms([("T", D[key + x]), ("TN", D[key + "2" + x])], False), [tok])
            p("I120 H8K IH C%s N1%s HF%s" % (x, x, x), tok, 12 * w,
              lambda lo=lo, terms=terms: terms([("I120", D["C" + x][:, :, lo:8]), ("H8K", D["N1" + x][:, :, lo:8]), ("IH", D["HF" + x][:, :, lo:8])], False), [tok])
            p("IH Q" + x, tok, 4 * w, lambda lo=lo, terms=terms: terms([("IH", D["Q" + x][:, :, lo:8])], True), [tok])
            v("%s %s" % (tok, rs), out + x, 4 * w, lambda bank=bank, w=w, rs=rs, out=out: sc(D[out + x], D[rs], bank[:, 0:4 * w], 0.0, A.min, A.max), [tok])
        for q in range(4):
            for k, src, w, e in (("SV", "OSV", 4, COPY[b][q]), ("SO", "OSO", 8, COPY[b][4 + q])):
                o, i, tok = D[k + y][:, :, q], D[src + x][:, 16 * w * q + w - 1:16 * w * (q + 1):w], "%s%s.%d" % (k, y, q)
                if e == "g":
                    gg(src + x, tok, 0.2, lambda o=o, i=i: gcopy(o, i, 16))
                elif e == "s":
                    s(src + x, tok, 64, lambda o=o, i=i: act(o, i, F.Copy))
                else:
                    v(src + x, tok, 64, lambda o=o, i=i: copy(o, i))
        so, sv = pcs("SO" + y, 0, 4), pcs("SV" + y, 0, 4)
        if t < NV - 1:
            i = op("g", so + " " + sv, "", 0.8, lambda: [send_pairs(y)], sem="none")
            op("r", "", "RO%s RV%s" % (y, y), 0.0, None, sem="rx" + y, inc=len(pair_engines(prv, core, 0)) + len(pair_engines(pr2, prv, 1)), after=[i], lat=3.5)
        else:
            i = op("g", sv, "", 0.8, lambda: [send_last(y)], sem="none")
            op("r", "", "RV" + y, 0.0, None, sem="rx" + y, inc=len(count_engines(prv, core)), after=[i], lat=3.5)

    def join(t, b):
        x, y, last = str(b), "%d%d" % (t, b), t == NV - 1
        J, NM, LP, wb, w_ = D["J" + x], D["NM" + x], D["LP" + x], WB[b], "W" + x
        own, ov = D[("SO" if last else "RO") + y], D["RV" + y]
        rd = "RV%s " % y + (pcs("SO" + y, 0, 4) if last else "RO" + y)
        if last:
            v(rd, "J" + x, 128, lambda: tt(J, own, ov, A.max))
            jt = "J" + x
        else:
            v(rd, "J%sa" % x, 112, lambda: tt(J[:, 2:16, :], own[:, 0:14, :], ov[:, 0:14, :], A.max))
            v(rd, "J%sb" % x, 64, lambda: tt(J[:, 0:2, :], own[:, 14:16, :], ov[:, 14:16, :], A.max))
            jt = "J%sa J%sb" % (x, x)
        v(jt, "NM%sa" % x, 64, lambda: ts(NM[:, :, 0::2], J, 13, 4095, A.arith_shift_right, A.bitwise_and))
        v(jt, "NM" + x, 64, lambda: ts(NM[:, :, 1::2], J, 4095, None, A.bitwise_and))
        v("NM%s NM%sa" % (x, x), "NF" + x, 128, lambda: ts(D["NF" + x], NM, -2048.0, None, A.add))
        p("NF%s IH" % x, w_ + ".0", 128, lambda: [mm(wb[0], D["NF" + x], D["IH"], True, True)], [w_])
        if not last:
            v(w_ + ".0", "OFF" + x, 128, lambda: ts(D["OFF" + x], wb[0], 2048.0, None, A.add), [w_])
        else:
            s(w_ + ".0", "YL" + x, 128, lambda: act(D["YL" + x], wb[0], F.Identity, bias=2048.0), [w_])
            ld("y", "yl" + x, T.yl[:, 128 * b:128 * b + 128], D["YL" + x], "YL" + x, "yl" + x, 2.5)
        v(jt, "LA" + x, 64, lambda: ts(LP[:, :, 1:5], J, 0.75 * EMPTY, -0.5, A.is_ge, A.add))
        if last:
            p("LA%s I2" % x, "L0", 1024, lambda: [mm(L[0][0:8, 256 * b + w1:256 * b + 256:2], LP[:, w1::2, 1 + j], D["I2"], j == 0, j == 3) for w1 in (0, 1) for j in range(4)], ["L0"])
            s("L0", "YN" + x, 256, lambda: act(D["YN"][:, 256 * b:256 * b + 256], L[0][0:8, 256 * b:256 * b + 256], F.Identity, bias=4.0), ["L0"])

    def total(t):
        a = Y[1][:, 3, 4, 0:1]
        p("ONEF AS0 AS1", "UF1", 512, lambda: [mm(a, D["ONEF"], D["AS0"], True, False), mm(a, D["ONEF"], D["AS1"], False, True)], ["Y1"])
        v("UF1", "AI", 64, lambda: copy(D["AI"], a), ["Y1"])
        v("AI", "AI2", 64, lambda: ts(D["AI2"], D["AI"], 510, None, A.bitwise_and))
        v("AI2", "A8", 64, lambda: ts(D["A8"], D["AI2"], 4096.0, 2.0 ** 24, A.mult, A.add))

    def count_engines(a, c):
        return topo.engines(a, c)[0:8]

    def pair_engines(a, c, k):
        e = topo.engines(a, c)
        return (e[8:16], e[0:8])[k] if len(e) == 16 else (e[0:4], e[4:8])[k]

    def mask(es):
        return sum(1 << e for e in es)
    lsum = [0]

    def send_one(dst, out, in_, sem):
        es = count_engines(core, dst)
        rid, pid, _ = topo.addr(dst)
        lsum[0] += len(es)
        g.remote_dma(D[out], D[in_], T.sem[sem], T.sem.ls, pid, rid, mask(es))

    def send_counts(y):
        send_one(prv, "MR" + y, "MX" + y, "rm" + y)

    def send_last(y):
        send_one(nxt, "RV" + y, "SV" + y, "rx" + y)

    def send_pairs(y):
        tr = []
        for k, dst, o, i in ((0, nxt, "RO", "SO"), (1, nx2, "RV", "SV")):
            es = pair_engines(core, nxt, k)
            lsum[0] += len(es)
            rid, pid, _ = topo.addr(dst)
            tr.append(RemoteDMATransfer(dst_ids=[DstId(rid=rid, pnc=pid)], dma_engine_mask=mask(es), remote_sem=T.sem["rx" + y], srcs=[D[i + y]], dsts=[D[o + y]]))
        g.remote_dma_fused(tr, local_sem=T.sem.ls)

    def part(key, fn, *a):
        cur[0] = key + "".join(str(k) for k in a[1:])
        fn(*a)
        cur[0] = ""

    for t in range(NV):
        visit[0] = t
        for b in (0, 1):
            part("phase1", phase1, t, b)
            part("runs", runs, t, b)
            if EARLY[b]:
                part("names1", names1, t, b)
            part("upart", upart, t, b)
            part("hpart", hpart, t, b)
            part("first1", first1, t, b)
        for b in (0, 1):
            if not EARLY[b]:
                part("names1", names1, t, b)
            part("keys", keys, t, b)
            part("phase2", phase2, t, b)
        part("first2", first2, t)
        part("update", update, t)
        if t == NV - 1:
            ld("y", "yx", T.yx[:], XS[NV % 2][:, 0:W], "X%d" % (NV % 2), "yx", 7.0)
        for b in (0, 1):
            part("names2", names2, t, b)
        if t < NV - 1:
            part("total", total, t)
        for b in (0, 1):
            part("join", join, t, b)
        if t < NV - 1:
            part("copy", lambda t: ld("y", "xc%d" % (t + 1), XS[t % 2][:, 0:W], XS[1 - t % 2][:, 0:W], "X%d RO%d1" % (1 - t % 2, t), "X%d" % (t % 2), 7.0), t)
    ld("y", "yn", T.yn[:], D["YN"], "YN0 YN1", "yn", 2.5)
    emit(g, T, ops)
    g.wait_ge(T.sem.ls, lsum[0])


BOOST = {'phase11p': -2.8, 'phase10p': -1.3, 'hpart0v': 4, 'hpart0p': 24, 'phase20v': 95, 'upart1p': -1, 'names10s': -3, 'phase11s': -1, 'names21s': -5.5, 'first10p': -1,
         'upart0s': 6, 'join0v': -1.4, 'runs0s': 2, 'phase21v': 2, 'first2p': -2, 'updates': -3}


ORDER = """
pL0#7 pL0#12+ sSQ1 vRS4! yyn!+ vCKC!- vBA! gFV12 vXH0.2 sV1.0 vM0.0 sN22! vZ0.3 pL0#2 vONEF! vXH0.3 pL1#3 pL1#2 sKP0 pD3.0 vZ0.0 vNF1+ vBASEa! vZ0.1 pUF1+ pL0#4 pL0#8 sYN1+ pD3.0#2 vA8! yX1! pL1#4 vCKh! pTO#2 vSGz1! sV1.1 sV1.2 vCS0 sMX0 pTO#5 pUB0 pL0#11+ vNM1+ sSO1.2+ vOFF1+ pL0#5 vJ1b+ vDD0.0 pL1#5 sT1! vK0 pL1#6 vXH1.2 sSO1.3+ pY1.2#2 vJ1a+ sC0 pW0.0 vM1.0 vNM1a+ vU0 vZ1.1 pUB0#2 vHF0 gSV0.3 yX+ yyl1+ pTV#4 pW0.0#2 sSO0.2 pL1#7 sV1.3 vZ1.0 sM1.3 sAE0.1 vM1.1 pL1#8 pW0.3#2 pW0.3 pW0.1 pD3.1 pW0.2 vWI0 pL0#6 vHI0 vBASE! pL0#9 sKX0 vZ1.3 sM1.2 vTI1 vHOFF0 sM0.2- vCKT2! gFV00 vDD0.2 pL1#9 pW0.0#3 vXH1.3 pL0#10 pL1#10 pD3.1#2 sK20 sXH0.1 sKP1 vHF1 sXH0.0 gFV01 pW1.0 pUB1 sSG1 vBX!- sYL0+ sMX1 vCS1 pUB1#2 pY0.2#2 pW1.3 vU1 gSV0.1 pTO#4 vFO0 sKY0 vK1 pL1- pW1.0#2 gFV02 vDD0.3 gSV0.0 sXH0.3 vDD0.1 vZX vTA0 vX rMR0 sKY20 sC1 vWI1 pW1.1 pY1.2 sAE0.0 gPID!- pTO pTV gFV13 vM192!- vW0.2 pW1.2 rMR1 vHOFF1 pW1.0#3 gFV10 pTO#6 gFV03 gBW1!- vOSV1 vHI1 sK21 yyl0+ pY0.2 sAE0.2 gE8!- vQ0 vTI0 vOSV0 vTHB!- pUF0 vTJ0 vWNB!- sAE0.3 sYL1+ gFV11 gsend vNK0!- vSGz0!- vOSO0 dTH!- vDD1.1 vDD1.3 pTV#6 vTBa!- pTV#5 vCKH!- sSO0.3 sXH1.0 vCR!- gsend#3 sXH1.2 gE81!- sAE1.1 sI120!- vTHC!- sKX1 gSV0.2 sSO0.0 vV0z!- vCKc!- vPR2!- vN10 vONES!- vC8!- vDD1.0 vN11 dWN!- gB!- pTV#2 sV0.0- gB1!- sSO0.1 sSQ0- vOSO1 vV1z!- vCRa!- vCKT0!- sAE1.3 vDD1.2 sAE1.0 vLH dWT!- sNH!- pTV#3 vCKf!- pTO!- pW1.3#2 pTO#3 sI2!- vLEz1!- vOFF1!- vAI pY0.2!- vWM!- vLI sAE1.2 sF4K!- vW1.2 vLA0!- rRO0 rRV0 vLRa vFO1 vLPz1!- vNZ!- rRO1 vTA1 vCOEF!- sF2!- sZS vLRb vOFF0!- vH8K!- vIH!- sKY1 vLQ sV0.2- sT2!- vCKT1!- sFN!- vQ1 gIB!- sT0!- sSG0- pW0.0#4 pW1.0#4 pY1.2!- pL0- vCKT!- yX0!- sM0.3- sV0.3- sTN!- vAI2 vRS!- vZ1.2- vRSFa!- vA8 vTJ1 vCKD!- vTB!- vCK0!- sCA!- gCKF!- sP4!- sB16!- sT3!- vCKT3!- sKY21 vBW!- vLOFF sCB!- sZH gSV1.2 vNM0 vRS4a!- vLA1!- vPR0!- gCKN!- gSV1.3 vNF0!- vCL!- vNK0a!- vNF1!- vRSa!- vZ0.2- gSV1.0 vFVM!- vNF0 vRSF!- vPR3!- vPI2!- vLPz0!- gsend#4 yWL!- yyx! vH2K!- vM0.1- gsend#2- gSV1.1 rRV1 vLA1 vWCOL!- vLEz0!- sYN0 vBY!- vJ0a vNM0a vJ0b vV0.1- pL0#3- sNB32!- vBE!- vOFF0 sSO1.0 vLA0 sSO1.1 vPR1!-
"""


def emit(g, T, ops):
    deps = links(ops)
    issue(g, T, ops, deps, arrange(ops, deps, BOOST, HOP)[0])


def links(ops):
    N = len(ops)
    lastw, readers, banks = {}, {}, {}
    deps = [dict() for _ in range(N)]

    def add(i, j, hard):
        if j != i:
            deps[i][j] = deps[i].get(j, False) or hard
    for i, o in enumerate(ops):
        for k in o["r"]:
            if k in lastw:
                add(i, lastw[k], True)
            readers.setdefault(k, []).append(i)
        for k in o["w"]:
            if k in lastw:
                add(i, lastw[k], not (o["q"] == "p" and ops[lastw[k]]["q"] == "p"))
            for j in readers.get(k, []):
                add(i, j, True)
            lastw[k] = i
            readers[k] = []
        for k in o["b"]:
            for j in banks.get(k, []):
                add(i, j, ops[j]["q"] != o["q"])
            banks.setdefault(k, []).append(i)
        for j in o["after"]:
            add(i, j, False)
    return deps


def arrange(ops, deps, boost, hop):
    N = len(ops)
    succ = [[] for _ in range(N)]
    for i in range(N):
        for j in deps[i]:
            succ[j].append(i)
    way = [0.0] * N
    for i in range(N - 1, -1, -1):
        way[i] = ops[i]["cost"] + ops[i]["lat"] + max([way[j] + hop for j in succ[i]] or [0.0])
    key = [way[i] + boost.get(ops[i]["k"], 0.0) for i in range(N)]
    if ORDER:
        names = ORDER.split()
        at = {x.rstrip("+-"): i + len(names) * (x.count("+") - x.count("-")) for i, x in enumerate(names)}
        key = [-at[o["name"]] - len(names) * o["t"] for o in ops]
    left = [len(d) for d in deps]
    cand = [i for i in range(N) if left[i] == 0]
    start, end, taken = [0.0] * N, [0.0] * N, {}
    while cand:
        i = max(cand, key=lambda i: (key[i], -i))
        cand.remove(i)
        q, c = ops[i]["q"], ops[i]["cost"]
        st = max([end[j] + (hop if hard else 0.0) for j, hard in deps[i].items()] or [0.0])
        if q != "r":
            iv = taken.setdefault("s" if q == "d" else q, [])
            k = len(iv)
            while k > 0 and iv[k - 1][0] >= st:
                k -= 1
            if k > 0:
                st = max(st, iv[k - 1][1])
            while k < len(iv) and st + c > iv[k][0] + 1e-9:
                st = iv[k][1]
                k += 1
            iv.insert(k, (st, st + c))
        start[i], end[i] = st, st + c + ops[i]["lat"]
        for j in succ[i]:
            left[j] -= 1
            if left[j] == 0:
                cand.append(j)
    return sorted(range(N), key=lambda i: (start[i], i)), max(end)


def issue(g, T, ops, deps, order):
    queues = {"v": g.vector, "s": g.scalar, "d": g.scalar, "p": g.tensor, "g": g, "y": g.sync}
    sems = {"v": "qv", "s": "qs", "p": "qp", "g": "qg"}
    level, done, seen, last_some = {}, {}, {}, [False]
    for i in order:
        o = ops[i]
        q = o["q"]
        if q == "r":
            level[o["sem"]] = level.get(o["sem"], 0) + o["inc"]
            done[i] = (o["sem"], level[o["sem"]])
            continue
        qk = "s" if q == "d" else q
        need = {}
        for j, hard in deps[i].items():
            if hard and done[j] is not None:
                sm, c = done[j]
                need[sm] = max(need.get(sm, 0), c)
        if q == "g" and not o["sem"]:
            some = o["w"][0].startswith("FV") and o["w"][0] != "FVM"
            if some != last_some[0]:
                need["qg"] = level.get("qg", 0)
            last_some[0] = some
        for sm in sorted(need):
            if seen.get((qk, sm), 0) < need[sm]:
                seen[(qk, sm)] = need[sm]
                queues[q].wait_ge(T.sem[sm], need[sm])
        res = o["fn"]()
        if o["sem"] == "none":
            done[i] = None
            continue
        sm, inc = (o["sem"], o["inc"]) if o["sem"] else (sems[q], 1)
        for r in res:
            r.then_inc(T.sem[sm], inc)
            level[sm] = level.get(sm, 0) + inc
        done[i] = (sm, level[sm])
    for sm in sorted(level):
        if seen.get(("g", sm), 0) < level[sm]:
            g.wait_ge(T.sem[sm], level[sm])
